import numpy as np
import ml_dtypes


def mxq(x, axis, fmt="e4m3"):
    dtype, down = {"e4m3": (ml_dtypes.float8_e4m3fn, 7), "e5m2": (ml_dtypes.float8_e5m2, 14)}[fmt]
    v = np.moveaxis(np.asarray(x, np.float32).astype(ml_dtypes.bfloat16).astype(np.float64), axis, -1)
    blocks = v.reshape(v.shape[:-1] + (-1, 32))
    amax = np.abs(blocks).max(-1, keepdims=True)
    byte = np.maximum(np.where(amax > 0, np.frexp(amax)[1] - 1 + 127, 0) - down, 1)
    scale = np.exp2(byte - 127.0)
    codes = (blocks / scale).astype(np.float32).astype(dtype).astype(np.float64)
    return np.moveaxis((codes * scale).reshape(v.shape), -1, axis)


WIDE = False


def mx_kscale(k):
    if not WIDE:
        return np.ones(k)
    levels = np.array([10, -10, 5, -5, 0])
    if k % 512:
        return np.exp2(np.random.permutation(np.resize(levels, k // 32))).repeat(32)
    a = np.empty((k // 512, 16))
    for p in range(k // 512):
        a[p, :8] = np.random.permutation(np.resize(levels, 8))
        for g in range(8):
            far = levels[np.abs(levels - a[p, g]) >= 10]
            a[p, g + 8] = far[np.random.randint(len(far))]
    return np.exp2(a.ravel()).repeat(32)


def f64(x):
    return np.asarray(x).astype(np.float64)


def striped(idx):
    return np.tile(idx.reshape(-1, 16).T, (8, 1)).astype(np.uint16)


def unstriped(offs):
    return offs[:16].T.reshape(-1).astype(np.int64)


def silu(v):
    return v / (1.0 + np.exp(-np.maximum(v, -700.0)))


K, T, E, C, H, N = 1024, 1280, 8, 128, 512, 256


def by_expert(wq, xq):
    return np.concatenate([wq[e].T @ xq[:, e * C:(e + 1) * C] for e in range(E)], axis=1)


def setup_inputs():
    n = np.random.standard_normal
    s = mx_kscale(K)[:, None]
    u = mx_kscale(H)
    return {
        "xT": (n((K, T)) * s).astype(np.float32),
        "w1": (n((E + 1, K, H)) / np.sqrt(K) / s[None] * u[None, None, :]).astype(np.float32),
        "w2": (n((E + 1, H, N)) / np.sqrt(H) / u[None, :, None]).astype(np.float32),
        "gate": np.tile(np.random.uniform(0.2, 1.0, E * C), (N, 1)).astype(np.float32),
        "offs": striped(np.random.permutation(T)[:E * C]),
    }


def reference(xT, w1, w2, gate, offs):
    idx = unstriped(offs)
    w1q, w2q = mxq(f64(w1), 1, "e4m3"), mxq(f64(w2), 1, "e4m3")
    xs = mxq(f64(xT), 0, "e4m3")
    hs = silu(w1q[E].T @ xs)
    ys = w2q[E].T @ mxq(hs, 0, "e4m3")
    xq = mxq(f64(xT)[:, idx], 0, "e4m3")
    h = silu(by_expert(w1q, xq))
    y = by_expert(w2q, mxq(h, 0, "e4m3"))
    out = ys
    out[:, idx] += f64(gate) * y
    return out

@@ -1,0 +1,425 @@
+from contextlib import ExitStack
+
+import concourse.mybir as mybir
+
+FLOPS = 3019898880
+
+K, T, E, C, H, N = 1024, 1280, 8, 128, 512, 256
+S = E * C
+SHARED = E
+
+F32 = mybir.dt.float32
+BF16 = mybir.dt.bfloat16
+U32 = mybir.dt.uint32
+U16 = mybir.dt.uint16
+U8 = mybir.dt.uint8
+FP8X4 = mybir.dt.float8_e4m3fn_x4
+SILU = mybir.ActivationFunctionType.Silu
+MULT = mybir.AluOpType.mult
+ADD = mybir.AluOpType.add
+
+P = 128
+PACK = 4
+PASS = P * PACK
+PASSES = K // PASS
+HALF = 512
+VECTOR_HALF = ((2, 0), (2, 1), (3, 0), (3, 1), (4, 0), (5, 0), (6, 0), (7, 0))
+SCALAR_W2 = (7, 8)
+PIECES = {3: (0, 256), 5: (256, 512), 7: (512, 672)}
+TAIL_PIECES = ((672, 1024),)
+SHARED_STEP = (1, 2, 3, 4, 5)
+FINISH = (
+    ((0, 512, "bank3"), (512, 512, "bank3"), (1024, 256, "bank_shared")),
+    ((0, 512, "bank_shared"), (512, 512, "bank_routed"), (1024, 256, "bank_routed")),
+)
+CHUNKS = ((0, 512), (512, 512), (1024, 256))
+VECTOR_X = ((0, 0, 0), (0, 0, 1))
+
+
+def tile_moe_shr_mlp_silu_kernel(tc, xT, w1, w2, gate, offs, out):
+    nc = tc.nc
+    with ExitStack() as ctx:
+        lists = ctx.enter_context(tc.tile_pool(name="lists", bufs=1))
+        held = ctx.enter_context(tc.tile_pool(name="held", bufs=1))
+        ring = ctx.enter_context(tc.tile_pool(name="ring", bufs=2))
+        psum = ctx.enter_context(tc.psum_pool(name="psum", bufs=2))
+
+        offsets = lists.tile([P, S // 16], U16, name="offsets")
+        nc.sync.dma_start(offsets[:], offs)
+
+        zero = held.tile([P, 1], F32, name="zero")
+        zero_out = held.tile([P, 1], F32, name="zero_out")
+        nc.vector.memset(zero[:], 0.0)
+        nc.scalar.activation(zero_out[:], zero[:], SILU)
+
+        gates = held.tile([P, S], F32, name="gates", align_bytes=64)
+        routed = []
+        for b in range(2):
+            window = held.tile([P, T], F32, name=f"routed{b}", align_bytes=64)
+            nc.vector.memset(window[:], 0.0)
+            routed.append(window)
+
+        x_codes = held.tile([P, PASSES, T], U32, name="x_codes", align_bytes=64)
+        x_scales = held.tile([P, PASSES, T], U8, name="x_scales", align_bytes=64)
+        pairs = [held.tile([P, 2, T, 2], BF16, name=f"pairs{c}", align_bytes=64) for c in range(PASSES)]
+        g_codes = held.tile([P, PASSES, S], U32, name="g_codes", align_bytes=64)
+        g_scales = held.tile([P, PASSES, S], U8, name="g_scales", align_bytes=64)
+        hs_codes = held.tile([P, T], U32, name="hs_codes", align_bytes=64)
+        hs_scales = held.tile([P, T], U8, name="hs_scales", align_bytes=64)
+
+        raw = {}
+
+        def load_gates():
+            nc.sync.dma_start(out=gates[:], in_=gate[0:P, :])
+
+        def load_x(c, u, h):
+            tile = ring.tile([P, 2, T // 2], F32, name="raw_x", tag="raw_x", bufs=4, align_bytes=64)
+            rows = xT[c * PASS : (c + 1) * PASS, h * (T // 2) : (h + 1) * (T // 2)].rearrange("(p u e) w -> u p e w", u=2, e=2)
+            nc.sync.dma_start(out=tile[:], in_=rows[u])
+            raw["x", c, u, h] = tile
+
+        def load_w1(e, c):
+            tile = ring.tile([P, PACK, H], F32, name="raw_wide", tag="raw_wide", bufs=7, align_bytes=64)
+            nc.sync.dma_start(out=tile[:], in_=w1[e, c * PASS : (c + 1) * PASS, :].rearrange("(p j) w -> p j w", j=PACK))
+            raw["w1", e, c] = tile
+
+        def load_w2(e):
+            tile = ring.tile([P, PACK, N], F32, name="raw_narrow", tag="raw_narrow", bufs=3, align_bytes=64)
+            nc.sync.dma_start(out=tile[:], in_=w2[e].rearrange("(p j) w -> p j w", j=PACK))
+            raw["w2", e] = tile
+
+        def interleave_words(dst, src):
+            nc.vector.tensor_copy(
+                out=dst.rearrange("p w t -> p (w t)").bitcast(F32).rearrange("p (c i u) -> p c u i", i=4, u=2),
+                in_=src.rearrange("p u w e -> p u (w e)").bitcast(F32).rearrange("p u (c i) -> p c u i", i=4),
+            )
+
+        def interleave(copy, dst, src):
+            copy(
+                out=dst.rearrange("p (c i) t -> p c t i", i=4),
+                in_=src.rearrange("p t (c i) -> p c t i", i=4),
+            )
+
+        grouped = {}
+
+        def pair_x(c, u, h):
+            copy = nc.vector.tensor_copy if (c, u, h) in VECTOR_X else nc.scalar.copy
+            copy(
+                out=pairs[c][:, u, h * (T // 2) : (h + 1) * (T // 2), :].rearrange("p (c i) e -> p c e i", i=4),
+                in_=raw["x", c, u, h][:].rearrange("p e (c i) -> p c e i", i=4),
+            )
+
+        def group_x(c, k):
+            start, width = CHUNKS[k]
+            tile = ring.tile([P, 512, PACK], BF16, name="grouped_x", tag="grouped_x", bufs=2, align_bytes=64)
+            interleave_words(tile[:, 0:width, :], pairs[c][:, :, start : start + width, :])
+            grouped["x", c, k] = tile
+
+        def quantize_x(c, k):
+            start, width = CHUNKS[k]
+            cols = slice(start, start + width)
+            nc.vector.quantize_mx(
+                out=x_codes[:, c, cols].bitcast(FP8X4),
+                scales=x_scales[:, c, cols],
+                in_=grouped["x", c, k][:, 0:width, :].rearrange("p w t -> p (w t)"),
+            )
+
+        looked_up = {}
+
+        def gather(c, half, u):
+            if u == 0:
+                looked_up[c, half] = ring.tile([P, 2, HALF, 2], BF16, name="gathered", tag="gathered", bufs=2, align_bytes=64)
+            window = pairs[c][:, u, :, :].rearrange("p t e -> p (t e)").bitcast(U32)
+            nc.vector.tensor_copy(
+                out=looked_up[c, half][:, u, :, :].rearrange("p t e -> p (t e)").bitcast(U32),
+                in_=window.indirect(offsets[:, half * (HALF // 16) : (half + 1) * (HALF // 16)]),
+            )
+
+        def group_g(c, half):
+            tile = ring.tile([P, HALF, PACK], BF16, name="grouped_g", tag="grouped_g", bufs=2, align_bytes=64)
+            interleave_words(tile[:], looked_up[c, half][:])
+            grouped["g", c, half] = tile
+
+        def quantize_g(c, half):
+            cols = slice(half * HALF, (half + 1) * HALF)
+            nc.vector.quantize_mx(
+                out=g_codes[:, c, cols].bitcast(FP8X4),
+                scales=g_scales[:, c, cols],
+                in_=grouped["g", c, half][:].rearrange("p w t -> p (w t)"),
+            )
+
+        def group_w1(e, c):
+            tile = ring.tile([P, PACK * H], BF16, name="grouped_w1", tag="grouped_w1", bufs=6, align_bytes=64)
+            dst = tile[:].rearrange("p (t m j) -> p m j t", t=PACK, j=PACK)
+            src = raw["w1", e, c][:].rearrange("p j (m t) -> p m j t", t=PACK)
+            if (e, c) in VECTOR_HALF:
+                nc.vector.tensor_copy(out=dst[:, :, :, 0:2], in_=src[:, :, :, 0:2])
+                nc.scalar.copy(out=dst[:, :, :, 2:4], in_=src[:, :, :, 2:4])
+            else:
+                nc.scalar.copy(out=dst, in_=src)
+            grouped["w1", e, c] = tile
+
+        def group_w2(e):
+            copy = nc.scalar.copy if e in SCALAR_W2 else nc.vector.tensor_copy
+            tile = ring.tile([P, N, PACK], BF16, name="grouped_w2", tag="grouped_w2", bufs=3, align_bytes=64)
+            interleave(copy, tile[:], raw["w2", e][:])
+            grouped["w2", e] = tile
+
+        weights = {}
+
+        def quantize_w1(e):
+            if e == SHARED:
+                codes = held.tile([P, PASSES, H], U32, name="shared_codes", align_bytes=64)
+                scales = held.tile([P, PASSES, H], U8, name="shared_scales", align_bytes=64)
+            else:
+                codes = ring.tile([P, PASSES, H], U32, name="w1_codes", tag="w1_codes", bufs=2, align_bytes=64)
+                scales = ring.tile([P, PASSES, H], U8, name="w1_scales", tag="w1_scales", bufs=2, align_bytes=64)
+            for c in range(PASSES):
+                nc.vector.quantize_mx(out=codes[:, c, :].bitcast(FP8X4), scales=scales[:, c, :], in_=grouped["w1", e, c][:])
+            weights["w1", e] = (codes, scales)
+
+        def quantize_w2(e):
+            codes = ring.tile([P, N], U32, name="w2_codes", tag="w2_codes", bufs=4, align_bytes=64)
+            scales = ring.tile([P, N], U8, name="w2_scales", tag="w2_scales", bufs=4, align_bytes=64)
+            nc.vector.quantize_mx(
+                out=codes[:].bitcast(FP8X4), scales=scales[:], in_=grouped["w2", e][:].rearrange("p w t -> p (w t)")
+            )
+            weights["w2", e] = (codes, scales)
+
+        banks = {}
+        hidden = {}
+
+        def multiply1(key, e, codes, scales, start, tag):
+            w_codes, w_scales = weights["w1", e]
+            cols = slice(start, start + C)
+            bank = psum.tile([P, PACK, C], F32, name="bank1", tag=tag, bufs=2)
+            for t in range(PACK):
+                for c in range(PASSES):
+                    rows = slice(t * P, (t + 1) * P)
+                    nc.tensor.matmul_mx(
+                        out=bank[:, t, :],
+                        lhsT=w_codes[:, c, rows].bitcast(FP8X4),
+                        lhsT_scale=w_scales[:, c, rows],
+                        rhs=codes[:, c, cols].bitcast(FP8X4),
+                        rhs_scale=scales[:, c, cols],
+                        start=(c == 0),
+                        stop=(c == PASSES - 1),
+                    )
+            banks[key] = bank
+
+        def multiply1_routed(e):
+            multiply1(e, e, g_codes, g_scales, e * C, "bank_routed")
+
+        def multiply1_shared(q):
+            for n in (2 * q, 2 * q + 1):
+                multiply1(("s", n), SHARED, x_codes, x_scales, n * C, "bank_shared")
+
+        def freed(e, c, first, last):
+            return raw["w1", e, c][:].rearrange("p j w -> p (j w)")[:, first:last].bitcast(BF16).rearrange("p (n t) -> p n t", t=PACK)
+
+        def silu_routed(e):
+            if e + 1 < E:
+                hidden[e] = freed(e + 1, 1, 0, 256)
+            else:
+                tile = ring.tile([P, C, PACK], BF16, name="hidden_routed", tag="hidden_routed", bufs=2, align_bytes=64)
+                hidden[e] = tile[:]
+            nc.scalar.activation(hidden[e], banks[e][:].rearrange("p t n -> p n t"), SILU)
+
+        def silu_shared(q):
+            if SHARED_STEP[q] < E:
+                tile = freed(SHARED_STEP[q], 1, 256, 768)
+            else:
+                own = ring.tile([P, 2 * C, PACK], BF16, name="hidden_shared", tag="hidden_shared", bufs=2, align_bytes=64)
+                tile = own[:]
+            for part in range(2):
+                nc.scalar.activation(
+                    tile[:, part * C : (part + 1) * C, :], banks["s", 2 * q + part][:].rearrange("p t n -> p n t"), SILU
+                )
+            hidden["s", q] = tile
+
+        def quantize_hs(q):
+            cols = slice(q * 2 * C, (q + 1) * 2 * C)
+            nc.vector.quantize_mx(
+                out=hs_codes[:, cols].bitcast(FP8X4),
+                scales=hs_scales[:, cols],
+                in_=hidden["s", q].rearrange("p w t -> p (w t)"),
+            )
+
+        hidden_codes = {}
+
+        def quantize_h(e):
+            codes = ring.tile([P, C], U32, name="h_codes", tag="h_codes", bufs=3, align_bytes=64)
+            scales = ring.tile([P, C], U8, name="h_scales", tag="h_scales", bufs=3, align_bytes=64)
+            nc.vector.quantize_mx(
+                out=codes[:].bitcast(FP8X4), scales=scales[:], in_=hidden[e].rearrange("p w t -> p (w t)")
+            )
+            hidden_codes[e] = (codes, scales)
+
+        y_place = {}
+
+        def next_y(e):
+            if e < 2:
+                return 0, 2, 3
+            if e < 4:
+                return 2, 4, 5
+            return 4, 8, 7
+
+        def multiply2(e):
+            h_codes, h_scales = hidden_codes[e]
+            w_codes, w_scales = weights["w2", e]
+            bank = psum.tile([P, 2, C], F32, name="bank2", tag="bank2", bufs=2)
+            for b in range(2):
+                rows = slice(b * P, (b + 1) * P)
+                nc.tensor.matmul_mx(
+                    out=bank[:, b, :],
+                    lhsT=w_codes[:, rows].bitcast(FP8X4),
+                    lhsT_scale=w_scales[:, rows],
+                    rhs=h_codes[:].bitcast(FP8X4),
+                    rhs_scale=h_scales[:],
+                    start=True,
+                    stop=True,
+                )
+            banks["y", e] = bank
+
+        def copy_y(e):
+            first, last, late = next_y(e)
+            words = raw["w1", late, 1][:].rearrange("p j w -> p (j w)")[:, 768 : 768 + 2 * C * (last - first)]
+            y_place[e] = (words.rearrange("p (b n) -> p b n", b=2), first * C)
+            place, base = y_place[e]
+            nc.scalar.copy(out=place[:, :, e * C - base : (e + 1) * C - base], in_=banks["y", e][:])
+
+        def scatter(b, first, last):
+            place, base = y_place[first // C]
+            nc.vector.tensor_tensor(
+                routed[b][:].indirect(offsets[:, first // 16 : last // 16]),
+                place[:, b, first - base : last - base],
+                gates[:, first:last],
+                MULT,
+            )
+
+        def finish(b, start, width, tag):
+            w_codes, w_scales = weights["w2", SHARED]
+            rows = slice(b * P, (b + 1) * P)
+            cols = slice(start, start + width)
+            bank = psum.tile([P, 512], F32, name="bank3", tag=tag, bufs=2)
+            nc.tensor.matmul_mx(
+                out=bank[:, 0:width],
+                lhsT=w_codes[:, rows].bitcast(FP8X4),
+                lhsT_scale=w_scales[:, rows],
+                rhs=hs_codes[:, cols].bitcast(FP8X4),
+                rhs_scale=hs_scales[:, cols],
+                start=True,
+                stop=True,
+            )
+            if b == 0:
+                tile = ring.tile([P, T // 2], F32, name="raw_x", tag="raw_x", bufs=4, align_bytes=64)
+            else:
+                tile = ring.tile([P, 512], F32, name="raw_narrow", tag="raw_narrow", bufs=3, align_bytes=64)
+            nc.vector.tensor_tensor(tile[:, 0:width], bank[:, 0:width], routed[b][:, cols], ADD)
+            nc.sync.dma_start(out=out[rows, cols], in_=tile[:, 0:width])
+
+        for h in range(2):
+            load_x(0, 0, h)
+        for h in range(2):
+            load_x(0, 1, h)
+        load_w1(SHARED, 0)
+        for h in range(2):
+            pair_x(0, 0, h)
+            load_x(1, 0, h)
+        load_w1(SHARED, 1)
+        gather(0, 0, 0)
+        gather(0, 1, 0)
+        for h in range(2):
+            pair_x(0, 1, h)
+            load_x(1, 1, h)
+        load_w1(0, 0)
+        load_w1(0, 1)
+        load_w1(1, 0)
+        load_w1(1, 1)
+        load_w2(0)
+        gather(0, 0, 1)
+        group_w1(SHARED, 0)
+        group_g(0, 0)
+        gather(0, 1, 1)
+        pair_x(1, 0, 0)
+        pair_x(1, 0, 1)
+        quantize_g(0, 0)
+        group_g(0, 1)
+        group_x(0, 0)
+        quantize_g(0, 1)
+        gather(1, 0, 0)
+        quantize_x(0, 0)
+        group_x(0, 1)
+        group_w1(SHARED, 1)
+        pair_x(1, 1, 0)
+        pair_x(1, 1, 1)
+        gather(1, 1, 0)
+        quantize_x(0, 1)
+        group_x(0, 2)
+        gather(1, 0, 1)
+        quantize_x(0, 2)
+        group_g(1, 0)
+        load_w1(2, 0)
+        load_w1(2, 1)
+        load_w2(1)
+        gather(1, 1, 1)
+        quantize_g(1, 0)
+        group_x(1, 0)
+        group_g(1, 1)
+        quantize_x(1, 0)
+        group_x(1, 1)
+        quantize_g(1, 1)
+        quantize_x(1, 1)
+        group_x(1, 2)
+        quantize_x(1, 2)
+        load_gates()
+
+        for i in range(E + 2):
+            prev = SHARED if i == 0 else i - 1
+            if i <= E:
+                quantize_w1(prev)
+            if i >= 2:
+                quantize_h(i - 2)
+                quantize_w2(i - 2)
+            for q in range(5):
+                if SHARED_STEP[q] == i - 1:
+                    quantize_hs(q)
+            if i < E:
+                group_w1(i, 0)
+                group_w1(i, 1)
+            if 1 <= i <= E:
+                multiply1_routed(i - 1)
+            if i >= 2:
+                multiply2(i - 2)
+            for q in range(5):
+                if SHARED_STEP[q] == i + 1:
+                    multiply1_shared(q)
+            if i in (3, 5, 7):
+                copy_y(i - 3)
+                copy_y(i - 2)
+            if 1 <= i <= E:
+                silu_routed(i - 1)
+            for q in range(5):
+                if SHARED_STEP[q] == i:
+                    silu_shared(q)
+            if i in PIECES:
+                scatter(0, *PIECES[i])
+                scatter(1, *PIECES[i])
+            if 1 <= i <= E:
+                group_w2(i - 1)
+            if i == E:
+                group_w2(SHARED)
+                quantize_w2(SHARED)
+            if i + 3 < E:
+                load_w1(i + 3, 0)
+                load_w1(i + 3, 1)
+            if 1 <= i + 1 and i + 2 <= E:
+                load_w2(i + 2)
+
+        copy_y(6)
+        copy_y(7)
+        for b in range(2):
+            for piece in TAIL_PIECES:
+                scatter(b, *piece)
+            for start, width, tag in FINISH[b]:
+                finish(b, start, width, tag)

@@ -23,17 +23,11 @@ PACK = 4
 PASS = P * PACK
 PASSES = K // PASS
 HALF = 512
-VECTOR_HALF = ((2, 0), (2, 1), (3, 0), (3, 1), (4, 0), (5, 0), (6, 0), (7, 0))
-SCALAR_W2 = (7, 8)
-PIECES = {3: (0, 256), 5: (256, 512), 7: (512, 672)}
-TAIL_PIECES = ((672, 1024),)
-SHARED_STEP = (1, 2, 3, 4, 5)
-FINISH = (
-    ((0, 512, "bank3"), (512, 512, "bank3"), (1024, 256, "bank_shared")),
-    ((0, 512, "bank_shared"), (512, 512, "bank_routed"), (1024, 256, "bank_routed")),
-)
-CHUNKS = ((0, 512), (512, 512), (1024, 256))
-VECTOR_X = ((0, 0, 0), (0, 0, 1))
+RAW_BUFS = 12
+PIECES = {1: (0, 224), 2: (224, 384), 4: (384, 544), 5: (544, 704), 6: (704, 864), 7: (864, 1024)}
+GATE = 3
+X_CUTS = ((0, 1024), (1024, 256))
+FINISH = ((0, 512), (512, 512), (1024, 256))
 
 
 def tile_moe_shr_mlp_silu_kernel(tc, xT, w1, w2, gate, offs, out):
@@ -45,265 +39,228 @@ def tile_moe_shr_mlp_silu_kernel(tc, xT, w1, w2, gate, offs, out):
         psum = ctx.enter_context(tc.psum_pool(name="psum", bufs=2))
 
         offsets = lists.tile([P, S // 16], U16, name="offsets")
-        nc.sync.dma_start(offsets[:], offs)
 
         zero = held.tile([P, 1], F32, name="zero")
         zero_out = held.tile([P, 1], F32, name="zero_out")
         nc.vector.memset(zero[:], 0.0)
         nc.scalar.activation(zero_out[:], zero[:], SILU)
 
-        gates = held.tile([P, S], F32, name="gates", align_bytes=64)
         routed = []
         for b in range(2):
             window = held.tile([P, T], F32, name=f"routed{b}", align_bytes=64)
             nc.vector.memset(window[:], 0.0)
             routed.append(window)
 
-        x_codes = held.tile([P, PASSES, T], U32, name="x_codes", align_bytes=64)
-        x_scales = held.tile([P, PASSES, T], U8, name="x_scales", align_bytes=64)
-        pairs = [held.tile([P, 2, T, 2], BF16, name=f"pairs{c}", align_bytes=64) for c in range(PASSES)]
-        g_codes = held.tile([P, PASSES, S], U32, name="g_codes", align_bytes=64)
-        g_scales = held.tile([P, PASSES, S], U8, name="g_scales", align_bytes=64)
-        hs_codes = held.tile([P, T], U32, name="hs_codes", align_bytes=64)
+        x_codes = held.tile([P, PASSES * T], U32, name="x_codes", align_bytes=64)
+        x_scales = held.tile([P, PASSES * T], U8, name="x_scales", align_bytes=64)
+        pairs = [held.tile([P, 4 * T], BF16, name=f"pairs{c}", tag=f"pairs{c}", align_bytes=64) for c in range(PASSES)]
+        g_codes = held.tile([P, PASSES * S], U32, name="g_codes", align_bytes=64)
+        g_scales = held.tile([P, PASSES * S], U8, name="g_scales", align_bytes=64)
         hs_scales = held.tile([P, T], U8, name="hs_scales", align_bytes=64)
 
         raw = {}
 
-        def load_gates():
-            nc.sync.dma_start(out=gates[:], in_=gate[0:P, :])
+        def raw_tile():
+            return ring.tile([P, PACK * H], F32, name="raw", tag="raw", bufs=RAW_BUFS, align_bytes=64)
 
         def load_x(c, u, h):
-            tile = ring.tile([P, 2, T // 2], F32, name="raw_x", tag="raw_x", bufs=4, align_bytes=64)
+            tile = raw_tile()
             rows = xT[c * PASS : (c + 1) * PASS, h * (T // 2) : (h + 1) * (T // 2)].rearrange("(p u e) w -> u p e w", u=2, e=2)
-            nc.sync.dma_start(out=tile[:], in_=rows[u])
+            nc.sync.dma_start(out=tile[:, 0:T].rearrange("p (e w) -> p e w", e=2), in_=rows[u])
             raw["x", c, u, h] = tile
 
         def load_w1(e, c):
-            tile = ring.tile([P, PACK, H], F32, name="raw_wide", tag="raw_wide", bufs=7, align_bytes=64)
-            nc.sync.dma_start(out=tile[:], in_=w1[e, c * PASS : (c + 1) * PASS, :].rearrange("(p j) w -> p j w", j=PACK))
+            tile = raw_tile()
+            nc.sync.dma_start(out=tile[:], in_=w1[e, c * PASS : (c + 1) * PASS, :].rearrange("(p j) w -> p (j w)", j=PACK))
             raw["w1", e, c] = tile
 
         def load_w2(e):
-            tile = ring.tile([P, PACK, N], F32, name="raw_narrow", tag="raw_narrow", bufs=3, align_bytes=64)
-            nc.sync.dma_start(out=tile[:], in_=w2[e].rearrange("(p j) w -> p j w", j=PACK))
+            tile = raw_tile()
+            nc.sync.dma_start(out=tile[:, 0 : PACK * N], in_=w2[e].rearrange("(p j) w -> p (j w)", j=PACK))
             raw["w2", e] = tile
 
         def interleave_words(dst, src):
             nc.vector.tensor_copy(
-                out=dst.rearrange("p w t -> p (w t)").bitcast(F32).rearrange("p (c i u) -> p c u i", i=4, u=2),
-                in_=src.rearrange("p u w e -> p u (w e)").bitcast(F32).rearrange("p u (c i) -> p c u i", i=4),
-            )
-
-        def interleave(copy, dst, src):
-            copy(
-                out=dst.rearrange("p (c i) t -> p c t i", i=4),
-                in_=src.rearrange("p t (c i) -> p c t i", i=4),
+                out=dst.bitcast(F32).rearrange("p (c i u) -> p c u i", i=4, u=2),
+                in_=src.rearrange("p u (c i) -> p c u i", i=4),
             )
 
         grouped = {}
 
-        def pair_x(c, u, h):
-            copy = nc.vector.tensor_copy if (c, u, h) in VECTOR_X else nc.scalar.copy
+        def pair_x(c, u, h, copy):
+            first = u * 2 * T + h * T
             copy(
-                out=pairs[c][:, u, h * (T // 2) : (h + 1) * (T // 2), :].rearrange("p (c i) e -> p c e i", i=4),
-                in_=raw["x", c, u, h][:].rearrange("p e (c i) -> p c e i", i=4),
+                out=pairs[c][:, first : first + T].rearrange("p (c i e) -> p c e i", i=4, e=2),
+                in_=raw["x", c, u, h][:, 0:T].rearrange("p (e c i) -> p c e i", i=4, e=2),
             )
 
-        def group_x(c, k):
-            start, width = CHUNKS[k]
-            tile = ring.tile([P, 512, PACK], BF16, name="grouped_x", tag="grouped_x", bufs=2, align_bytes=64)
-            interleave_words(tile[:, 0:width, :], pairs[c][:, :, start : start + width, :])
-            grouped["x", c, k] = tile
+        def group_x(c):
+            tile = ring.tile([P, PACK * T], BF16, name="grouped_x", tag="grouped_x", bufs=1, align_bytes=64)
+            interleave_words(tile[:], pairs[c][:].bitcast(F32).rearrange("p (u t) -> p u t", u=2))
+            grouped["x", c] = tile
 
-        def quantize_x(c, k):
-            start, width = CHUNKS[k]
-            cols = slice(start, start + width)
-            nc.vector.quantize_mx(
-                out=x_codes[:, c, cols].bitcast(FP8X4),
-                scales=x_scales[:, c, cols],
-                in_=grouped["x", c, k][:, 0:width, :].rearrange("p w t -> p (w t)"),
-            )
+        def quantize_x(c):
+            for start, width in X_CUTS:
+                cols = slice(c * T + start, c * T + start + width)
+                nc.vector.quantize_mx(
+                    out=x_codes[:, cols].bitcast(FP8X4),
+                    scales=x_scales[:, cols],
+                    in_=grouped["x", c][:, PACK * start : PACK * (start + width)],
+                )
 
         looked_up = {}
 
-        def gather(c, half, u):
+        def gather(c, u):
             if u == 0:
-                looked_up[c, half] = ring.tile([P, 2, HALF, 2], BF16, name="gathered", tag="gathered", bufs=2, align_bytes=64)
-            window = pairs[c][:, u, :, :].rearrange("p t e -> p (t e)").bitcast(U32)
-            nc.vector.tensor_copy(
-                out=looked_up[c, half][:, u, :, :].rearrange("p t e -> p (t e)").bitcast(U32),
-                in_=window.indirect(offsets[:, half * (HALF // 16) : (half + 1) * (HALF // 16)]),
-            )
+                looked_up[c] = ring.tile([P, 2 * S], U32, name="gathered", tag="gathered", bufs=1, align_bytes=64)
+            window = pairs[c][:, u * 2 * T : (u + 1) * 2 * T].bitcast(U32)
+            for half in range(2):
+                nc.vector.tensor_copy(
+                    out=looked_up[c][:, u * S + half * HALF : u * S + (half + 1) * HALF],
+                    in_=window.indirect(offsets[:, half * (HALF // 16) : (half + 1) * (HALF // 16)]),
+                )
 
-        def group_g(c, half):
-            tile = ring.tile([P, HALF, PACK], BF16, name="grouped_g", tag="grouped_g", bufs=2, align_bytes=64)
-            interleave_words(tile[:], looked_up[c, half][:])
-            grouped["g", c, half] = tile
+        def group_g(c):
+            tile = ring.tile([P, PACK * S], BF16, name="grouped_g", tag="grouped_g", bufs=1, align_bytes=64)
+            interleave_words(tile[:], looked_up[c][:].bitcast(F32).rearrange("p (u t) -> p u t", u=2))
+            grouped["g", c] = tile
 
-        def quantize_g(c, half):
-            cols = slice(half * HALF, (half + 1) * HALF)
-            nc.vector.quantize_mx(
-                out=g_codes[:, c, cols].bitcast(FP8X4),
-                scales=g_scales[:, c, cols],
-                in_=grouped["g", c, half][:].rearrange("p w t -> p (w t)"),
-            )
+        def quantize_g(c):
+            cols = slice(c * S, (c + 1) * S)
+            nc.vector.quantize_mx(out=g_codes[:, cols].bitcast(FP8X4), scales=g_scales[:, cols], in_=grouped["g", c][:])
 
-        def group_w1(e, c):
+        def group_w1(e, c, copy, between=None):
             tile = ring.tile([P, PACK * H], BF16, name="grouped_w1", tag="grouped_w1", bufs=6, align_bytes=64)
             dst = tile[:].rearrange("p (t m j) -> p m j t", t=PACK, j=PACK)
-            src = raw["w1", e, c][:].rearrange("p j (m t) -> p m j t", t=PACK)
-            if (e, c) in VECTOR_HALF:
+            src = raw["w1", e, c][:].rearrange("p (j m t) -> p m j t", t=PACK, j=PACK)
+            if copy is None:
                 nc.vector.tensor_copy(out=dst[:, :, :, 0:2], in_=src[:, :, :, 0:2])
                 nc.scalar.copy(out=dst[:, :, :, 2:4], in_=src[:, :, :, 2:4])
+            elif between is not None:
+                copy(out=dst[:, 0 : P // 2], in_=src[:, 0 : P // 2])
+                copy(out=dst[:, P // 2 : 5 * P // 8], in_=src[:, P // 2 : 5 * P // 8])
+                between()
+                copy(out=dst[:, 5 * P // 8 : P], in_=src[:, 5 * P // 8 : P])
             else:
-                nc.scalar.copy(out=dst, in_=src)
+                copy(out=dst, in_=src)
             grouped["w1", e, c] = tile
 
-        def group_w2(e):
-            copy = nc.scalar.copy if e in SCALAR_W2 else nc.vector.tensor_copy
-            tile = ring.tile([P, N, PACK], BF16, name="grouped_w2", tag="grouped_w2", bufs=3, align_bytes=64)
-            interleave(copy, tile[:], raw["w2", e][:])
+        def group_w2(e, copy):
+            tile = ring.tile([P, PACK * N], BF16, name="grouped_w2", tag="grouped_w2", bufs=2, align_bytes=64)
+            copy(
+                out=tile[:].rearrange("p (c i t) -> p c t i", i=4, t=PACK),
+                in_=raw["w2", e][:, 0 : PACK * N].rearrange("p (t c i) -> p c t i", i=4, t=PACK),
+            )
             grouped["w2", e] = tile
 
         weights = {}
 
-        def quantize_w1(e):
-            if e == SHARED:
-                codes = held.tile([P, PASSES, H], U32, name="shared_codes", align_bytes=64)
-                scales = held.tile([P, PASSES, H], U8, name="shared_scales", align_bytes=64)
-            else:
-                codes = ring.tile([P, PASSES, H], U32, name="w1_codes", tag="w1_codes", bufs=2, align_bytes=64)
-                scales = ring.tile([P, PASSES, H], U8, name="w1_scales", tag="w1_scales", bufs=2, align_bytes=64)
-            for c in range(PASSES):
-                nc.vector.quantize_mx(out=codes[:, c, :].bitcast(FP8X4), scales=scales[:, c, :], in_=grouped["w1", e, c][:])
-            weights["w1", e] = (codes, scales)
+        def quantize_w1(e, c):
+            if c == 0:
+                tag = "shared" if e == SHARED else "w1"
+                bufs = 1 if e == SHARED else 2
+                codes = ring.tile([P, PASSES * H], U32, name="w1_codes", tag=tag + "_codes", bufs=bufs, align_bytes=64)
+                scales = ring.tile([P, PASSES * H], U8, name="w1_scales", tag=tag + "_scales", bufs=bufs, align_bytes=64)
+                weights["w1", e] = (codes, scales)
+            codes, scales = weights["w1", e]
+            cols = slice(c * H, (c + 1) * H)
+            nc.vector.quantize_mx(out=codes[:, cols].bitcast(FP8X4), scales=scales[:, cols], in_=grouped["w1", e, c][:])
 
         def quantize_w2(e):
             codes = ring.tile([P, N], U32, name="w2_codes", tag="w2_codes", bufs=4, align_bytes=64)
             scales = ring.tile([P, N], U8, name="w2_scales", tag="w2_scales", bufs=4, align_bytes=64)
-            nc.vector.quantize_mx(
-                out=codes[:].bitcast(FP8X4), scales=scales[:], in_=grouped["w2", e][:].rearrange("p w t -> p (w t)")
-            )
+            nc.vector.quantize_mx(out=codes[:].bitcast(FP8X4), scales=scales[:], in_=grouped["w2", e][:])
             weights["w2", e] = (codes, scales)
 
         banks = {}
         hidden = {}
 
-        def multiply1(key, e, codes, scales, start, tag):
+        def multiply1(key, e, codes, scales, width, start, tag):
             w_codes, w_scales = weights["w1", e]
-            cols = slice(start, start + C)
-            bank = psum.tile([P, PACK, C], F32, name="bank1", tag=tag, bufs=2)
+            bank = psum.tile([P, PACK * C], F32, name="bank1", tag=tag, bufs=2)
             for t in range(PACK):
                 for c in range(PASSES):
-                    rows = slice(t * P, (t + 1) * P)
+                    rows = slice(c * H + t * P, c * H + (t + 1) * P)
+                    cols = slice(c * width + start, c * width + start + C)
                     nc.tensor.matmul_mx(
-                        out=bank[:, t, :],
-                        lhsT=w_codes[:, c, rows].bitcast(FP8X4),
-                        lhsT_scale=w_scales[:, c, rows],
-                        rhs=codes[:, c, cols].bitcast(FP8X4),
-                        rhs_scale=scales[:, c, cols],
+                        out=bank[:, t * C : (t + 1) * C],
+                        lhsT=w_codes[:, rows].bitcast(FP8X4),
+                        lhsT_scale=w_scales[:, rows],
+                        rhs=codes[:, cols].bitcast(FP8X4),
+                        rhs_scale=scales[:, cols],
                         start=(c == 0),
                         stop=(c == PASSES - 1),
                     )
             banks[key] = bank
 
-        def multiply1_routed(e):
-            multiply1(e, e, g_codes, g_scales, e * C, "bank_routed")
+        def freed(e, c, j):
+            return raw["w1", e, c][:, j * H + H // 2 : (j + 1) * H].bitcast(BF16)
 
-        def multiply1_shared(q):
-            for n in (2 * q, 2 * q + 1):
-                multiply1(("s", n), SHARED, x_codes, x_scales, n * C, "bank_shared")
-
-        def freed(e, c, first, last):
-            return raw["w1", e, c][:].rearrange("p j w -> p (j w)")[:, first:last].bitcast(BF16).rearrange("p (n t) -> p n t", t=PACK)
-
-        def silu_routed(e):
-            if e + 1 < E:
-                hidden[e] = freed(e + 1, 1, 0, 256)
-            else:
-                tile = ring.tile([P, C, PACK], BF16, name="hidden_routed", tag="hidden_routed", bufs=2, align_bytes=64)
-                hidden[e] = tile[:]
-            nc.scalar.activation(hidden[e], banks[e][:].rearrange("p t n -> p n t"), SILU)
-
-        def silu_shared(q):
-            if SHARED_STEP[q] < E:
-                tile = freed(SHARED_STEP[q], 1, 256, 768)
-            else:
-                own = ring.tile([P, 2 * C, PACK], BF16, name="hidden_shared", tag="hidden_shared", bufs=2, align_bytes=64)
-                tile = own[:]
-            for part in range(2):
-                nc.scalar.activation(
-                    tile[:, part * C : (part + 1) * C, :], banks["s", 2 * q + part][:].rearrange("p t n -> p n t"), SILU
-                )
-            hidden["s", q] = tile
-
-        def quantize_hs(q):
-            cols = slice(q * 2 * C, (q + 1) * 2 * C)
-            nc.vector.quantize_mx(
-                out=hs_codes[:, cols].bitcast(FP8X4),
-                scales=hs_scales[:, cols],
-                in_=hidden["s", q].rearrange("p w t -> p (w t)"),
+        def silu(place, key):
+            nc.scalar.activation(
+                place.rearrange("p (n t) -> p n t", t=PACK), banks[key][:].rearrange("p (t n) -> p n t", t=PACK), SILU
             )
 
         hidden_codes = {}
 
-        def quantize_h(e):
-            codes = ring.tile([P, C], U32, name="h_codes", tag="h_codes", bufs=3, align_bytes=64)
-            scales = ring.tile([P, C], U8, name="h_scales", tag="h_scales", bufs=3, align_bytes=64)
-            nc.vector.quantize_mx(
-                out=codes[:].bitcast(FP8X4), scales=scales[:], in_=hidden[e].rearrange("p w t -> p (w t)")
-            )
+        def first_routed(e, place):
+            multiply1(e, e, g_codes, g_scales, S, e * C, "bank_routed")
+            silu(place, e)
+            hidden[e] = place
+
+        def quantize_h(e, behind=None):
+            if behind is None:
+                own_codes = ring.tile([P, C], U32, name="h_codes", tag="h_codes", bufs=3, align_bytes=64)
+                own_scales = ring.tile([P, C], U8, name="h_scales", tag="h_scales", bufs=3, align_bytes=64)
+                codes, scales = own_codes[:], own_scales[:]
+            else:
+                codes, scales = behind[:, 0:C].bitcast(U32), behind[:, C : C + C // 4].bitcast(U8)
+            nc.vector.quantize_mx(out=codes.bitcast(FP8X4), scales=scales, in_=hidden[e])
             hidden_codes[e] = (codes, scales)
 
-        y_place = {}
+        def first_shared(n, place):
+            multiply1(("s", n), SHARED, x_codes, x_scales, T, n * C, "bank_shared")
+            silu(place, ("s", n))
 
-        def next_y(e):
-            if e < 2:
-                return 0, 2, 3
-            if e < 4:
-                return 2, 4, 5
-            return 4, 8, 7
+        def quantize_hs(q, place):
+            cols = slice(q * 2 * C, (q + 1) * 2 * C)
+            nc.vector.quantize_mx(out=hs_codes[:, cols].bitcast(FP8X4), scales=hs_scales[:, cols], in_=place)
 
-        def multiply2(e):
+        def second_routed(e, tag, copy):
             h_codes, h_scales = hidden_codes[e]
             w_codes, w_scales = weights["w2", e]
-            bank = psum.tile([P, 2, C], F32, name="bank2", tag="bank2", bufs=2)
+            bank = psum.tile([P, 2 * C], F32, name="bank2", tag=tag, bufs=1)
             for b in range(2):
                 rows = slice(b * P, (b + 1) * P)
                 nc.tensor.matmul_mx(
-                    out=bank[:, b, :],
+                    out=bank[:, b * C : (b + 1) * C],
                     lhsT=w_codes[:, rows].bitcast(FP8X4),
                     lhsT_scale=w_scales[:, rows],
-                    rhs=h_codes[:].bitcast(FP8X4),
-                    rhs_scale=h_scales[:],
+                    rhs=h_codes.bitcast(FP8X4),
+                    rhs_scale=h_scales,
                     start=True,
                     stop=True,
                 )
-            banks["y", e] = bank
-
-        def copy_y(e):
-            first, last, late = next_y(e)
-            words = raw["w1", late, 1][:].rearrange("p j w -> p (j w)")[:, 768 : 768 + 2 * C * (last - first)]
-            y_place[e] = (words.rearrange("p (b n) -> p b n", b=2), first * C)
-            place, base = y_place[e]
-            nc.scalar.copy(out=place[:, :, e * C - base : (e + 1) * C - base], in_=banks["y", e][:])
-
-        def scatter(b, first, last):
-            place, base = y_place[first // C]
-            nc.vector.tensor_tensor(
-                routed[b][:].indirect(offsets[:, first // 16 : last // 16]),
-                place[:, b, first - base : last - base],
-                gates[:, first:last],
-                MULT,
+            copy(
+                out=y[:].rearrange("p (b s) -> p b s", b=2)[:, :, e * C : (e + 1) * C],
+                in_=bank[:].rearrange("p (b n) -> p b n", b=2),
             )
 
-        def finish(b, start, width, tag):
+        def scatter(first, last):
+            for b in range(2):
+                nc.vector.tensor_tensor(
+                    routed[b][:].indirect(offsets[:, first // 16 : last // 16]),
+                    y[:, b * S + first : b * S + last],
+                    gates[:, first:last],
+                    MULT,
+                )
+
+        def second_shared(b, start, width, bank):
             w_codes, w_scales = weights["w2", SHARED]
             rows = slice(b * P, (b + 1) * P)
             cols = slice(start, start + width)
-            bank = psum.tile([P, 512], F32, name="bank3", tag=tag, bufs=2)
             nc.tensor.matmul_mx(
-                out=bank[:, 0:width],
+                out=bank,
                 lhsT=w_codes[:, rows].bitcast(FP8X4),
                 lhsT_scale=w_scales[:, rows],
                 rhs=hs_codes[:, cols].bitcast(FP8X4),
@@ -311,115 +268,110 @@ def tile_moe_shr_mlp_silu_kernel(tc, xT, w1, w2, gate, offs, out):
                 start=True,
                 stop=True,
             )
-            if b == 0:
-                tile = ring.tile([P, T // 2], F32, name="raw_x", tag="raw_x", bufs=4, align_bytes=64)
-            else:
-                tile = ring.tile([P, 512], F32, name="raw_narrow", tag="raw_narrow", bufs=3, align_bytes=64)
-            nc.vector.tensor_tensor(tile[:, 0:width], bank[:, 0:width], routed[b][:, cols], ADD)
+
+        def finish(b, start, width, bank):
+            rows = slice(b * P, (b + 1) * P)
+            cols = slice(start, start + width)
+            tile = raw_tile()
+            nc.vector.tensor_tensor(tile[:, 0:width], bank, routed[b][:, cols], ADD)
             nc.sync.dma_start(out=out[rows, cols], in_=tile[:, 0:width])
 
-        for h in range(2):
-            load_x(0, 0, h)
-        for h in range(2):
-            load_x(0, 1, h)
-        load_w1(SHARED, 0)
-        for h in range(2):
-            pair_x(0, 0, h)
-            load_x(1, 0, h)
-        load_w1(SHARED, 1)
-        gather(0, 0, 0)
-        gather(0, 1, 0)
-        for h in range(2):
-            pair_x(0, 1, h)
-            load_x(1, 1, h)
-        load_w1(0, 0)
-        load_w1(0, 1)
-        load_w1(1, 0)
-        load_w1(1, 1)
-        load_w2(0)
-        gather(0, 0, 1)
-        group_w1(SHARED, 0)
-        group_g(0, 0)
-        gather(0, 1, 1)
-        pair_x(1, 0, 0)
-        pair_x(1, 0, 1)
-        quantize_g(0, 0)
-        group_g(0, 1)
-        group_x(0, 0)
-        quantize_g(0, 1)
-        gather(1, 0, 0)
-        quantize_x(0, 0)
-        group_x(0, 1)
-        group_w1(SHARED, 1)
-        pair_x(1, 1, 0)
-        pair_x(1, 1, 1)
-        gather(1, 1, 0)
-        quantize_x(0, 1)
-        group_x(0, 2)
-        gather(1, 0, 1)
-        quantize_x(0, 2)
-        group_g(1, 0)
-        load_w1(2, 0)
-        load_w1(2, 1)
-        load_w2(1)
-        gather(1, 1, 1)
-        quantize_g(1, 0)
-        group_x(1, 0)
-        group_g(1, 1)
-        quantize_x(1, 0)
-        group_x(1, 1)
-        quantize_g(1, 1)
-        quantize_x(1, 1)
-        group_x(1, 2)
-        quantize_x(1, 2)
-        load_gates()
+        load_x(0, 0, 0)
+        load_x(0, 0, 1)
+        nc.sync.dma_start(offsets[:], offs)
+        for c, u in ((0, 1), (1, 0), (1, 1)):
+            load_x(c, u, 0)
+            load_x(c, u, 1)
+        for c in range(PASSES):
+            for u in range(2):
+                for h in range(2):
+                    pair_x(c, u, h, nc.vector.tensor_copy if (c, u) == (0, 0) else nc.scalar.copy)
+                gather(c, u)
+            group_g(c)
+            group_x(c)
+            quantize_g(c)
+            quantize_x(c)
+        y = held.tile([P, 2 * S], F32, name="y", tag="pairs0", align_bytes=64)
+        hs_codes = held.tile([P, T], U32, name="hs_codes", tag="pairs1", align_bytes=64)
+        gates = ring.tile([P, S], F32, name="gates", tag="gathered", bufs=1, align_bytes=64)
 
-        for i in range(E + 2):
-            prev = SHARED if i == 0 else i - 1
-            if i <= E:
-                quantize_w1(prev)
-            if i >= 2:
-                quantize_h(i - 2)
-                quantize_w2(i - 2)
-            for q in range(5):
-                if SHARED_STEP[q] == i - 1:
-                    quantize_hs(q)
-            if i < E:
-                group_w1(i, 0)
-                group_w1(i, 1)
-            if 1 <= i <= E:
-                multiply1_routed(i - 1)
-            if i >= 2:
-                multiply2(i - 2)
-            for q in range(5):
-                if SHARED_STEP[q] == i + 1:
-                    multiply1_shared(q)
-            if i in (3, 5, 7):
-                copy_y(i - 3)
-                copy_y(i - 2)
-            if 1 <= i <= E:
-                silu_routed(i - 1)
-            for q in range(5):
-                if SHARED_STEP[q] == i:
-                    silu_shared(q)
-            if i in PIECES:
-                scatter(0, *PIECES[i])
-                scatter(1, *PIECES[i])
-            if 1 <= i <= E:
-                group_w2(i - 1)
-            if i == E:
-                group_w2(SHARED)
-                quantize_w2(SHARED)
-            if i + 3 < E:
-                load_w1(i + 3, 0)
-                load_w1(i + 3, 1)
-            if 1 <= i + 1 and i + 2 <= E:
-                load_w2(i + 2)
+        def prepare(e, c, copy, between=None):
+            load_w1(e, c)
+            group_w1(e, c, copy, between)
+            quantize_w1(e, c)
 
-        copy_y(6)
-        copy_y(7)
+        def prepare_w2(e, copy):
+            load_w2(e)
+            group_w2(e, copy)
+            quantize_w2(e)
+
+        def back(e, copy):
+            second_routed(e, "bank2", copy)
+            if e in PIECES:
+                scatter(*PIECES[e])
+
+        def shared_pair(q):
+            if q == 0:
+                place = raw["w1", 1, 1][:, 3 * H : 4 * H].bitcast(BF16)
+            else:
+                own = ring.tile([P, 2 * PACK * C], BF16, name="hidden_shared", tag="hidden_shared", bufs=2, align_bytes=64)
+                place = own[:]
+            for part in range(2):
+                first_shared(2 * q + part, place[:, part * H : (part + 1) * H])
+            quantize_hs(q, place)
+
+        def hidden_place(e):
+            tile = ring.tile([P, PACK * C], BF16, name="hidden", tag="hidden", bufs=2, align_bytes=64)
+            return tile[:]
+
+        on_vector, on_scalar = nc.vector.tensor_copy, nc.scalar.copy
+        for e in (SHARED, 0, 1):
+            prepare(e, 0, on_scalar)
+            prepare(e, 1, on_scalar)
+        shared_pair(0)
+        first_routed(0, freed(1, 1, 0))
+        quantize_h(0)
+        prepare(2, 0, on_vector)
+        shared_pair(1)
+        first_routed(1, freed(1, 1, 1))
+        quantize_h(1)
+        shared_pair(2)
+        prepare(2, 1, on_vector)
+        shared_pair(3)
+        shared_pair(4)
+        prepare_w2(0, on_vector)
+        back(0, on_vector)
+        prepare_w2(1, on_vector)
+        second_routed(1, "bank2", on_vector)
+        def hidden_of(e):
+            first_routed(e, raw["w1", e + 1, 1][:, 0 : H // 2].bitcast(BF16))
+            quantize_h(e)
+
+        for e in range(3, E):
+            prepare(e, 0, on_scalar)
+            load_w1(e, 1)
+            group_w1(e, 1, on_scalar, lambda: hidden_of(e - 1))
+            prepare_w2(e - 1, on_vector if e < E - 1 else on_vector)
+            quantize_w1(e, 1)
+            if e == GATE:
+                nc.sync.dma_start(out=gates[:], in_=gate[0:P, :])
+                scatter(*PIECES[1])
+            back(e - 1, on_vector if e < E - 1 else on_scalar)
+        prepare_w2(7, on_scalar)
+        first_routed(7, hidden_place(7))
+        quantize_h(7)
+        prepare_w2(SHARED, on_scalar)
+        back(7, on_scalar)
+        narrow = psum.tile([P, 512], F32, name="narrow", tag="narrow", bufs=1)
+        places = {}
         for b in range(2):
-            for piece in TAIL_PIECES:
-                scatter(b, *piece)
-            for start, width, tag in FINISH[b]:
-                finish(b, start, width, tag)
+            for start, width in FINISH:
+                if width == 512:
+                    wide = psum.tile([P, 512], F32, name="wide", tag=("bank3", "bank_shared")[b], bufs=2)
+                    places[b, start] = wide[:]
+                else:
+                    places[b, start] = narrow[:, b * width : (b + 1) * width]
+                second_shared(b, start, width, places[b, start])
+        for b in range(2):
+            for start, width in FINISH:
+                finish(b, start, width, places[b, start])

@@ -1,6 +1,7 @@
 from contextlib import ExitStack
 
 import concourse.mybir as mybir
+from concourse.masks import make_identity
 
 FLOPS = 3019898880
 
@@ -23,9 +24,11 @@ PACK = 4
 PASS = P * PACK
 PASSES = K // PASS
 HALF = 512
-RAW_BUFS = 12
+RAW_BUFS = 10
 PIECES = {1: (0, 224), 2: (224, 384), 4: (384, 544), 5: (544, 704), 6: (704, 864), 7: (864, 1024)}
-GATE = 3
+MERGED = ()
+X_SHARE = {(0, 0): 208, (0, 1): 144}
+X_PARTS = (1, 2)
 X_CUTS = ((0, 1024), (1024, 256))
 FINISH = ((0, 512), (512, 512), (1024, 256))
 
@@ -51,6 +54,23 @@ def tile_moe_shr_mlp_silu_kernel(tc, xT, w1, w2, gate, offs, out):
             nc.vector.memset(window[:], 0.0)
             routed.append(window)
 
+        gates = held.tile([P, S], F32, name="gates", align_bytes=64)
+        gate_rows = held.tile([P, E], F32, name="gate_rows")
+        identity = held.tile([P, P], F32, name="identity")
+        make_identity(nc, identity[:])
+
+        def spread_gates():
+            nc.sync.dma_start(out=gate_rows[:], in_=gate[0].rearrange("(n j) -> n j", j=E))
+            for half in range(2):
+                bank = psum.tile([P, 512], F32, name="gate_bank", tag="bank3", bufs=2)
+                for j in range(4):
+                    column = gate_rows[:, 4 * half + j : 4 * half + j + 1].to_broadcast([P, P])
+                    nc.tensor.transpose(bank[:, j * P : (j + 1) * P], column, identity[:])
+                nc.scalar.copy(
+                    out=gates[:].rearrange("p (n h j) -> p h n j", h=2, j=4)[:, half],
+                    in_=bank[:].rearrange("p (j n) -> p n j", j=4),
+                )
+
         x_codes = held.tile([P, PASSES * T], U32, name="x_codes", align_bytes=64)
         x_scales = held.tile([P, PASSES * T], U8, name="x_scales", align_bytes=64)
         pairs = [held.tile([P, 4 * T], BF16, name=f"pairs{c}", tag=f"pairs{c}", align_bytes=64) for c in range(PASSES)]
@@ -58,16 +78,22 @@ def tile_moe_shr_mlp_silu_kernel(tc, xT, w1, w2, gate, offs, out):
         g_scales = held.tile([P, PASSES * S], U8, name="g_scales", align_bytes=64)
         hs_scales = held.tile([P, T], U8, name="hs_scales", align_bytes=64)
 
+        last_hidden = held.tile([P, PACK * N], BF16, name="last_hidden", align_bytes=64)
         raw = {}
 
         def raw_tile():
             return ring.tile([P, PACK * H], F32, name="raw", tag="raw", bufs=RAW_BUFS, align_bytes=64)
 
-        def load_x(c, u, h):
-            tile = raw_tile()
-            rows = xT[c * PASS : (c + 1) * PASS, h * (T // 2) : (h + 1) * (T // 2)].rearrange("(p u e) w -> u p e w", u=2, e=2)
-            nc.sync.dma_start(out=tile[:, 0:T].rearrange("p (e w) -> p e w", e=2), in_=rows[u])
-            raw["x", c, u, h] = tile
+        def stage_tile():
+            return ring.tile([P, PACK * T], BF16, name="stage", tag="stage", bufs=4, align_bytes=64)
+
+        def load_x(c, u):
+            tile = stage_tile()
+            rows = xT[c * PASS : (c + 1) * PASS, :].rearrange("(p u e) (h w) -> u h p e w", u=2, e=2, h=X_PARTS[c])
+            place = tile[:].bitcast(F32).rearrange("p (h e w) -> p h e w", e=2, h=X_PARTS[c])
+            for h in range(X_PARTS[c]):
+                nc.sync.dma_start(out=place[:, h], in_=rows[u, h])
+            raw["x", c, u] = place
 
         def load_w1(e, c):
             tile = raw_tile()
@@ -87,12 +113,15 @@ def tile_moe_shr_mlp_silu_kernel(tc, xT, w1, w2, gate, offs, out):
 
         grouped = {}
 
-        def pair_x(c, u, h, copy):
-            first = u * 2 * T + h * T
-            copy(
-                out=pairs[c][:, first : first + T].rearrange("p (c i e) -> p c e i", i=4, e=2),
-                in_=raw["x", c, u, h][:, 0:T].rearrange("p (e c i) -> p c e i", i=4, e=2),
-            )
+        def pair_x(c, u, share):
+            width = T // X_PARTS[c]
+            for h in range(X_PARTS[c]):
+                first = u * 2 * T + h * 2 * width
+                dst = pairs[c][:, first : first + 2 * width].rearrange("p (c i e) -> p c e i", i=4, e=2)
+                src = raw["x", c, u][:, h].rearrange("p e (c i) -> p c e i", i=4)
+                if share > 0:
+                    nc.vector.tensor_copy(out=dst[:, 0:share], in_=src[:, 0:share])
+                nc.scalar.copy(out=dst[:, share : width // 4], in_=src[:, share : width // 4])
 
         def group_x(c):
             tile = ring.tile([P, PACK * T], BF16, name="grouped_x", tag="grouped_x", bufs=1, align_bytes=64)
@@ -130,8 +159,10 @@ def tile_moe_shr_mlp_silu_kernel(tc, xT, w1, w2, gate, offs, out):
             nc.vector.quantize_mx(out=g_codes[:, cols].bitcast(FP8X4), scales=g_scales[:, cols], in_=grouped["g", c][:])
 
         def group_w1(e, c, copy, between=None):
-            tile = ring.tile([P, PACK * H], BF16, name="grouped_w1", tag="grouped_w1", bufs=6, align_bytes=64)
-            dst = tile[:].rearrange("p (t m j) -> p m j t", t=PACK, j=PACK)
+            if c == 0:
+                grouped["w1", e] = stage_tile()
+            tile = grouped["w1", e][:, c * PACK * H : (c + 1) * PACK * H]
+            dst = tile.rearrange("p (t m j) -> p m j t", t=PACK, j=PACK)
             src = raw["w1", e, c][:].rearrange("p (j m t) -> p m j t", t=PACK, j=PACK)
             if copy is None:
                 nc.vector.tensor_copy(out=dst[:, :, :, 0:2], in_=src[:, :, :, 0:2])
@@ -146,7 +177,10 @@ def tile_moe_shr_mlp_silu_kernel(tc, xT, w1, w2, gate, offs, out):
             grouped["w1", e, c] = tile
 
         def group_w2(e, copy):
-            tile = ring.tile([P, PACK * N], BF16, name="grouped_w2", tag="grouped_w2", bufs=2, align_bytes=64)
+            if e == SHARED:
+                tile = last_hidden
+            else:
+                tile = ring.tile([P, PACK * N], BF16, name="grouped_w2", tag="grouped_w2", bufs=2, align_bytes=64)
             copy(
                 out=tile[:].rearrange("p (c i t) -> p c t i", i=4, t=PACK),
                 in_=raw["w2", e][:, 0 : PACK * N].rearrange("p (t c i) -> p c t i", i=4, t=PACK),
@@ -158,13 +192,17 @@ def tile_moe_shr_mlp_silu_kernel(tc, xT, w1, w2, gate, offs, out):
         def quantize_w1(e, c):
             if c == 0:
                 tag = "shared" if e == SHARED else "w1"
-                bufs = 1 if e == SHARED else 2
-                codes = ring.tile([P, PASSES * H], U32, name="w1_codes", tag=tag + "_codes", bufs=bufs, align_bytes=64)
+                bufs = 1 if e == SHARED else 3
+                codes = ring.tile([P, PASSES * H], U32, name="w1_codes", tag="grouped_x" if e == SHARED else "w1_codes", bufs=bufs, align_bytes=64)
                 scales = ring.tile([P, PASSES * H], U8, name="w1_scales", tag=tag + "_scales", bufs=bufs, align_bytes=64)
                 weights["w1", e] = (codes, scales)
             codes, scales = weights["w1", e]
-            cols = slice(c * H, (c + 1) * H)
-            nc.vector.quantize_mx(out=codes[:, cols].bitcast(FP8X4), scales=scales[:, cols], in_=grouped["w1", e, c][:])
+            if e in MERGED:
+                if c == 1:
+                    nc.vector.quantize_mx(out=codes[:].bitcast(FP8X4), scales=scales[:], in_=grouped["w1", e][:, 0 : PASSES * PACK * H])
+            else:
+                cols = slice(c * H, (c + 1) * H)
+                nc.vector.quantize_mx(out=codes[:, cols].bitcast(FP8X4), scales=scales[:, cols], in_=grouped["w1", e, c])
 
         def quantize_w2(e):
             codes = ring.tile([P, N], U32, name="w2_codes", tag="w2_codes", bufs=4, align_bytes=64)
@@ -218,13 +256,9 @@ def tile_moe_shr_mlp_silu_kernel(tc, xT, w1, w2, gate, offs, out):
             nc.vector.quantize_mx(out=codes.bitcast(FP8X4), scales=scales, in_=hidden[e])
             hidden_codes[e] = (codes, scales)
 
-        def first_shared(n, place):
-            multiply1(("s", n), SHARED, x_codes, x_scales, T, n * C, "bank_shared")
+        def first_shared(n, place, tag):
+            multiply1(("s", n), SHARED, x_codes, x_scales, T, n * C, tag)
             silu(place, ("s", n))
-
-        def quantize_hs(q, place):
-            cols = slice(q * 2 * C, (q + 1) * 2 * C)
-            nc.vector.quantize_mx(out=hs_codes[:, cols].bitcast(FP8X4), scales=hs_scales[:, cols], in_=place)
 
         def second_routed(e, tag, copy):
             h_codes, h_scales = hidden_codes[e]
@@ -276,16 +310,14 @@ def tile_moe_shr_mlp_silu_kernel(tc, xT, w1, w2, gate, offs, out):
             nc.vector.tensor_tensor(tile[:, 0:width], bank, routed[b][:, cols], ADD)
             nc.sync.dma_start(out=out[rows, cols], in_=tile[:, 0:width])
 
-        load_x(0, 0, 0)
-        load_x(0, 0, 1)
+        spread_gates()
+        load_x(0, 0)
         nc.sync.dma_start(offsets[:], offs)
         for c, u in ((0, 1), (1, 0), (1, 1)):
-            load_x(c, u, 0)
-            load_x(c, u, 1)
+            load_x(c, u)
         for c in range(PASSES):
             for u in range(2):
-                for h in range(2):
-                    pair_x(c, u, h, nc.vector.tensor_copy if (c, u) == (0, 0) else nc.scalar.copy)
+                pair_x(c, u, X_SHARE.get((c, u), 0))
                 gather(c, u)
             group_g(c)
             group_x(c)
@@ -293,7 +325,6 @@ def tile_moe_shr_mlp_silu_kernel(tc, xT, w1, w2, gate, offs, out):
             quantize_x(c)
         y = held.tile([P, 2 * S], F32, name="y", tag="pairs0", align_bytes=64)
         hs_codes = held.tile([P, T], U32, name="hs_codes", tag="pairs1", align_bytes=64)
-        gates = ring.tile([P, S], F32, name="gates", tag="gathered", bufs=1, align_bytes=64)
 
         def prepare(e, c, copy, between=None):
             load_w1(e, c)
@@ -310,57 +341,49 @@ def tile_moe_shr_mlp_silu_kernel(tc, xT, w1, w2, gate, offs, out):
             if e in PIECES:
                 scatter(*PIECES[e])
 
-        def shared_pair(q):
-            if q == 0:
-                place = raw["w1", 1, 1][:, 3 * H : 4 * H].bitcast(BF16)
+        def shared_run(first, count):
+            if first == 0:
+                place = raw["w1", 2, 0][:, 2 * H : 4 * H].bitcast(BF16)
             else:
-                own = ring.tile([P, 2 * PACK * C], BF16, name="hidden_shared", tag="hidden_shared", bufs=2, align_bytes=64)
-                place = own[:]
-            for part in range(2):
-                first_shared(2 * q + part, place[:, part * H : (part + 1) * H])
-            quantize_hs(q, place)
-
-        def hidden_place(e):
-            tile = ring.tile([P, PACK * C], BF16, name="hidden", tag="hidden", bufs=2, align_bytes=64)
-            return tile[:]
+                own = ring.tile([P, 4 * PACK * C], BF16, name="hidden_shared", tag=("gathered", "grouped_g")[first // 8], bufs=1, align_bytes=64)
+                place = own[:, 0 : count * PACK * C]
+            for part in range(count):
+                first_shared(first + part, place[:, part * H : (part + 1) * H], ("bank_shared", "bank3")[part // 2])
+            cols = slice(first * C, (first + count) * C)
+            nc.vector.quantize_mx(out=hs_codes[:, cols].bitcast(FP8X4), scales=hs_scales[:, cols], in_=place)
 
         on_vector, on_scalar = nc.vector.tensor_copy, nc.scalar.copy
         for e in (SHARED, 0, 1):
             prepare(e, 0, on_scalar)
             prepare(e, 1, on_scalar)
-        shared_pair(0)
-        first_routed(0, freed(1, 1, 0))
+        prepare(2, 0, on_scalar)
+        shared_run(0, 4)
+        first_routed(0, freed(2, 0, 0))
         quantize_h(0)
-        prepare(2, 0, on_vector)
-        shared_pair(1)
-        first_routed(1, freed(1, 1, 1))
-        quantize_h(1)
-        shared_pair(2)
         prepare(2, 1, on_vector)
-        shared_pair(3)
-        shared_pair(4)
+        first_routed(1, freed(2, 0, 1))
+        quantize_h(1)
+        shared_run(4, 4)
+        shared_run(8, 2)
         prepare_w2(0, on_vector)
         back(0, on_vector)
         prepare_w2(1, on_vector)
-        second_routed(1, "bank2", on_vector)
+        back(1, on_vector)
         def hidden_of(e):
             first_routed(e, raw["w1", e + 1, 1][:, 0 : H // 2].bitcast(BF16))
             quantize_h(e)
 
         for e in range(3, E):
-            prepare(e, 0, on_scalar)
+            prepare(e, 0, None if e == 5 else on_scalar)
             load_w1(e, 1)
             group_w1(e, 1, on_scalar, lambda: hidden_of(e - 1))
             prepare_w2(e - 1, on_vector if e < E - 1 else on_vector)
             quantize_w1(e, 1)
-            if e == GATE:
-                nc.sync.dma_start(out=gates[:], in_=gate[0:P, :])
-                scatter(*PIECES[1])
             back(e - 1, on_vector if e < E - 1 else on_scalar)
         prepare_w2(7, on_scalar)
-        first_routed(7, hidden_place(7))
+        first_routed(7, last_hidden[:, 0 : PACK * C])
         quantize_h(7)
-        prepare_w2(SHARED, on_scalar)
+        prepare_w2(SHARED, on_vector)
         back(7, on_scalar)
         narrow = psum.tile([P, 512], F32, name="narrow", tag="narrow", bufs=1)
         places = {}

@@ -78,8 +78,9 @@ def tile_moe_shr_mlp_silu_kernel(tc, xT, w1, w2, gate, offs, out):
         g_scales = held.tile([P, PASSES * S], U8, name="g_scales", align_bytes=64)
         hs_scales = held.tile([P, T], U8, name="hs_scales", align_bytes=64)
 
-        last_hidden = held.tile([P, PACK * N], BF16, name="last_hidden", align_bytes=64)
+        last_hidden = held.tile([P, PACK * C], BF16, name="last_hidden", tag="last_hidden", align_bytes=64)
         raw = {}
+        on_vector, on_scalar = nc.vector.tensor_copy, nc.scalar.copy
 
         def raw_tile():
             return ring.tile([P, PACK * H], F32, name="raw", tag="raw", bufs=RAW_BUFS, align_bytes=64)
@@ -177,10 +178,7 @@ def tile_moe_shr_mlp_silu_kernel(tc, xT, w1, w2, gate, offs, out):
             grouped["w1", e, c] = tile
 
         def group_w2(e, copy):
-            if e == SHARED:
-                tile = last_hidden
-            else:
-                tile = ring.tile([P, PACK * N], BF16, name="grouped_w2", tag="grouped_w2", bufs=2, align_bytes=64)
+            tile = ring.tile([P, PACK * N], BF16, name="grouped_w2", tag="grouped_w2", bufs=2, align_bytes=64)
             copy(
                 out=tile[:].rearrange("p (c i t) -> p c t i", i=4, t=PACK),
                 in_=raw["w2", e][:, 0 : PACK * N].rearrange("p (t c i) -> p c t i", i=4, t=PACK),
@@ -205,7 +203,10 @@ def tile_moe_shr_mlp_silu_kernel(tc, xT, w1, w2, gate, offs, out):
                 nc.vector.quantize_mx(out=codes[:, cols].bitcast(FP8X4), scales=scales[:, cols], in_=grouped["w1", e, c])
 
         def quantize_w2(e):
-            codes = ring.tile([P, N], U32, name="w2_codes", tag="w2_codes", bufs=4, align_bytes=64)
+            if e == SHARED:
+                codes = held.tile([P, N], U32, name="w2_shared_codes", tag="last_hidden", align_bytes=64)
+            else:
+                codes = ring.tile([P, N], U32, name="w2_codes", tag="w2_codes", bufs=4, align_bytes=64)
             scales = ring.tile([P, N], U8, name="w2_scales", tag="w2_scales", bufs=4, align_bytes=64)
             nc.vector.quantize_mx(out=codes[:].bitcast(FP8X4), scales=scales[:], in_=grouped["w2", e][:])
             weights["w2", e] = (codes, scales)
@@ -275,10 +276,14 @@ def tile_moe_shr_mlp_silu_kernel(tc, xT, w1, w2, gate, offs, out):
                     start=True,
                     stop=True,
                 )
-            copy(
-                out=y[:].rearrange("p (b s) -> p b s", b=2)[:, :, e * C : (e + 1) * C],
-                in_=bank[:].rearrange("p (b n) -> p b n", b=2),
-            )
+            if copy is on_vector:
+                for b in range(2):
+                    copy(out=y[:, b * S + e * C : b * S + (e + 1) * C], in_=bank[:, b * C : (b + 1) * C])
+            else:
+                copy(
+                    out=y[:].rearrange("p (b s) -> p b s", b=2)[:, :, e * C : (e + 1) * C],
+                    in_=bank[:].rearrange("p (b n) -> p b n", b=2),
+                )
 
         def scatter(first, last):
             for b in range(2):
@@ -310,8 +315,8 @@ def tile_moe_shr_mlp_silu_kernel(tc, xT, w1, w2, gate, offs, out):
             nc.vector.tensor_tensor(tile[:, 0:width], bank, routed[b][:, cols], ADD)
             nc.sync.dma_start(out=out[rows, cols], in_=tile[:, 0:width])
 
-        spread_gates()
         load_x(0, 0)
+        spread_gates()
         nc.sync.dma_start(offsets[:], offs)
         for c, u in ((0, 1), (1, 0), (1, 1)):
             load_x(c, u)
@@ -352,7 +357,7 @@ def tile_moe_shr_mlp_silu_kernel(tc, xT, w1, w2, gate, offs, out):
             cols = slice(first * C, (first + count) * C)
             nc.vector.quantize_mx(out=hs_codes[:, cols].bitcast(FP8X4), scales=hs_scales[:, cols], in_=place)
 
-        on_vector, on_scalar = nc.vector.tensor_copy, nc.scalar.copy
+        FIRST = {5: None}
         for e in (SHARED, 0, 1):
             prepare(e, 0, on_scalar)
             prepare(e, 1, on_scalar)
@@ -374,7 +379,7 @@ def tile_moe_shr_mlp_silu_kernel(tc, xT, w1, w2, gate, offs, out):
             quantize_h(e)
 
         for e in range(3, E):
-            prepare(e, 0, None if e == 5 else on_scalar)
+            prepare(e, 0, FIRST.get(e, on_scalar))
             load_w1(e, 1)
             group_w1(e, 1, on_scalar, lambda: hidden_of(e - 1))
             prepare_w2(e - 1, on_vector if e < E - 1 else on_vector)
@@ -383,7 +388,7 @@ def tile_moe_shr_mlp_silu_kernel(tc, xT, w1, w2, gate, offs, out):
         prepare_w2(7, on_scalar)
         first_routed(7, last_hidden[:, 0 : PACK * C])
         quantize_h(7)
-        prepare_w2(SHARED, on_vector)
+        prepare_w2(SHARED, on_scalar)
         back(7, on_scalar)
         narrow = psum.tile([P, 512], F32, name="narrow", tag="narrow", bufs=1)
         places = {}

@@ -8,6 +8,7 @@ FLOPS = 3019898880
 K, T, E, C, H, N = 1024, 1280, 8, 128, 512, 256
 S = E * C
 SHARED = E
+LAST = E - 1
 
 F32 = mybir.dt.float32
 BF16 = mybir.dt.bfloat16
@@ -23,18 +24,20 @@ P = 128
 PACK = 4
 PASS = P * PACK
 PASSES = K // PASS
-HALF = 512
-RAW_BUFS = 10
+BANK = 512
+BLOCKS = N // P
+GATHER = 512
+LOAD_BUFS = 10
+VECTOR_TOKENS = {(0, 0): 208, (0, 1): 144, (1, 0): 64}
 PIECES = {1: (0, 224), 2: (224, 384), 4: (384, 544), 5: (544, 704), 6: (704, 864), 7: (864, 1024)}
-MERGED = ()
-X_SHARE = {(0, 0): 208, (0, 1): 144}
-X_PARTS = (1, 2)
+SHARED_CAST = 5
 X_CUTS = ((0, 1024), (1024, 256))
-FINISH = ((0, 512), (512, 512), (1024, 256))
+OUT_CUTS = ((0, 512), (512, 512), (1024, 256))
 
 
 def tile_moe_shr_mlp_silu_kernel(tc, xT, w1, w2, gate, offs, out):
     nc = tc.nc
+    on_vector, on_scalar = nc.vector.tensor_copy, nc.scalar.copy
     with ExitStack() as ctx:
         lists = ctx.enter_context(tc.tile_pool(name="lists", bufs=1))
         held = ctx.enter_context(tc.tile_pool(name="held", bufs=1))
@@ -49,22 +52,22 @@ def tile_moe_shr_mlp_silu_kernel(tc, xT, w1, w2, gate, offs, out):
         nc.scalar.activation(zero_out[:], zero[:], SILU)
 
         routed = []
-        for b in range(2):
+        for b in range(BLOCKS):
             window = held.tile([P, T], F32, name=f"routed{b}", align_bytes=64)
             nc.vector.memset(window[:], 0.0)
             routed.append(window)
 
         gates = held.tile([P, S], F32, name="gates", align_bytes=64)
-        gate_rows = held.tile([P, E], F32, name="gate_rows")
+        gate_columns = held.tile([P, E], F32, name="gate_columns")
         identity = held.tile([P, P], F32, name="identity")
         make_identity(nc, identity[:])
 
         def spread_gates():
-            nc.sync.dma_start(out=gate_rows[:], in_=gate[0].rearrange("(n j) -> n j", j=E))
+            nc.sync.dma_start(out=gate_columns[:], in_=gate[0].rearrange("(n j) -> n j", j=E))
             for half in range(2):
-                bank = psum.tile([P, 512], F32, name="gate_bank", tag="bank3", bufs=2)
+                bank = psum.tile([P, BANK], F32, name="gate_bank", tag="bank_spare", bufs=2)
                 for j in range(4):
-                    column = gate_rows[:, 4 * half + j : 4 * half + j + 1].to_broadcast([P, P])
+                    column = gate_columns[:, 4 * half + j : 4 * half + j + 1].to_broadcast([P, P])
                     nc.tensor.transpose(bank[:, j * P : (j + 1) * P], column, identity[:])
                 nc.scalar.copy(
                     out=gates[:].rearrange("p (n h j) -> p h n j", h=2, j=4)[:, half],
@@ -73,247 +76,56 @@ def tile_moe_shr_mlp_silu_kernel(tc, xT, w1, w2, gate, offs, out):
 
         x_codes = held.tile([P, PASSES * T], U32, name="x_codes", align_bytes=64)
         x_scales = held.tile([P, PASSES * T], U8, name="x_scales", align_bytes=64)
-        pairs = [held.tile([P, 4 * T], BF16, name=f"pairs{c}", tag=f"pairs{c}", align_bytes=64) for c in range(PASSES)]
-        g_codes = held.tile([P, PASSES * S], U32, name="g_codes", align_bytes=64)
-        g_scales = held.tile([P, PASSES * S], U8, name="g_scales", align_bytes=64)
+        pairs = [held.tile([P, PACK * T], BF16, name=f"pairs{c}", tag=f"pairs{c}", align_bytes=64) for c in range(PASSES)]
+        slot_codes = held.tile([P, PASSES * S], U32, name="slot_codes", align_bytes=64)
+        slot_scales = held.tile([P, PASSES * S], U8, name="slot_scales", align_bytes=64)
         hs_scales = held.tile([P, T], U8, name="hs_scales", align_bytes=64)
-
         last_hidden = held.tile([P, PACK * C], BF16, name="last_hidden", tag="last_hidden", align_bytes=64)
-        raw = {}
-        on_vector, on_scalar = nc.vector.tensor_copy, nc.scalar.copy
 
-        def raw_tile():
-            return ring.tile([P, PACK * H], F32, name="raw", tag="raw", bufs=RAW_BUFS, align_bytes=64)
+        loaded = {}
+        grouped = {}
+        weights = {}
+        hidden_codes = {}
+
+        def load_tile():
+            return ring.tile([P, PACK * H], F32, name="load", tag="load", bufs=LOAD_BUFS, align_bytes=64)
 
         def stage_tile():
             return ring.tile([P, PACK * T], BF16, name="stage", tag="stage", bufs=4, align_bytes=64)
 
         def load_x(c, u):
             tile = stage_tile()
-            rows = xT[c * PASS : (c + 1) * PASS, :].rearrange("(p u e) (h w) -> u h p e w", u=2, e=2, h=X_PARTS[c])
-            place = tile[:].bitcast(F32).rearrange("p (h e w) -> p h e w", e=2, h=X_PARTS[c])
-            for h in range(X_PARTS[c]):
-                nc.sync.dma_start(out=place[:, h], in_=rows[u, h])
-            raw["x", c, u] = place
+            rows = xT[c * PASS : (c + 1) * PASS, :].rearrange("(p u e) w -> u p e w", u=2, e=2)
+            place = tile[:].bitcast(F32).rearrange("p (e w) -> p e w", e=2)
+            nc.sync.dma_start(out=place, in_=rows[u])
+            loaded["x", c, u] = place
 
-        def load_w1(e, c):
-            tile = raw_tile()
-            nc.sync.dma_start(out=tile[:], in_=w1[e, c * PASS : (c + 1) * PASS, :].rearrange("(p j) w -> p (j w)", j=PACK))
-            raw["w1", e, c] = tile
+        def pair_x(c, u):
+            dst = pairs[c][:, u * 2 * T : (u + 1) * 2 * T].rearrange("p (g i e) -> p g e i", i=4, e=2)
+            src = loaded["x", c, u].rearrange("p e (g i) -> p g e i", i=4)
+            share = VECTOR_TOKENS.get((c, u), 0)
+            if share > 0:
+                on_vector(out=dst[:, 0:share], in_=src[:, 0:share])
+            on_scalar(out=dst[:, share : T // 4], in_=src[:, share : T // 4])
 
-        def load_w2(e):
-            tile = raw_tile()
-            nc.sync.dma_start(out=tile[:, 0 : PACK * N], in_=w2[e].rearrange("(p j) w -> p (j w)", j=PACK))
-            raw["w2", e] = tile
-
-        def interleave_words(dst, src):
-            nc.vector.tensor_copy(
-                out=dst.bitcast(F32).rearrange("p (c i u) -> p c u i", i=4, u=2),
-                in_=src.rearrange("p u (c i) -> p c u i", i=4),
-            )
-
-        grouped = {}
-
-        def pair_x(c, u, share):
-            width = T // X_PARTS[c]
-            for h in range(X_PARTS[c]):
-                first = u * 2 * T + h * 2 * width
-                dst = pairs[c][:, first : first + 2 * width].rearrange("p (c i e) -> p c e i", i=4, e=2)
-                src = raw["x", c, u][:, h].rearrange("p e (c i) -> p c e i", i=4)
-                if share > 0:
-                    nc.vector.tensor_copy(out=dst[:, 0:share], in_=src[:, 0:share])
-                nc.scalar.copy(out=dst[:, share : width // 4], in_=src[:, share : width // 4])
-
-        def group_x(c):
-            tile = ring.tile([P, PACK * T], BF16, name="grouped_x", tag="grouped_x", bufs=1, align_bytes=64)
-            interleave_words(tile[:], pairs[c][:].bitcast(F32).rearrange("p (u t) -> p u t", u=2))
-            grouped["x", c] = tile
-
-        def quantize_x(c):
-            for start, width in X_CUTS:
-                cols = slice(c * T + start, c * T + start + width)
-                nc.vector.quantize_mx(
-                    out=x_codes[:, cols].bitcast(FP8X4),
-                    scales=x_scales[:, cols],
-                    in_=grouped["x", c][:, PACK * start : PACK * (start + width)],
-                )
-
-        looked_up = {}
-
-        def gather(c, u):
-            if u == 0:
-                looked_up[c] = ring.tile([P, 2 * S], U32, name="gathered", tag="gathered", bufs=1, align_bytes=64)
+        def gather(c, u, gathered):
             window = pairs[c][:, u * 2 * T : (u + 1) * 2 * T].bitcast(U32)
-            for half in range(2):
-                nc.vector.tensor_copy(
-                    out=looked_up[c][:, u * S + half * HALF : u * S + (half + 1) * HALF],
-                    in_=window.indirect(offsets[:, half * (HALF // 16) : (half + 1) * (HALF // 16)]),
+            for first in range(0, S, GATHER):
+                on_vector(
+                    out=gathered[:, u * S + first : u * S + first + GATHER],
+                    in_=window.indirect(offsets[:, first // 16 : (first + GATHER) // 16]),
                 )
 
-        def group_g(c):
-            tile = ring.tile([P, PACK * S], BF16, name="grouped_g", tag="grouped_g", bufs=1, align_bytes=64)
-            interleave_words(tile[:], looked_up[c][:].bitcast(F32).rearrange("p (u t) -> p u t", u=2))
-            grouped["g", c] = tile
-
-        def quantize_g(c):
-            cols = slice(c * S, (c + 1) * S)
-            nc.vector.quantize_mx(out=g_codes[:, cols].bitcast(FP8X4), scales=g_scales[:, cols], in_=grouped["g", c][:])
-
-        def group_w1(e, c, copy, between=None):
-            if c == 0:
-                grouped["w1", e] = stage_tile()
-            tile = grouped["w1", e][:, c * PACK * H : (c + 1) * PACK * H]
-            dst = tile.rearrange("p (t m j) -> p m j t", t=PACK, j=PACK)
-            src = raw["w1", e, c][:].rearrange("p (j m t) -> p m j t", t=PACK, j=PACK)
-            if copy is None:
-                nc.vector.tensor_copy(out=dst[:, :, :, 0:2], in_=src[:, :, :, 0:2])
-                nc.scalar.copy(out=dst[:, :, :, 2:4], in_=src[:, :, :, 2:4])
-            elif between is not None:
-                copy(out=dst[:, 0 : P // 2], in_=src[:, 0 : P // 2])
-                copy(out=dst[:, P // 2 : 5 * P // 8], in_=src[:, P // 2 : 5 * P // 8])
-                between()
-                copy(out=dst[:, 5 * P // 8 : P], in_=src[:, 5 * P // 8 : P])
-            else:
-                copy(out=dst, in_=src)
-            grouped["w1", e, c] = tile
-
-        def group_w2(e, copy):
-            tile = ring.tile([P, PACK * N], BF16, name="grouped_w2", tag="grouped_w2", bufs=2, align_bytes=64)
-            copy(
-                out=tile[:].rearrange("p (c i t) -> p c t i", i=4, t=PACK),
-                in_=raw["w2", e][:, 0 : PACK * N].rearrange("p (t c i) -> p c t i", i=4, t=PACK),
+        def join_pairs(name, source, width):
+            tile = ring.tile([P, PACK * width], BF16, name=name, tag=name, bufs=1, align_bytes=64)
+            on_vector(
+                out=tile[:].bitcast(F32).rearrange("p (g i u) -> p g u i", i=4, u=2),
+                in_=source[:].bitcast(F32).rearrange("p (u g i) -> p g u i", i=4, u=2),
             )
-            grouped["w2", e] = tile
+            return tile
 
-        weights = {}
-
-        def quantize_w1(e, c):
-            if c == 0:
-                tag = "shared" if e == SHARED else "w1"
-                bufs = 1 if e == SHARED else 3
-                codes = ring.tile([P, PASSES * H], U32, name="w1_codes", tag="grouped_x" if e == SHARED else "w1_codes", bufs=bufs, align_bytes=64)
-                scales = ring.tile([P, PASSES * H], U8, name="w1_scales", tag=tag + "_scales", bufs=bufs, align_bytes=64)
-                weights["w1", e] = (codes, scales)
-            codes, scales = weights["w1", e]
-            if e in MERGED:
-                if c == 1:
-                    nc.vector.quantize_mx(out=codes[:].bitcast(FP8X4), scales=scales[:], in_=grouped["w1", e][:, 0 : PASSES * PACK * H])
-            else:
-                cols = slice(c * H, (c + 1) * H)
-                nc.vector.quantize_mx(out=codes[:, cols].bitcast(FP8X4), scales=scales[:, cols], in_=grouped["w1", e, c])
-
-        def quantize_w2(e):
-            if e == SHARED:
-                codes = held.tile([P, N], U32, name="w2_shared_codes", tag="last_hidden", align_bytes=64)
-            else:
-                codes = ring.tile([P, N], U32, name="w2_codes", tag="w2_codes", bufs=4, align_bytes=64)
-            scales = ring.tile([P, N], U8, name="w2_scales", tag="w2_scales", bufs=4, align_bytes=64)
-            nc.vector.quantize_mx(out=codes[:].bitcast(FP8X4), scales=scales[:], in_=grouped["w2", e][:])
-            weights["w2", e] = (codes, scales)
-
-        banks = {}
-        hidden = {}
-
-        def multiply1(key, e, codes, scales, width, start, tag):
-            w_codes, w_scales = weights["w1", e]
-            bank = psum.tile([P, PACK * C], F32, name="bank1", tag=tag, bufs=2)
-            for t in range(PACK):
-                for c in range(PASSES):
-                    rows = slice(c * H + t * P, c * H + (t + 1) * P)
-                    cols = slice(c * width + start, c * width + start + C)
-                    nc.tensor.matmul_mx(
-                        out=bank[:, t * C : (t + 1) * C],
-                        lhsT=w_codes[:, rows].bitcast(FP8X4),
-                        lhsT_scale=w_scales[:, rows],
-                        rhs=codes[:, cols].bitcast(FP8X4),
-                        rhs_scale=scales[:, cols],
-                        start=(c == 0),
-                        stop=(c == PASSES - 1),
-                    )
-            banks[key] = bank
-
-        def freed(e, c, j):
-            return raw["w1", e, c][:, j * H + H // 2 : (j + 1) * H].bitcast(BF16)
-
-        def silu(place, key):
-            nc.scalar.activation(
-                place.rearrange("p (n t) -> p n t", t=PACK), banks[key][:].rearrange("p (t n) -> p n t", t=PACK), SILU
-            )
-
-        hidden_codes = {}
-
-        def first_routed(e, place):
-            multiply1(e, e, g_codes, g_scales, S, e * C, "bank_routed")
-            silu(place, e)
-            hidden[e] = place
-
-        def quantize_h(e, behind=None):
-            if behind is None:
-                own_codes = ring.tile([P, C], U32, name="h_codes", tag="h_codes", bufs=3, align_bytes=64)
-                own_scales = ring.tile([P, C], U8, name="h_scales", tag="h_scales", bufs=3, align_bytes=64)
-                codes, scales = own_codes[:], own_scales[:]
-            else:
-                codes, scales = behind[:, 0:C].bitcast(U32), behind[:, C : C + C // 4].bitcast(U8)
-            nc.vector.quantize_mx(out=codes.bitcast(FP8X4), scales=scales, in_=hidden[e])
-            hidden_codes[e] = (codes, scales)
-
-        def first_shared(n, place, tag):
-            multiply1(("s", n), SHARED, x_codes, x_scales, T, n * C, tag)
-            silu(place, ("s", n))
-
-        def second_routed(e, tag, copy):
-            h_codes, h_scales = hidden_codes[e]
-            w_codes, w_scales = weights["w2", e]
-            bank = psum.tile([P, 2 * C], F32, name="bank2", tag=tag, bufs=1)
-            for b in range(2):
-                rows = slice(b * P, (b + 1) * P)
-                nc.tensor.matmul_mx(
-                    out=bank[:, b * C : (b + 1) * C],
-                    lhsT=w_codes[:, rows].bitcast(FP8X4),
-                    lhsT_scale=w_scales[:, rows],
-                    rhs=h_codes.bitcast(FP8X4),
-                    rhs_scale=h_scales,
-                    start=True,
-                    stop=True,
-                )
-            if copy is on_vector:
-                for b in range(2):
-                    copy(out=y[:, b * S + e * C : b * S + (e + 1) * C], in_=bank[:, b * C : (b + 1) * C])
-            else:
-                copy(
-                    out=y[:].rearrange("p (b s) -> p b s", b=2)[:, :, e * C : (e + 1) * C],
-                    in_=bank[:].rearrange("p (b n) -> p b n", b=2),
-                )
-
-        def scatter(first, last):
-            for b in range(2):
-                nc.vector.tensor_tensor(
-                    routed[b][:].indirect(offsets[:, first // 16 : last // 16]),
-                    y[:, b * S + first : b * S + last],
-                    gates[:, first:last],
-                    MULT,
-                )
-
-        def second_shared(b, start, width, bank):
-            w_codes, w_scales = weights["w2", SHARED]
-            rows = slice(b * P, (b + 1) * P)
-            cols = slice(start, start + width)
-            nc.tensor.matmul_mx(
-                out=bank,
-                lhsT=w_codes[:, rows].bitcast(FP8X4),
-                lhsT_scale=w_scales[:, rows],
-                rhs=hs_codes[:, cols].bitcast(FP8X4),
-                rhs_scale=hs_scales[:, cols],
-                start=True,
-                stop=True,
-            )
-
-        def finish(b, start, width, bank):
-            rows = slice(b * P, (b + 1) * P)
-            cols = slice(start, start + width)
-            tile = raw_tile()
-            nc.vector.tensor_tensor(tile[:, 0:width], bank, routed[b][:, cols], ADD)
-            nc.sync.dma_start(out=out[rows, cols], in_=tile[:, 0:width])
+        def quantize(codes, scales, values):
+            nc.vector.quantize_mx(out=codes.bitcast(FP8X4), scales=scales, in_=values)
 
         load_x(0, 0)
         spread_gates()
@@ -321,85 +133,189 @@ def tile_moe_shr_mlp_silu_kernel(tc, xT, w1, w2, gate, offs, out):
         for c, u in ((0, 1), (1, 0), (1, 1)):
             load_x(c, u)
         for c in range(PASSES):
-            for u in range(2):
-                pair_x(c, u, X_SHARE.get((c, u), 0))
-                gather(c, u)
-            group_g(c)
-            group_x(c)
-            quantize_g(c)
-            quantize_x(c)
-        y = held.tile([P, 2 * S], F32, name="y", tag="pairs0", align_bytes=64)
+            pair_x(c, 0)
+            gathered = ring.tile([P, 2 * S], U32, name="gathered", tag="gathered", bufs=1, align_bytes=64)
+            gather(c, 0, gathered)
+            pair_x(c, 1)
+            gather(c, 1, gathered)
+            slot_values = join_pairs("slot_values", gathered, S)
+            token_values = join_pairs("token_values", pairs[c], T)
+            quantize(slot_codes[:, c * S : (c + 1) * S], slot_scales[:, c * S : (c + 1) * S], slot_values[:])
+            for start, width in X_CUTS:
+                cols = slice(c * T + start, c * T + start + width)
+                quantize(x_codes[:, cols], x_scales[:, cols], token_values[:, PACK * start : PACK * (start + width)])
+
+        y = held.tile([P, BLOCKS * S], F32, name="y", tag="pairs0", align_bytes=64)
         hs_codes = held.tile([P, T], U32, name="hs_codes", tag="pairs1", align_bytes=64)
 
-        def prepare(e, c, copy, between=None):
-            load_w1(e, c)
-            group_w1(e, c, copy, between)
+        def load_w1(e, c):
+            tile = load_tile()
+            nc.sync.dma_start(out=tile[:], in_=w1[e, c * PASS : (c + 1) * PASS, :].rearrange("(p j) w -> p (j w)", j=PACK))
+            loaded["w1", e, c] = tile
+            if c == 0:
+                grouped["w1", e] = stage_tile()
+            values = grouped["w1", e][:, c * PACK * H : (c + 1) * PACK * H]
+            dst = values.rearrange("p (t m j) -> p m j t", t=PACK, j=PACK)
+            src = tile[:].rearrange("p (j m t) -> p m j t", t=PACK, j=PACK)
+            return dst, src
+
+        def quantize_w1(e, c):
+            if c == 0 and e == SHARED:
+                codes = ring.tile([P, PASSES * H], U32, name="shared_codes", tag="token_values", bufs=1, align_bytes=64)
+                scales = ring.tile([P, PASSES * H], U8, name="shared_scales", tag="shared_scales", bufs=1, align_bytes=64)
+                weights["w1", e] = (codes, scales)
+            elif c == 0:
+                codes = ring.tile([P, PASSES * H], U32, name="w1_codes", tag="w1_codes", bufs=3, align_bytes=64)
+                scales = ring.tile([P, PASSES * H], U8, name="w1_scales", tag="w1_scales", bufs=3, align_bytes=64)
+                weights["w1", e] = (codes, scales)
+            codes, scales = weights["w1", e]
+            cols = slice(c * H, (c + 1) * H)
+            quantize(codes[:, cols], scales[:, cols], grouped["w1", e][:, c * PACK * H : (c + 1) * PACK * H])
+
+        def prepare_w1(e, c, copy):
+            dst, src = load_w1(e, c)
+            copy(out=dst, in_=src)
             quantize_w1(e, c)
 
+        def on_both(out, in_):
+            on_vector(out=out[:, :, :, 0:2], in_=in_[:, :, :, 0:2])
+            on_scalar(out=out[:, :, :, 2:4], in_=in_[:, :, :, 2:4])
+
         def prepare_w2(e, copy):
-            load_w2(e)
-            group_w2(e, copy)
-            quantize_w2(e)
-
-        def back(e, copy):
-            second_routed(e, "bank2", copy)
-            if e in PIECES:
-                scatter(*PIECES[e])
-
-        def shared_run(first, count):
-            if first == 0:
-                place = raw["w1", 2, 0][:, 2 * H : 4 * H].bitcast(BF16)
+            tile = load_tile()
+            nc.sync.dma_start(out=tile[:, 0 : PACK * N], in_=w2[e].rearrange("(p j) w -> p (j w)", j=PACK))
+            values = ring.tile([P, PACK * N], BF16, name="w2_values", tag="w2_values", bufs=2, align_bytes=64)
+            copy(
+                out=values[:].rearrange("p (g i t) -> p g t i", i=4, t=PACK),
+                in_=tile[:, 0 : PACK * N].rearrange("p (t g i) -> p g t i", i=4, t=PACK),
+            )
+            if e == SHARED:
+                codes = held.tile([P, N], U32, name="w2_shared_codes", tag="last_hidden", align_bytes=64)
             else:
-                own = ring.tile([P, 4 * PACK * C], BF16, name="hidden_shared", tag=("gathered", "grouped_g")[first // 8], bufs=1, align_bytes=64)
-                place = own[:, 0 : count * PACK * C]
-            for part in range(count):
-                first_shared(first + part, place[:, part * H : (part + 1) * H], ("bank_shared", "bank3")[part // 2])
-            cols = slice(first * C, (first + count) * C)
-            nc.vector.quantize_mx(out=hs_codes[:, cols].bitcast(FP8X4), scales=hs_scales[:, cols], in_=place)
+                codes = ring.tile([P, N], U32, name="w2_codes", tag="w2_codes", bufs=4, align_bytes=64)
+            scales = ring.tile([P, N], U8, name="w2_scales", tag="w2_scales", bufs=4, align_bytes=64)
+            quantize(codes[:], scales[:], values[:])
+            weights["w2", e] = (codes, scales)
 
-        FIRST = {5: None}
+        def multiply(bank, w_codes, w_scales, codes, scales, start=True, stop=True):
+            nc.tensor.matmul_mx(
+                out=bank,
+                lhsT=w_codes.bitcast(FP8X4),
+                lhsT_scale=w_scales,
+                rhs=codes.bitcast(FP8X4),
+                rhs_scale=scales,
+                start=start,
+                stop=stop,
+            )
+
+        def first_layer(e, codes, scales, width, first, tag, place):
+            w_codes, w_scales = weights["w1", e]
+            bank = psum.tile([P, PACK * C], F32, name="bank_first", tag=tag, bufs=2)
+            for t in range(PACK):
+                for c in range(PASSES):
+                    rows = slice(c * H + t * P, c * H + (t + 1) * P)
+                    cols = slice(c * width + first, c * width + first + C)
+                    multiply(
+                        bank[:, t * C : (t + 1) * C],
+                        w_codes[:, rows],
+                        w_scales[:, rows],
+                        codes[:, cols],
+                        scales[:, cols],
+                        start=(c == 0),
+                        stop=(c == PASSES - 1),
+                    )
+            nc.scalar.activation(
+                place.rearrange("p (n t) -> p n t", t=PACK), bank[:].rearrange("p (t n) -> p n t", t=PACK), SILU
+            )
+
+        def hidden_routed(e, place):
+            first_layer(e, slot_codes, slot_scales, S, e * C, "bank_routed", place)
+            codes = ring.tile([P, C], U32, name="h_codes", tag="h_codes", bufs=3, align_bytes=64)
+            scales = ring.tile([P, C], U8, name="h_scales", tag="h_scales", bufs=3, align_bytes=64)
+            quantize(codes[:], scales[:], place)
+            hidden_codes[e] = (codes, scales)
+
+        def hidden_shared(first, count, place):
+            for part in range(count):
+                tag = ("bank_shared", "bank_spare")[part // 2]
+                first_layer(SHARED, x_codes, x_scales, T, (first + part) * C, tag, place[:, part * H : (part + 1) * H])
+            cols = slice(first * C, (first + count) * C)
+            quantize(hs_codes[:, cols], hs_scales[:, cols], place)
+
+        def way_back(e):
+            h_codes, h_scales = hidden_codes[e]
+            w_codes, w_scales = weights["w2", e]
+            bank = psum.tile([P, BLOCKS * C], F32, name="bank_second", tag="bank_second", bufs=1)
+            for b in range(BLOCKS):
+                rows = slice(b * P, (b + 1) * P)
+                multiply(bank[:, b * C : (b + 1) * C], w_codes[:, rows], w_scales[:, rows], h_codes[:], h_scales[:])
+            if e < LAST - 1:
+                for b in range(BLOCKS):
+                    on_vector(out=y[:, b * S + e * C : b * S + (e + 1) * C], in_=bank[:, b * C : (b + 1) * C])
+            else:
+                on_scalar(
+                    out=y[:].rearrange("p (b s) -> p b s", b=BLOCKS)[:, :, e * C : (e + 1) * C],
+                    in_=bank[:].rearrange("p (b n) -> p b n", b=BLOCKS),
+                )
+            if e in PIECES:
+                first, last = PIECES[e]
+                for b in range(BLOCKS):
+                    nc.vector.tensor_tensor(
+                        routed[b][:].indirect(offsets[:, first // 16 : last // 16]),
+                        y[:, b * S + first : b * S + last],
+                        gates[:, first:last],
+                        MULT,
+                    )
+
         for e in (SHARED, 0, 1):
-            prepare(e, 0, on_scalar)
-            prepare(e, 1, on_scalar)
-        prepare(2, 0, on_scalar)
-        shared_run(0, 4)
-        first_routed(0, freed(2, 0, 0))
-        quantize_h(0)
-        prepare(2, 1, on_vector)
-        first_routed(1, freed(2, 0, 1))
-        quantize_h(1)
-        shared_run(4, 4)
-        shared_run(8, 2)
-        prepare_w2(0, on_vector)
-        back(0, on_vector)
-        prepare_w2(1, on_vector)
-        back(1, on_vector)
-        def hidden_of(e):
-            first_routed(e, raw["w1", e + 1, 1][:, 0 : H // 2].bitcast(BF16))
-            quantize_h(e)
+            prepare_w1(e, 0, on_scalar)
+            prepare_w1(e, 1, on_scalar)
+        prepare_w1(2, 0, on_scalar)
+
+        cast = loaded["w1", 2, 0]
+        hidden_shared(0, 4, cast[:, 2 * H : 4 * H].bitcast(BF16))
+        hidden_routed(0, cast[:, H // 2 : H].bitcast(BF16))
+        prepare_w1(2, 1, on_vector)
+        hidden_routed(1, cast[:, H + H // 2 : 2 * H].bitcast(BF16))
+        for first, count, tag in ((4, 4, "gathered"), (8, 2, "slot_values")):
+            tile = ring.tile([P, 4 * PACK * C], BF16, name="hidden_shared", tag=tag, bufs=1, align_bytes=64)
+            hidden_shared(first, count, tile[:, 0 : count * PACK * C])
+        for e in range(2):
+            prepare_w2(e, on_vector)
+            way_back(e)
 
         for e in range(3, E):
-            prepare(e, 0, FIRST.get(e, on_scalar))
-            load_w1(e, 1)
-            group_w1(e, 1, on_scalar, lambda: hidden_of(e - 1))
-            prepare_w2(e - 1, on_vector if e < E - 1 else on_vector)
+            prepare_w1(e, 0, on_both if e == SHARED_CAST else on_scalar)
+            dst, src = load_w1(e, 1)
+            on_scalar(out=dst[:, 0 : P // 2], in_=src[:, 0 : P // 2])
+            on_scalar(out=dst[:, P // 2 : 5 * P // 8], in_=src[:, P // 2 : 5 * P // 8])
+            hidden_routed(e - 1, loaded["w1", e, 1][:, 0 : H // 2].bitcast(BF16))
+            on_scalar(out=dst[:, 5 * P // 8 : P], in_=src[:, 5 * P // 8 : P])
+            prepare_w2(e - 1, on_vector)
             quantize_w1(e, 1)
-            back(e - 1, on_vector if e < E - 1 else on_scalar)
-        prepare_w2(7, on_scalar)
-        first_routed(7, last_hidden[:, 0 : PACK * C])
-        quantize_h(7)
+            way_back(e - 1)
+
+        prepare_w2(LAST, on_scalar)
+        hidden_routed(LAST, last_hidden[:])
         prepare_w2(SHARED, on_scalar)
-        back(7, on_scalar)
-        narrow = psum.tile([P, 512], F32, name="narrow", tag="narrow", bufs=1)
-        places = {}
-        for b in range(2):
-            for start, width in FINISH:
-                if width == 512:
-                    wide = psum.tile([P, 512], F32, name="wide", tag=("bank3", "bank_shared")[b], bufs=2)
-                    places[b, start] = wide[:]
+        way_back(LAST)
+
+        w_codes, w_scales = weights["w2", SHARED]
+        narrow = psum.tile([P, BANK], F32, name="narrow", tag="narrow", bufs=1)
+        ys = {}
+        for b in range(BLOCKS):
+            rows = slice(b * P, (b + 1) * P)
+            for start, width in OUT_CUTS:
+                if width == BANK:
+                    wide = psum.tile([P, BANK], F32, name="wide", tag=("bank_spare", "bank_shared")[b], bufs=2)
+                    ys[b, start] = wide[:]
                 else:
-                    places[b, start] = narrow[:, b * width : (b + 1) * width]
-                second_shared(b, start, width, places[b, start])
-        for b in range(2):
-            for start, width in FINISH:
-                finish(b, start, width, places[b, start])
+                    ys[b, start] = narrow[:, b * width : (b + 1) * width]
+                cols = slice(start, start + width)
+                multiply(ys[b, start], w_codes[:, rows], w_scales[:, rows], hs_codes[:, cols], hs_scales[:, cols])
+        for b in range(BLOCKS):
+            for start, width in OUT_CUTS:
+                cols = slice(start, start + width)
+                tile = load_tile()
+                nc.vector.tensor_tensor(tile[:, 0:width], ys[b, start], routed[b][:, cols], ADD)
+                nc.sync.dma_start(out=out[b * P : (b + 1) * P, cols], in_=tile[:, 0:width])

@@ -26,9 +26,9 @@ PASS = P * PACK
 PASSES = K // PASS
 BANK = 512
 BLOCKS = N // P
-GATHER = 512
+WINDOW = 1408
 LOAD_BUFS = 10
-VECTOR_TOKENS = {(0, 0): 208, (0, 1): 144, (1, 0): 64}
+VECTOR_TOKENS = {(0, 1): 176, (1, 1): 64}
 PIECES = {1: (0, 224), 2: (224, 384), 4: (384, 544), 5: (544, 704), 6: (704, 864), 7: (864, 1024)}
 SHARED_CAST = 5
 X_CUTS = ((0, 1024), (1024, 256))
@@ -76,7 +76,9 @@ def tile_moe_shr_mlp_silu_kernel(tc, xT, w1, w2, gate, offs, out):
 
         x_codes = held.tile([P, PASSES * T], U32, name="x_codes", align_bytes=64)
         x_scales = held.tile([P, PASSES * T], U8, name="x_scales", align_bytes=64)
-        pairs = [held.tile([P, PACK * T], BF16, name=f"pairs{c}", tag=f"pairs{c}", align_bytes=64) for c in range(PASSES)]
+        pairs = [held.tile([P, PACK * WINDOW], BF16, name=f"pairs{c}", tag=f"pairs{c}", align_bytes=64) for c in range(PASSES)]
+        for tile in pairs:
+            nc.vector.memset(tile[:].rearrange("p (u w) -> p u w", u=2)[:, :, 2 * T : 2 * WINDOW], 0.0)
         slot_codes = held.tile([P, PASSES * S], U32, name="slot_codes", align_bytes=64)
         slot_scales = held.tile([P, PASSES * S], U8, name="slot_scales", align_bytes=64)
         hs_scales = held.tile([P, T], U8, name="hs_scales", align_bytes=64)
@@ -96,12 +98,25 @@ def tile_moe_shr_mlp_silu_kernel(tc, xT, w1, w2, gate, offs, out):
         def load_x(c, u):
             tile = stage_tile()
             rows = xT[c * PASS : (c + 1) * PASS, :].rearrange("(p u e) w -> u p e w", u=2, e=2)
+            if (c, u) == (0, 0):
+                halves = tile[:].bitcast(F32).rearrange("p (h e w) -> p h e w", h=2, e=2)
+                for h in range(2):
+                    nc.sync.dma_start(out=halves[:, h], in_=rows[u][:, :, h * T // 2 : (h + 1) * T // 2])
+                loaded["x", c, u] = halves
+                return
             place = tile[:].bitcast(F32).rearrange("p (e w) -> p e w", e=2)
             nc.sync.dma_start(out=place, in_=rows[u])
             loaded["x", c, u] = place
 
         def pair_x(c, u):
-            dst = pairs[c][:, u * 2 * T : (u + 1) * 2 * T].rearrange("p (g i e) -> p g e i", i=4, e=2)
+            dst = pairs[c][:, u * 2 * WINDOW : u * 2 * WINDOW + 2 * T].rearrange("p (g i e) -> p g e i", i=4, e=2)
+            if (c, u) == (0, 0):
+                for h in range(2):
+                    src = loaded["x", c, u][:, h].rearrange("p e (g i) -> p g e i", i=4)
+                    part = dst[:, h * T // 8 : (h + 1) * T // 8]
+                    on_vector(out=part[:, 0:104], in_=src[:, 0:104])
+                    on_scalar(out=part[:, 104 : T // 8], in_=src[:, 104 : T // 8])
+                return
             src = loaded["x", c, u].rearrange("p e (g i) -> p g e i", i=4)
             share = VECTOR_TOKENS.get((c, u), 0)
             if share > 0:
@@ -109,18 +124,14 @@ def tile_moe_shr_mlp_silu_kernel(tc, xT, w1, w2, gate, offs, out):
             on_scalar(out=dst[:, share : T // 4], in_=src[:, share : T // 4])
 
         def gather(c, u, gathered):
-            window = pairs[c][:, u * 2 * T : (u + 1) * 2 * T].bitcast(U32)
-            for first in range(0, S, GATHER):
-                on_vector(
-                    out=gathered[:, u * S + first : u * S + first + GATHER],
-                    in_=window.indirect(offsets[:, first // 16 : (first + GATHER) // 16]),
-                )
+            window = pairs[c][:, u * 2 * WINDOW : (u + 1) * 2 * WINDOW].bitcast(U32)
+            on_vector(out=gathered[:, u * S : (u + 1) * S], in_=window.indirect(offsets[:]))
 
         def join_pairs(name, source, width):
             tile = ring.tile([P, PACK * width], BF16, name=name, tag=name, bufs=1, align_bytes=64)
             on_vector(
                 out=tile[:].bitcast(F32).rearrange("p (g i u) -> p g u i", i=4, u=2),
-                in_=source[:].bitcast(F32).rearrange("p (u g i) -> p g u i", i=4, u=2),
+                in_=source[:].bitcast(F32).rearrange("p (u w) -> p u w", u=2)[:, :, 0:width].rearrange("p u (g i) -> p g u i", i=4),
             )
             return tile
 
@@ -138,12 +149,12 @@ def tile_moe_shr_mlp_silu_kernel(tc, xT, w1, w2, gate, offs, out):
             gather(c, 0, gathered)
             pair_x(c, 1)
             gather(c, 1, gathered)
-            slot_values = join_pairs("slot_values", gathered, S)
             token_values = join_pairs("token_values", pairs[c], T)
-            quantize(slot_codes[:, c * S : (c + 1) * S], slot_scales[:, c * S : (c + 1) * S], slot_values[:])
+            slot_values = join_pairs("slot_values", gathered, S)
             for start, width in X_CUTS:
                 cols = slice(c * T + start, c * T + start + width)
                 quantize(x_codes[:, cols], x_scales[:, cols], token_values[:, PACK * start : PACK * (start + width)])
+            quantize(slot_codes[:, c * S : (c + 1) * S], slot_scales[:, c * S : (c + 1) * S], slot_values[:])
 
         y = held.tile([P, BLOCKS * S], F32, name="y", tag="pairs0", align_bytes=64)
         hs_codes = held.tile([P, T], U32, name="hs_codes", tag="pairs1", align_bytes=64)
@@ -155,8 +166,8 @@ def tile_moe_shr_mlp_silu_kernel(tc, xT, w1, w2, gate, offs, out):
             if c == 0:
                 grouped["w1", e] = stage_tile()
             values = grouped["w1", e][:, c * PACK * H : (c + 1) * PACK * H]
-            dst = values.rearrange("p (t m j) -> p m j t", t=PACK, j=PACK)
-            src = tile[:].rearrange("p (j m t) -> p m j t", t=PACK, j=PACK)
+            dst = values.rearrange("p (t m a b) -> p m a t b", t=PACK, a=2, b=2)
+            src = tile[:].rearrange("p (a b m t) -> p m a t b", t=PACK, a=2, b=2)
             return dst, src
 
         def quantize_w1(e, c):
@@ -184,6 +195,7 @@ def tile_moe_shr_mlp_silu_kernel(tc, xT, w1, w2, gate, offs, out):
         def prepare_w2(e, copy):
             tile = load_tile()
             nc.sync.dma_start(out=tile[:, 0 : PACK * N], in_=w2[e].rearrange("(p j) w -> p (j w)", j=PACK))
+            loaded["w2", e] = tile
             values = ring.tile([P, PACK * N], BF16, name="w2_values", tag="w2_values", bufs=2, align_bytes=64)
             copy(
                 out=values[:].rearrange("p (g i t) -> p g t i", i=4, t=PACK),
@@ -211,8 +223,8 @@ def tile_moe_shr_mlp_silu_kernel(tc, xT, w1, w2, gate, offs, out):
         def first_layer(e, codes, scales, width, first, tag, place):
             w_codes, w_scales = weights["w1", e]
             bank = psum.tile([P, PACK * C], F32, name="bank_first", tag=tag, bufs=2)
-            for t in range(PACK):
-                for c in range(PASSES):
+            for c in range(PASSES):
+                for t in range(PACK):
                     rows = slice(c * H + t * P, c * H + (t + 1) * P)
                     cols = slice(c * width + first, c * width + first + C)
                     multiply(
@@ -221,8 +233,8 @@ def tile_moe_shr_mlp_silu_kernel(tc, xT, w1, w2, gate, offs, out):
                         w_scales[:, rows],
                         codes[:, cols],
                         scales[:, cols],
-                        start=(c == 0),
-                        stop=(c == PASSES - 1),
+                        start=(c == 0 and t == 0),
+                        stop=(c == PASSES - 1 and t == PACK - 1),
                     )
             nc.scalar.activation(
                 place.rearrange("p (n t) -> p n t", t=PACK), bank[:].rearrange("p (t n) -> p n t", t=PACK), SILU
@@ -275,17 +287,14 @@ def tile_moe_shr_mlp_silu_kernel(tc, xT, w1, w2, gate, offs, out):
         cast = loaded["w1", 2, 0]
         hidden_shared(0, 4, cast[:, 2 * H : 4 * H].bitcast(BF16))
         hidden_routed(0, cast[:, H // 2 : H].bitcast(BF16))
-        prepare_w1(2, 1, on_vector)
         hidden_routed(1, cast[:, H + H // 2 : 2 * H].bitcast(BF16))
-        for first, count, tag in ((4, 4, "gathered"), (8, 2, "slot_values")):
-            tile = ring.tile([P, 4 * PACK * C], BF16, name="hidden_shared", tag=tag, bufs=1, align_bytes=64)
-            hidden_shared(first, count, tile[:, 0 : count * PACK * C])
+        prepare_w1(2, 1, on_both)
         for e in range(2):
             prepare_w2(e, on_vector)
             way_back(e)
 
         for e in range(3, E):
-            prepare_w1(e, 0, on_both if e == SHARED_CAST else on_scalar)
+            prepare_w1(e, 0, on_scalar)
             dst, src = load_w1(e, 1)
             on_scalar(out=dst[:, 0 : P // 2], in_=src[:, 0 : P // 2])
             on_scalar(out=dst[:, P // 2 : 5 * P // 8], in_=src[:, P // 2 : 5 * P // 8])
@@ -299,22 +308,24 @@ def tile_moe_shr_mlp_silu_kernel(tc, xT, w1, w2, gate, offs, out):
         hidden_routed(LAST, last_hidden[:])
         prepare_w2(SHARED, on_scalar)
         way_back(LAST)
+        hidden_shared(4, 4, loaded["w2", SHARED][:, 0 : 2 * H].bitcast(BF16))
+        hidden_shared(8, 2, loaded["w2", SHARED][:, 2 * H : 3 * H].bitcast(BF16))
 
         w_codes, w_scales = weights["w2", SHARED]
         narrow = psum.tile([P, BANK], F32, name="narrow", tag="narrow", bufs=1)
         ys = {}
-        for b in range(BLOCKS):
-            rows = slice(b * P, (b + 1) * P)
-            for start, width in OUT_CUTS:
+        for start, width in OUT_CUTS:
+            for b in range(BLOCKS):
+                rows = slice(b * P, (b + 1) * P)
                 if width == BANK:
-                    wide = psum.tile([P, BANK], F32, name="wide", tag=("bank_spare", "bank_shared")[b], bufs=2)
+                    wide = psum.tile([P, BANK], F32, name="wide", tag=("bank_routed" if start else "bank_spare"), bufs=2)
                     ys[b, start] = wide[:]
                 else:
                     ys[b, start] = narrow[:, b * width : (b + 1) * width]
                 cols = slice(start, start + width)
                 multiply(ys[b, start], w_codes[:, rows], w_scales[:, rows], hs_codes[:, cols], hs_scales[:, cols])
-        for b in range(BLOCKS):
-            for start, width in OUT_CUTS:
+        for start, width in OUT_CUTS:
+            for b in range(BLOCKS):
                 cols = slice(start, start + width)
                 tile = load_tile()
                 nc.vector.tensor_tensor(tile[:, 0:width], ys[b, start], routed[b][:, cols], ADD)

@@ -28,9 +28,9 @@ BANK = 512
 BLOCKS = N // P
 WINDOW = 1408
 LOAD_BUFS = 10
+FIRST_SHARE = 104
 VECTOR_TOKENS = {(0, 1): 176, (1, 1): 64}
 PIECES = {1: (0, 224), 2: (224, 384), 4: (384, 544), 5: (544, 704), 6: (704, 864), 7: (864, 1024)}
-SHARED_CAST = 5
 X_CUTS = ((0, 1024), (1024, 256))
 OUT_CUTS = ((0, 512), (512, 512), (1024, 256))
 
@@ -95,33 +95,26 @@ def tile_moe_shr_mlp_silu_kernel(tc, xT, w1, w2, gate, offs, out):
         def stage_tile():
             return ring.tile([P, PACK * T], BF16, name="stage", tag="stage", bufs=4, align_bytes=64)
 
-        def load_x(c, u):
+        def load_x(c, u, parts=1):
             tile = stage_tile()
-            rows = xT[c * PASS : (c + 1) * PASS, :].rearrange("(p u e) w -> u p e w", u=2, e=2)
-            if (c, u) == (0, 0):
-                halves = tile[:].bitcast(F32).rearrange("p (h e w) -> p h e w", h=2, e=2)
-                for h in range(2):
-                    nc.sync.dma_start(out=halves[:, h], in_=rows[u][:, :, h * T // 2 : (h + 1) * T // 2])
-                loaded["x", c, u] = halves
-                return
-            place = tile[:].bitcast(F32).rearrange("p (e w) -> p e w", e=2)
-            nc.sync.dma_start(out=place, in_=rows[u])
-            loaded["x", c, u] = place
+            rows = xT[c * PASS : (c + 1) * PASS, :].rearrange("(p u e) w -> u p e w", u=2, e=2)[u]
+            places = tile[:].bitcast(F32).rearrange("p (h e w) -> p h e w", h=parts, e=2)
+            width = T // parts
+            for h in range(parts):
+                nc.sync.dma_start(out=places[:, h], in_=rows[:, :, h * width : (h + 1) * width])
+            loaded["x", c, u] = [places[:, h] for h in range(parts)]
 
         def pair_x(c, u):
-            dst = pairs[c][:, u * 2 * WINDOW : u * 2 * WINDOW + 2 * T].rearrange("p (g i e) -> p g e i", i=4, e=2)
-            if (c, u) == (0, 0):
-                for h in range(2):
-                    src = loaded["x", c, u][:, h].rearrange("p e (g i) -> p g e i", i=4)
-                    part = dst[:, h * T // 8 : (h + 1) * T // 8]
-                    on_vector(out=part[:, 0:104], in_=src[:, 0:104])
-                    on_scalar(out=part[:, 104 : T // 8], in_=src[:, 104 : T // 8])
-                return
-            src = loaded["x", c, u].rearrange("p e (g i) -> p g e i", i=4)
-            share = VECTOR_TOKENS.get((c, u), 0)
-            if share > 0:
-                on_vector(out=dst[:, 0:share], in_=src[:, 0:share])
-            on_scalar(out=dst[:, share : T // 4], in_=src[:, share : T // 4])
+            tokens = pairs[c][:, u * 2 * WINDOW : u * 2 * WINDOW + 2 * T].rearrange("p (g i e) -> p g e i", i=4, e=2)
+            parts = loaded["x", c, u]
+            groups = T // 4 // len(parts)
+            share = FIRST_SHARE if len(parts) > 1 else VECTOR_TOKENS.get((c, u), 0)
+            for h, place in enumerate(parts):
+                dst = tokens[:, h * groups : (h + 1) * groups]
+                src = place.rearrange("p e (g i) -> p g e i", i=4)
+                if share > 0:
+                    on_vector(out=dst[:, 0:share], in_=src[:, 0:share])
+                on_scalar(out=dst[:, share:groups], in_=src[:, share:groups])
 
         def gather(c, u, gathered):
             window = pairs[c][:, u * 2 * WINDOW : (u + 1) * 2 * WINDOW].bitcast(U32)
@@ -129,16 +122,17 @@ def tile_moe_shr_mlp_silu_kernel(tc, xT, w1, w2, gate, offs, out):
 
         def join_pairs(name, source, width):
             tile = ring.tile([P, PACK * width], BF16, name=name, tag=name, bufs=1, align_bytes=64)
+            words = source[:].bitcast(F32).rearrange("p (u w) -> p u w", u=2)[:, :, 0:width]
             on_vector(
                 out=tile[:].bitcast(F32).rearrange("p (g i u) -> p g u i", i=4, u=2),
-                in_=source[:].bitcast(F32).rearrange("p (u w) -> p u w", u=2)[:, :, 0:width].rearrange("p u (g i) -> p g u i", i=4),
+                in_=words.rearrange("p u (g i) -> p g u i", i=4),
             )
             return tile
 
         def quantize(codes, scales, values):
             nc.vector.quantize_mx(out=codes.bitcast(FP8X4), scales=scales, in_=values)
 
-        load_x(0, 0)
+        load_x(0, 0, parts=2)
         spread_gates()
         nc.sync.dma_start(offsets[:], offs)
         for c, u in ((0, 1), (1, 0), (1, 1)):
@@ -257,7 +251,7 @@ def tile_moe_shr_mlp_silu_kernel(tc, xT, w1, w2, gate, offs, out):
         def way_back(e):
             h_codes, h_scales = hidden_codes[e]
             w_codes, w_scales = weights["w2", e]
-            bank = psum.tile([P, BLOCKS * C], F32, name="bank_second", tag="bank_second", bufs=1)
+            bank = psum.tile([P, BLOCKS * C], F32, name="bank_second", tag="bank_second", bufs=2)
             for b in range(BLOCKS):
                 rows = slice(b * P, (b + 1) * P)
                 multiply(bank[:, b * C : (b + 1) * C], w_codes[:, rows], w_scales[:, rows], h_codes[:], h_scales[:])
@@ -293,7 +287,7 @@ def tile_moe_shr_mlp_silu_kernel(tc, xT, w1, w2, gate, offs, out):
             prepare_w2(e, on_vector)
             way_back(e)
 
-        for e in range(3, E):
+        for e in range(3, LAST):
             prepare_w1(e, 0, on_scalar)
             dst, src = load_w1(e, 1)
             on_scalar(out=dst[:, 0 : P // 2], in_=src[:, 0 : P // 2])
@@ -304,15 +298,25 @@ def tile_moe_shr_mlp_silu_kernel(tc, xT, w1, w2, gate, offs, out):
             quantize_w1(e, 1)
             way_back(e - 1)
 
+        prepare_w1(LAST, 0, on_scalar)
+        dst, src = load_w1(LAST, 1)
+        on_scalar(out=dst[:, 0 : P // 2], in_=src[:, 0 : P // 2])
+        on_scalar(out=dst[:, P // 2 : 5 * P // 8], in_=src[:, P // 2 : 5 * P // 8])
+        on_vector(out=dst[:, 5 * P // 8 : P], in_=src[:, 5 * P // 8 : P])
+        quantize_w1(LAST, 1)
+        hidden_routed(LAST - 1, loaded["w1", LAST, 1][:, 0 : H // 2].bitcast(BF16))
         prepare_w2(LAST, on_scalar)
+        prepare_w2(LAST - 1, on_vector)
         hidden_routed(LAST, last_hidden[:])
+        way_back(LAST - 1)
         prepare_w2(SHARED, on_scalar)
         way_back(LAST)
+
         hidden_shared(4, 4, loaded["w2", SHARED][:, 0 : 2 * H].bitcast(BF16))
         hidden_shared(8, 2, loaded["w2", SHARED][:, 2 * H : 3 * H].bitcast(BF16))
 
         w_codes, w_scales = weights["w2", SHARED]
-        narrow = psum.tile([P, BANK], F32, name="narrow", tag="narrow", bufs=1)
+        narrow = psum.tile([P, BANK], F32, name="narrow", tag="bank_second", bufs=2)
         ys = {}
         for start, width in OUT_CUTS:
             for b in range(BLOCKS):

@@ -16,6 +16,7 @@ U32 = mybir.dt.uint32
 U16 = mybir.dt.uint16
 U8 = mybir.dt.uint8
 FP8X4 = mybir.dt.float8_e4m3fn_x4
+COPY = mybir.ActivationFunctionType.Copy
 SILU = mybir.ActivationFunctionType.Silu
 MULT = mybir.AluOpType.mult
 ADD = mybir.AluOpType.add
@@ -29,8 +30,12 @@ BLOCKS = N // P
 WINDOW = 1408
 LOAD_BUFS = 10
 FIRST_SHARE = 104
-VECTOR_TOKENS = {(0, 1): 176, (1, 1): 64}
+VECTOR_TOKENS = {(0, 1): 176}
 PIECES = {1: (0, 224), 2: (224, 384), 4: (384, 544), 5: (544, 704), 6: (704, 864), 7: (864, 1024)}
+AT_H, AT_W2, AT_W1, STEP_WORDS = 0, C, C + N, C + N + PASSES * H
+WOVEN = (2, 3, 4, 5, 6)
+EARLY = 6
+LATE = {4: (6, 1), 5: (7, 3)}
 X_CUTS = ((0, 1024), (1024, 256))
 OUT_CUTS = ((0, 512), (512, 512), (1024, 256))
 
@@ -51,21 +56,22 @@ def tile_moe_shr_mlp_silu_kernel(tc, xT, w1, w2, gate, offs, out):
         nc.vector.memset(zero[:], 0.0)
         nc.scalar.activation(zero_out[:], zero[:], SILU)
 
+        identity = held.tile([P, P], F32, name="identity")
+        make_identity(nc, identity[:])
+
         routed = []
         for b in range(BLOCKS):
             window = held.tile([P, T], F32, name=f"routed{b}", align_bytes=64)
-            nc.vector.memset(window[:], 0.0)
+            (nc.gpsimd if b else nc.vector).memset(window[:], 0.0)
             routed.append(window)
 
         gates = held.tile([P, S], F32, name="gates", align_bytes=64)
         gate_columns = held.tile([P, E], F32, name="gate_columns")
-        identity = held.tile([P, P], F32, name="identity")
-        make_identity(nc, identity[:])
 
         def spread_gates():
             nc.sync.dma_start(out=gate_columns[:], in_=gate[0].rearrange("(n j) -> n j", j=E))
             for half in range(2):
-                bank = psum.tile([P, BANK], F32, name="gate_bank", tag="bank_spare", bufs=2)
+                bank = psum.tile([P, BANK], F32, name="gate_bank", tag="bank_shared", bufs=4)
                 for j in range(4):
                     column = gate_columns[:, 4 * half + j : 4 * half + j + 1].to_broadcast([P, P])
                     nc.tensor.transpose(bank[:, j * P : (j + 1) * P], column, identity[:])
@@ -82,23 +88,20 @@ def tile_moe_shr_mlp_silu_kernel(tc, xT, w1, w2, gate, offs, out):
         slot_codes = held.tile([P, PASSES * S], U32, name="slot_codes", align_bytes=64)
         slot_scales = held.tile([P, PASSES * S], U8, name="slot_scales", align_bytes=64)
         hs_scales = held.tile([P, T], U8, name="hs_scales", align_bytes=64)
-        last_hidden = held.tile([P, PACK * C], BF16, name="last_hidden", tag="last_hidden", align_bytes=64)
 
         loaded = {}
-        grouped = {}
-        weights = {}
-        hidden_codes = {}
+        steps = {}
 
         def load_tile():
             return ring.tile([P, PACK * H], F32, name="load", tag="load", bufs=LOAD_BUFS, align_bytes=64)
 
         def stage_tile():
-            return ring.tile([P, PACK * T], BF16, name="stage", tag="stage", bufs=4, align_bytes=64)
+            return ring.tile([P, PACK * STEP_WORDS], BF16, name="stage", tag="stage", bufs=4, align_bytes=64)
 
         def load_x(c, u, parts=1):
             tile = stage_tile()
             rows = xT[c * PASS : (c + 1) * PASS, :].rearrange("(p u e) w -> u p e w", u=2, e=2)[u]
-            places = tile[:].bitcast(F32).rearrange("p (h e w) -> p h e w", h=parts, e=2)
+            places = tile[:, 0 : PACK * T].bitcast(F32).rearrange("p (h e w) -> p h e w", h=parts, e=2)
             width = T // parts
             for h in range(parts):
                 nc.sync.dma_start(out=places[:, h], in_=rows[:, :, h * width : (h + 1) * width])
@@ -120,13 +123,14 @@ def tile_moe_shr_mlp_silu_kernel(tc, xT, w1, w2, gate, offs, out):
             window = pairs[c][:, u * 2 * WINDOW : (u + 1) * 2 * WINDOW].bitcast(U32)
             on_vector(out=gathered[:, u * S : (u + 1) * S], in_=window.indirect(offsets[:]))
 
-        def join_pairs(name, source, width):
+        def join_pairs(name, source, width, helped=0):
             tile = ring.tile([P, PACK * width], BF16, name=name, tag=name, bufs=1, align_bytes=64)
             words = source[:].bitcast(F32).rearrange("p (u w) -> p u w", u=2)[:, :, 0:width]
-            on_vector(
-                out=tile[:].bitcast(F32).rearrange("p (g i u) -> p g u i", i=4, u=2),
-                in_=words.rearrange("p u (g i) -> p g u i", i=4),
-            )
+            dst = tile[:].bitcast(F32).rearrange("p (g i u) -> p g u i", i=4, u=2)
+            src = words.rearrange("p u (g i) -> p g u i", i=4)
+            on_vector(out=dst[:, helped:], in_=src[:, helped:])
+            if helped:
+                on_scalar(out=dst[:, 0:helped], in_=src[:, 0:helped])
             return tile
 
         def quantize(codes, scales, values):
@@ -143,7 +147,7 @@ def tile_moe_shr_mlp_silu_kernel(tc, xT, w1, w2, gate, offs, out):
             gather(c, 0, gathered)
             pair_x(c, 1)
             gather(c, 1, gathered)
-            token_values = join_pairs("token_values", pairs[c], T)
+            token_values = join_pairs("token_values", pairs[c], T, 160 if c == 0 else 0)
             slot_values = join_pairs("slot_values", gathered, S)
             for start, width in X_CUTS:
                 cols = slice(c * T + start, c * T + start + width)
@@ -153,55 +157,72 @@ def tile_moe_shr_mlp_silu_kernel(tc, xT, w1, w2, gate, offs, out):
         y = held.tile([P, BLOCKS * S], F32, name="y", tag="pairs0", align_bytes=64)
         hs_codes = held.tile([P, T], U32, name="hs_codes", tag="pairs1", align_bytes=64)
 
-        def load_w1(e, c):
+        def step(e):
+            if e not in steps:
+                values = stage_tile()
+                if e == "shared":
+                    codes = ring.tile([P, STEP_WORDS], U32, name="shared_codes", tag="token_values", bufs=1, align_bytes=64)
+                    scales = ring.tile([P, STEP_WORDS], U8, name="shared_scales", tag="shared_scales", bufs=1, align_bytes=64)
+                else:
+                    codes = ring.tile([P, STEP_WORDS], U32, name="step_codes", tag="step_codes", bufs=3, align_bytes=64)
+                    scales = ring.tile([P, STEP_WORDS], U8, name="step_scales", tag="step_scales", bufs=3, align_bytes=64)
+                steps[e] = (values, codes, scales)
+            return steps[e]
+
+        def w1_at(e):
+            return 2 * P if e in WOVEN else AT_W1
+
+        def hidden_at(e):
+            return (E, (e - LAST + 1) * 4 * P) if e >= LAST - 1 else (e + 1, AT_H)
+
+        def w2_at(e, b):
+            if e >= LAST - 1:
+                return (E, {LAST - 1: (1 + b) * P, LAST: (3 + 2 * b) * P, SHARED: (6 + b) * P}[e])
+            return (e + 1, STEP_WORDS - P if e + 1 in WOVEN and b == 1 else AT_W2 + b * P)
+
+        def hidden_values(e):
+            place, at = hidden_at(e)
+            return step(place)[0][:, PACK * at : PACK * (at + C)]
+
+        def quantize_words(e, first, last):
+            values, codes, scales = step(e)
+            quantize(codes[:, first:last], scales[:, first:last], values[:, PACK * first : PACK * last])
+
+        def cast_w1(e, c, engine):
             tile = load_tile()
-            nc.sync.dma_start(out=tile[:], in_=w1[e, c * PASS : (c + 1) * PASS, :].rearrange("(p j) w -> p (j w)", j=PACK))
+            source = w1[SHARED if e == "shared" else e, c * PASS : (c + 1) * PASS, :]
+            nc.sync.dma_start(out=tile[:], in_=source.rearrange("(p j) w -> p (j w)", j=PACK))
             loaded["w1", e, c] = tile
-            if c == 0:
-                grouped["w1", e] = stage_tile()
-            values = grouped["w1", e][:, c * PACK * H : (c + 1) * PACK * H]
-            dst = values.rearrange("p (t m a b) -> p m a t b", t=PACK, a=2, b=2)
+            values = step(e)[0][:, PACK * w1_at(e) : PACK * (w1_at(e) + PASSES * H)]
+            if e in WOVEN:
+                dst = values.rearrange("p (t c m a b) -> p c m a t b", t=PACK, c=PASSES, a=2, b=2)[:, 1 - c]
+            else:
+                dst = values.rearrange("p (c t m a b) -> p c m a t b", t=PACK, c=PASSES, a=2, b=2)[:, c]
             src = tile[:].rearrange("p (a b m t) -> p m a t b", t=PACK, a=2, b=2)
-            return dst, src
+            if engine == "scalar":
+                on_scalar(out=dst, in_=src)
+            elif engine == "vector":
+                on_vector(out=dst, in_=src)
+            elif engine == "both":
+                on_scalar(out=dst[:, :, :, 2:4], in_=src[:, :, :, 2:4])
+                on_vector(out=dst[:, :, :, 0:2], in_=src[:, :, :, 0:2])
+            else:
+                on_vector(out=dst[:, :, :, 0:2], in_=src[:, :, :, 0:2])
+                on_vector(out=dst[:, :, :, 2:4], in_=src[:, :, :, 2:4])
 
-        def quantize_w1(e, c):
-            if c == 0 and e == SHARED:
-                codes = ring.tile([P, PASSES * H], U32, name="shared_codes", tag="token_values", bufs=1, align_bytes=64)
-                scales = ring.tile([P, PASSES * H], U8, name="shared_scales", tag="shared_scales", bufs=1, align_bytes=64)
-                weights["w1", e] = (codes, scales)
-            elif c == 0:
-                codes = ring.tile([P, PASSES * H], U32, name="w1_codes", tag="w1_codes", bufs=3, align_bytes=64)
-                scales = ring.tile([P, PASSES * H], U8, name="w1_scales", tag="w1_scales", bufs=3, align_bytes=64)
-                weights["w1", e] = (codes, scales)
-            codes, scales = weights["w1", e]
-            cols = slice(c * H, (c + 1) * H)
-            quantize(codes[:, cols], scales[:, cols], grouped["w1", e][:, c * PACK * H : (c + 1) * PACK * H])
-
-        def prepare_w1(e, c, copy):
-            dst, src = load_w1(e, c)
-            copy(out=dst, in_=src)
-            quantize_w1(e, c)
-
-        def on_both(out, in_):
-            on_vector(out=out[:, :, :, 0:2], in_=in_[:, :, :, 0:2])
-            on_scalar(out=out[:, :, :, 2:4], in_=in_[:, :, :, 2:4])
-
-        def prepare_w2(e, copy):
+        def cast_w2(e, copy):
             tile = load_tile()
             nc.sync.dma_start(out=tile[:, 0 : PACK * N], in_=w2[e].rearrange("(p j) w -> p (j w)", j=PACK))
-            loaded["w2", e] = tile
-            values = ring.tile([P, PACK * N], BF16, name="w2_values", tag="w2_values", bufs=2, align_bytes=64)
-            copy(
-                out=values[:].rearrange("p (g i t) -> p g t i", i=4, t=PACK),
-                in_=tile[:, 0 : PACK * N].rearrange("p (t g i) -> p g t i", i=4, t=PACK),
-            )
-            if e == SHARED:
-                codes = held.tile([P, N], U32, name="w2_shared_codes", tag="last_hidden", align_bytes=64)
+            src = tile[:, 0 : PACK * N].rearrange("p (t g i) -> p g t i", i=4, t=PACK)
+            place, at = w2_at(e, 0)
+            if w2_at(e, 1)[1] == at + P:
+                values = step(place)[0][:, PACK * at : PACK * (at + N)]
+                copy(out=values.rearrange("p (g i t) -> p g t i", i=4, t=PACK), in_=src)
             else:
-                codes = ring.tile([P, N], U32, name="w2_codes", tag="w2_codes", bufs=4, align_bytes=64)
-            scales = ring.tile([P, N], U8, name="w2_scales", tag="w2_scales", bufs=4, align_bytes=64)
-            quantize(codes[:], scales[:], values[:])
-            weights["w2", e] = (codes, scales)
+                for b in range(BLOCKS):
+                    at = w2_at(e, b)[1]
+                    values = step(place)[0][:, PACK * at : PACK * (at + P)]
+                    copy(out=values.rearrange("p (g i t) -> p g t i", i=4, t=PACK), in_=src[:, b * P // 4 : (b + 1) * P // 4])
 
         def multiply(bank, w_codes, w_scales, codes, scales, start=True, stop=True):
             nc.tensor.matmul_mx(
@@ -214,122 +235,178 @@ def tile_moe_shr_mlp_silu_kernel(tc, xT, w1, w2, gate, offs, out):
                 stop=stop,
             )
 
-        def first_layer(e, codes, scales, width, first, tag, place):
-            w_codes, w_scales = weights["w1", e]
-            bank = psum.tile([P, PACK * C], F32, name="bank_first", tag=tag, bufs=2)
-            for c in range(PASSES):
-                for t in range(PACK):
-                    rows = slice(c * H + t * P, c * H + (t + 1) * P)
-                    cols = slice(c * width + first, c * width + first + C)
-                    multiply(
-                        bank[:, t * C : (t + 1) * C],
-                        w_codes[:, rows],
-                        w_scales[:, rows],
-                        codes[:, cols],
-                        scales[:, cols],
-                        start=(c == 0 and t == 0),
-                        stop=(c == PASSES - 1 and t == PACK - 1),
-                    )
+        def first_layer(e, order, bank, codes, scales, width, first):
+            w_codes, w_scales = step(e)[1:]
+            for c, t in order:
+                at = w1_at(e) + (2 * t + 1 - c) * P if e in WOVEN else AT_W1 + c * H + t * P
+                rows = slice(at, at + P)
+                cols = slice(c * width + first, c * width + first + C)
+                multiply(
+                    bank[:, t * C : (t + 1) * C],
+                    w_codes[:, rows],
+                    w_scales[:, rows],
+                    codes[:, cols],
+                    scales[:, cols],
+                    start=((c, t) == ((1, 0) if e in WOVEN else (0, 0))),
+                    stop=((c, t) == ((0, 3) if e in WOVEN else (1, 3))),
+                )
+
+        def first_pass(e, c, bank, codes, scales, width, first):
+            first_layer(e, [(c, t) for t in range(PACK)], bank, codes, scales, width, first)
+
+        def silu(place, bank):
             nc.scalar.activation(
                 place.rearrange("p (n t) -> p n t", t=PACK), bank[:].rearrange("p (t n) -> p n t", t=PACK), SILU
             )
 
-        def hidden_routed(e, place):
-            first_layer(e, slot_codes, slot_scales, S, e * C, "bank_routed", place)
-            codes = ring.tile([P, C], U32, name="h_codes", tag="h_codes", bufs=3, align_bytes=64)
-            scales = ring.tile([P, C], U8, name="h_scales", tag="h_scales", bufs=3, align_bytes=64)
-            quantize(codes[:], scales[:], place)
-            hidden_codes[e] = (codes, scales)
+        def routed_bank():
+            return psum.tile([P, PACK * C], F32, name="bank_first", tag="bank_routed", bufs=2)
 
-        def hidden_shared(first, count, place):
-            for part in range(count):
-                tag = ("bank_shared", "bank_spare")[part // 2]
-                first_layer(SHARED, x_codes, x_scales, T, (first + part) * C, tag, place[:, part * H : (part + 1) * H])
+        def silu_shared(group, place):
+            bank = psum.tile([P, PACK * C], F32, name="bank_shared", tag="bank_shared", bufs=4)
+            for c in range(PASSES):
+                first_pass("shared", c, bank, x_codes, x_scales, T, group * C)
+            silu(place, bank)
+
+        def quantize_shared(first, count, place):
             cols = slice(first * C, (first + count) * C)
             quantize(hs_codes[:, cols], hs_scales[:, cols], place)
 
-        def way_back(e):
-            h_codes, h_scales = hidden_codes[e]
-            w_codes, w_scales = weights["w2", e]
-            bank = psum.tile([P, BLOCKS * C], F32, name="bank_second", tag="bank_second", bufs=2)
-            for b in range(BLOCKS):
-                rows = slice(b * P, (b + 1) * P)
-                multiply(bank[:, b * C : (b + 1) * C], w_codes[:, rows], w_scales[:, rows], h_codes[:], h_scales[:])
-            if e < LAST - 1:
-                for b in range(BLOCKS):
-                    on_vector(out=y[:, b * S + e * C : b * S + (e + 1) * C], in_=bank[:, b * C : (b + 1) * C])
-            else:
-                on_scalar(
-                    out=y[:].rearrange("p (b s) -> p b s", b=BLOCKS)[:, :, e * C : (e + 1) * C],
-                    in_=bank[:].rearrange("p (b n) -> p b n", b=BLOCKS),
-                )
+        def second_bank():
+            return psum.tile([P, BLOCKS * C], F32, name="bank_second", tag="bank_second", bufs=2)
+
+        def second_layer(e, bank, blocks):
+            place, at = hidden_at(e)
+            codes, scales = step(place)[1:]
+            slots = slice(at, at + C)
+            for b in blocks:
+                rows = slice(w2_at(e, b)[1], w2_at(e, b)[1] + P)
+                multiply(bank[:, b * C : (b + 1) * C], codes[:, rows], scales[:, rows], codes[:, slots], scales[:, slots])
+
+        def scatter(e, b):
             if e in PIECES:
                 first, last = PIECES[e]
-                for b in range(BLOCKS):
-                    nc.vector.tensor_tensor(
-                        routed[b][:].indirect(offsets[:, first // 16 : last // 16]),
-                        y[:, b * S + first : b * S + last],
-                        gates[:, first:last],
-                        MULT,
-                    )
+                window = routed[b][:].indirect(offsets[:, first // 16 : last // 16])
+                if (e, b) == (LAST, 0):
+                    on_vector(out=window, in_=y[:, b * S + first : b * S + last])
+                else:
+                    nc.scalar.activation(window, y[:, b * S + first : b * S + last], COPY)
 
-        for e in (SHARED, 0, 1):
-            prepare_w1(e, 0, on_scalar)
-            prepare_w1(e, 1, on_scalar)
-        prepare_w1(2, 0, on_scalar)
+        def way_back(e, bank):
+            slots = slice(e * C, (e + 1) * C)
+            nc.vector.tensor_tensor(
+                y[:].rearrange("p (b s) -> p b s", b=BLOCKS)[:, :, slots],
+                bank[:].rearrange("p (b n) -> p b n", b=BLOCKS),
+                gates[:, slots].rearrange("p (o n) -> p o n", o=1).to_broadcast([P, BLOCKS, C]),
+                MULT,
+            )
+            for b in range(BLOCKS):
+                scatter(e, b)
 
-        cast = loaded["w1", 2, 0]
-        hidden_shared(0, 4, cast[:, 2 * H : 4 * H].bitcast(BF16))
-        hidden_routed(0, cast[:, H // 2 : H].bitcast(BF16))
-        hidden_routed(1, cast[:, H + H // 2 : 2 * H].bitcast(BF16))
-        prepare_w1(2, 1, on_both)
-        for e in range(2):
-            prepare_w2(e, on_vector)
-            way_back(e)
+        def way_back_block(e, bank, b):
+            slots = slice(e * C, (e + 1) * C)
+            nc.vector.tensor_tensor(
+                y[:, b * S + e * C : b * S + (e + 1) * C], bank[:, b * C : (b + 1) * C], gates[:, slots], MULT
+            )
+            scatter(e, b)
 
-        for e in range(3, LAST):
-            prepare_w1(e, 0, on_scalar)
-            dst, src = load_w1(e, 1)
-            on_scalar(out=dst[:, 0 : P // 2], in_=src[:, 0 : P // 2])
-            on_scalar(out=dst[:, P // 2 : 5 * P // 8], in_=src[:, P // 2 : 5 * P // 8])
-            hidden_routed(e - 1, loaded["w1", e, 1][:, 0 : H // 2].bitcast(BF16))
-            on_scalar(out=dst[:, 5 * P // 8 : P], in_=src[:, 5 * P // 8 : P])
-            prepare_w2(e - 1, on_vector)
-            quantize_w1(e, 1)
-            way_back(e - 1)
+        for c in range(PASSES):
+            cast_w1("shared", c, "scalar")
+            quantize_words("shared", AT_W1 + c * H, AT_W1 + (c + 1) * H)
+        bank = routed_bank()
+        for c in range(PASSES):
+            cast_w1(0, c, "scalar")
+            quantize_words(0, AT_W1 + c * H, AT_W1 + (c + 1) * H)
+            first_pass(0, c, bank, slot_codes, slot_scales, S, 0)
+        cast_w2(0, on_scalar)
+        cast_w1(1, 0, "scalar")
+        quantize_words(1, AT_W2, AT_W1 + P)
+        quantize_words(1, AT_W1 + P, AT_W1 + H)
+        cast_w2(1, on_scalar)
+        cast = loaded["w1", 1, 0][:].bitcast(BF16)
+        for group in range(2):
+            silu_shared(group, cast[:, group * H : (group + 1) * H])
+        silu(cast[:, EARLY * H : (EARLY + 1) * H], bank)
+        quantize(step(1)[1][:, 0:C], step(1)[2][:, 0:C], cast[:, EARLY * H : (EARLY + 1) * H])
+        for group in range(2, EARLY):
+            silu_shared(group, cast[:, group * H : (group + 1) * H])
 
-        prepare_w1(LAST, 0, on_scalar)
-        dst, src = load_w1(LAST, 1)
-        on_scalar(out=dst[:, 0 : P // 2], in_=src[:, 0 : P // 2])
-        on_scalar(out=dst[:, P // 2 : 5 * P // 8], in_=src[:, P // 2 : 5 * P // 8])
-        on_vector(out=dst[:, 5 * P // 8 : P], in_=src[:, 5 * P // 8 : P])
-        quantize_w1(LAST, 1)
-        hidden_routed(LAST - 1, loaded["w1", LAST, 1][:, 0 : H // 2].bitcast(BF16))
-        prepare_w2(LAST, on_scalar)
-        prepare_w2(LAST - 1, on_vector)
-        hidden_routed(LAST, last_hidden[:])
-        way_back(LAST - 1)
-        prepare_w2(SHARED, on_scalar)
-        way_back(LAST)
+        for e in range(1, E):
+            bank = routed_bank()
+            if e == LAST:
+                cast_w1(e, 0, "vector")
+                quantize_words(e, AT_W1, AT_W1 + H)
+                first_pass(e, 0, bank, slot_codes, slot_scales, S, e * C)
+                cast_w1(e, 1, "halves")
+                quantize_words(e, AT_W1 + H, AT_W1 + H + H // 2)
+                quantize_words(e, AT_W1 + H + H // 2, STEP_WORDS)
+                first_pass(e, 1, bank, slot_codes, slot_scales, S, e * C)
+                cast_w2(LAST - 1, on_scalar)
+                cast_w2(LAST, on_vector)
+                silu(hidden_values(e), bank)
+            elif e in WOVEN:
+                cast_w1(e, 0, "vector")
+                if e < LAST - 1:
+                    cast_w2(e, on_scalar)
+                cast_w1(e, 1, "halves")
+                if e in LATE:
+                    place = loaded["w1", e, 1][:].bitcast(BF16)[:, 0 : LATE[e][1] * H]
+                    for part in range(LATE[e][1]):
+                        silu_shared(LATE[e][0] + part, place[:, part * H : (part + 1) * H])
+                quantize_words(e, 0, 3 * P)
+                second = second_bank()
+                second_layer(e - 1, second, [0])
+                first_layer(e, [(1, 0)], bank, slot_codes, slot_scales, S, e * C)
+                quantize_words(e, 3 * P, 7 * P)
+                first_layer(e, [(0, 0), (1, 1), (0, 1), (1, 2)], bank, slot_codes, slot_scales, S, e * C)
+                way_back_block(e - 1, second, 0)
+                quantize_words(e, 7 * P, STEP_WORDS)
+                first_layer(e, [(0, 2), (1, 3), (0, 3)], bank, slot_codes, slot_scales, S, e * C)
+                silu(hidden_values(e), bank)
+                second_layer(e - 1, second, [1])
+                way_back_block(e - 1, second, 1)
+                if e in LATE:
+                    quantize_shared(LATE[e][0], LATE[e][1], place)
+            else:
+                second = second_bank()
+                second_layer(0, second, range(BLOCKS))
+                first_pass(e, 0, bank, slot_codes, slot_scales, S, e * C)
+                cast_w1(e, 1, "halves")
+                quantize_words(e, AT_W1 + H, AT_W1 + H + H // 2)
+                quantize_words(e, AT_W1 + H + H // 2, STEP_WORDS)
+                first_pass(e, 1, bank, slot_codes, slot_scales, S, e * C)
+                silu(hidden_values(e), bank)
+                way_back(0, second)
+                quantize_shared(0, 4, cast[:, 0 : 4 * H])
+                quantize_shared(4, EARLY - 4, cast[:, 4 * H : EARLY * H])
 
-        hidden_shared(4, 4, loaded["w2", SHARED][:, 0 : 2 * H].bitcast(BF16))
-        hidden_shared(8, 2, loaded["w2", SHARED][:, 2 * H : 3 * H].bitcast(BF16))
+        quantize_words(E, 0, 4 * P)
+        second = second_bank()
+        second_layer(LAST - 1, second, range(BLOCKS))
+        way_back(LAST - 1, second)
+        quantize_words(E, 4 * P, 6 * P)
+        second = second_bank()
+        second_layer(LAST, second, range(BLOCKS))
+        cast_w2(SHARED, on_scalar)
+        quantize_words(E, 6 * P, 8 * P)
+        for b in range(BLOCKS):
+            way_back_block(LAST, second, b)
 
-        w_codes, w_scales = weights["w2", SHARED]
+        w_codes, w_scales = step(E)[1:]
         narrow = psum.tile([P, BANK], F32, name="narrow", tag="bank_second", bufs=2)
         ys = {}
-        for start, width in OUT_CUTS:
-            for b in range(BLOCKS):
-                rows = slice(b * P, (b + 1) * P)
+        for b in range(BLOCKS):
+            for start, width in OUT_CUTS:
+                rows = slice((6 + b) * P, (7 + b) * P)
                 if width == BANK:
-                    wide = psum.tile([P, BANK], F32, name="wide", tag=("bank_routed" if start else "bank_spare"), bufs=2)
+                    wide = psum.tile([P, BANK], F32, name="wide", tag="bank_shared", bufs=4)
                     ys[b, start] = wide[:]
                 else:
                     ys[b, start] = narrow[:, b * width : (b + 1) * width]
                 cols = slice(start, start + width)
                 multiply(ys[b, start], w_codes[:, rows], w_scales[:, rows], hs_codes[:, cols], hs_scales[:, cols])
-        for start, width in OUT_CUTS:
-            for b in range(BLOCKS):
+        for b in range(BLOCKS):
+            for start, width in OUT_CUTS:
                 cols = slice(start, start + width)
                 tile = load_tile()
                 nc.vector.tensor_tensor(tile[:, 0:width], ys[b, start], routed[b][:, cols], ADD)

@@ -28,14 +28,15 @@ PASSES = K // PASS
 BANK = 512
 BLOCKS = N // P
 WINDOW = 1408
-LOAD_BUFS = 10
+LOAD_BUFS = 5
 FIRST_SHARE = 104
 VECTOR_TOKENS = {(0, 1): 176}
-PIECES = {1: (0, 224), 2: (224, 384), 4: (384, 544), 5: (544, 704), 6: (704, 864), 7: (864, 1024)}
+PIECES = {1: (0, 160), 2: (160, 320), 4: (320, 544), 5: (544, 704), 6: (704, 864), 7: (864, 1024)}
 AT_H, AT_W2, AT_W1, STEP_WORDS = 0, C, C + N, C + N + PASSES * H
-WOVEN = (2, 3, 4, 5, 6)
+JOINED = (2, 3, 4)
+WOVEN = (5, 6)
 EARLY = 6
-LATE = {4: (6, 1), 5: (7, 3)}
+LATE = {4: (6, 3), 5: (9, 1)}
 X_CUTS = ((0, 1024), (1024, 256))
 OUT_CUTS = ((0, 512), (512, 512), (1024, 256))
 
@@ -92,8 +93,15 @@ def tile_moe_shr_mlp_silu_kernel(tc, xT, w1, w2, gate, offs, out):
         loaded = {}
         steps = {}
 
-        def load_tile():
-            return ring.tile([P, PACK * H], F32, name="load", tag="load", bufs=LOAD_BUFS, align_bytes=64)
+        room = {}
+
+        def load_place(width):
+            if room.get("free", 0) < width:
+                room["tile"] = ring.tile([P, 2 * PACK * H], F32, name="load", tag="load", bufs=LOAD_BUFS, align_bytes=64)
+                room["free"] = 2 * PACK * H
+            at = 2 * PACK * H - room["free"]
+            room["free"] = room["free"] - width
+            return room["tile"][:, at : at + width]
 
         def stage_tile():
             return ring.tile([P, PACK * STEP_WORDS], BF16, name="stage", tag="stage", bufs=4, align_bytes=64)
@@ -188,17 +196,28 @@ def tile_moe_shr_mlp_silu_kernel(tc, xT, w1, w2, gate, offs, out):
             values, codes, scales = step(e)
             quantize(codes[:, first:last], scales[:, first:last], values[:, PACK * first : PACK * last])
 
+        def load_joined(e):
+            tile = ring.tile([P, 2 * PACK * H], F32, name="load", tag="load", bufs=LOAD_BUFS, align_bytes=64)
+            nc.sync.dma_start(
+                out=tile[:].rearrange("p (c x) -> p c x", c=PASSES),
+                in_=w1[e].rearrange("(c p j) w -> p c (j w)", c=PASSES, j=PACK),
+            )
+            for c in range(PASSES):
+                loaded["w1", e, c] = tile[:, c * PACK * H : (c + 1) * PACK * H]
+
         def cast_w1(e, c, engine):
-            tile = load_tile()
-            source = w1[SHARED if e == "shared" else e, c * PASS : (c + 1) * PASS, :]
-            nc.sync.dma_start(out=tile[:], in_=source.rearrange("(p j) w -> p (j w)", j=PACK))
-            loaded["w1", e, c] = tile
+            if e not in JOINED:
+                tile = load_place(PACK * H)
+                source = w1[SHARED if e == "shared" else e, c * PASS : (c + 1) * PASS, :]
+                nc.sync.dma_start(out=tile, in_=source.rearrange("(p j) w -> p (j w)", j=PACK))
+                loaded["w1", e, c] = tile
+            tile = loaded["w1", e, c]
             values = step(e)[0][:, PACK * w1_at(e) : PACK * (w1_at(e) + PASSES * H)]
             if e in WOVEN:
                 dst = values.rearrange("p (t c m a b) -> p c m a t b", t=PACK, c=PASSES, a=2, b=2)[:, 1 - c]
             else:
-                dst = values.rearrange("p (c t m a b) -> p c m a t b", t=PACK, c=PASSES, a=2, b=2)[:, c]
-            src = tile[:].rearrange("p (a b m t) -> p m a t b", t=PACK, a=2, b=2)
+                dst = values.rearrange("p (c t m a b) -> p c m a t b", t=PACK, c=PASSES, a=2, b=2)[:, 1 - c if e in JOINED else c]
+            src = tile.rearrange("p (a b m t) -> p m a t b", t=PACK, a=2, b=2)
             if engine == "scalar":
                 on_scalar(out=dst, in_=src)
             elif engine == "vector":
@@ -211,9 +230,9 @@ def tile_moe_shr_mlp_silu_kernel(tc, xT, w1, w2, gate, offs, out):
                 on_vector(out=dst[:, :, :, 2:4], in_=src[:, :, :, 2:4])
 
         def cast_w2(e, copy):
-            tile = load_tile()
-            nc.sync.dma_start(out=tile[:, 0 : PACK * N], in_=w2[e].rearrange("(p j) w -> p (j w)", j=PACK))
-            src = tile[:, 0 : PACK * N].rearrange("p (t g i) -> p g t i", i=4, t=PACK)
+            tile = load_place(PACK * N)
+            nc.sync.dma_start(out=tile, in_=w2[e].rearrange("(p j) w -> p (j w)", j=PACK))
+            src = tile.rearrange("p (t g i) -> p g t i", i=4, t=PACK)
             place, at = w2_at(e, 0)
             if w2_at(e, 1)[1] == at + P:
                 values = step(place)[0][:, PACK * at : PACK * (at + N)]
@@ -238,7 +257,7 @@ def tile_moe_shr_mlp_silu_kernel(tc, xT, w1, w2, gate, offs, out):
         def first_layer(e, order, bank, codes, scales, width, first):
             w_codes, w_scales = step(e)[1:]
             for c, t in order:
-                at = w1_at(e) + (2 * t + 1 - c) * P if e in WOVEN else AT_W1 + c * H + t * P
+                at = w1_at(e) + (2 * t + 1 - c) * P if e in WOVEN else AT_W1 + (1 - c if e in JOINED else c) * H + t * P
                 rows = slice(at, at + P)
                 cols = slice(c * width + first, c * width + first + C)
                 multiply(
@@ -247,8 +266,8 @@ def tile_moe_shr_mlp_silu_kernel(tc, xT, w1, w2, gate, offs, out):
                     w_scales[:, rows],
                     codes[:, cols],
                     scales[:, cols],
-                    start=((c, t) == ((1, 0) if e in WOVEN else (0, 0))),
-                    stop=((c, t) == ((0, 3) if e in WOVEN else (1, 3))),
+                    start=((c, t) == ((1, 0) if e in WOVEN + JOINED else (0, 0))),
+                    stop=((c, t) == ((0, 3) if e in WOVEN + JOINED else (1, 3))),
                 )
 
         def first_pass(e, c, bank, codes, scales, width, first):
@@ -323,7 +342,7 @@ def tile_moe_shr_mlp_silu_kernel(tc, xT, w1, w2, gate, offs, out):
         quantize_words(1, AT_W2, AT_W1 + P)
         quantize_words(1, AT_W1 + P, AT_W1 + H)
         cast_w2(1, on_scalar)
-        cast = loaded["w1", 1, 0][:].bitcast(BF16)
+        cast = loaded["w1", 1, 0].bitcast(BF16)
         for group in range(2):
             silu_shared(group, cast[:, group * H : (group + 1) * H])
         silu(cast[:, EARLY * H : (EARLY + 1) * H], bank)
@@ -344,13 +363,34 @@ def tile_moe_shr_mlp_silu_kernel(tc, xT, w1, w2, gate, offs, out):
                 cast_w2(LAST - 1, on_scalar)
                 cast_w2(LAST, on_vector)
                 silu(hidden_values(e), bank)
+            elif e in JOINED:
+                load_joined(e)
+                cast_w1(e, 1, "vector")
+                cast_w1(e, 0, "vector")
+                if e in LATE:
+                    place = loaded["w1", e, 1].bitcast(BF16)[:, 0 : LATE[e][1] * H]
+                    for part in range(LATE[e][1]):
+                        silu_shared(LATE[e][0] + part, place[:, part * H : (part + 1) * H])
+                cast_w2(e, on_scalar)
+                quantize_words(e, 0, 4 * P)
+                second = second_bank()
+                second_layer(e - 1, second, range(BLOCKS))
+                first_layer(e, [(1, 0)], bank, slot_codes, slot_scales, S, e * C)
+                quantize_words(e, 4 * P, 8 * P)
+                first_layer(e, [(1, 1), (1, 2), (1, 3), (0, 0)], bank, slot_codes, slot_scales, S, e * C)
+                way_back(e - 1, second)
+                quantize_words(e, 8 * P, STEP_WORDS)
+                first_layer(e, [(0, 1), (0, 2), (0, 3)], bank, slot_codes, slot_scales, S, e * C)
+                silu(hidden_values(e), bank)
+                if e in LATE:
+                    quantize_shared(LATE[e][0], LATE[e][1], place)
             elif e in WOVEN:
                 cast_w1(e, 0, "vector")
                 if e < LAST - 1:
                     cast_w2(e, on_scalar)
                 cast_w1(e, 1, "halves")
                 if e in LATE:
-                    place = loaded["w1", e, 1][:].bitcast(BF16)[:, 0 : LATE[e][1] * H]
+                    place = loaded["w1", e, 1].bitcast(BF16)[:, 0 : LATE[e][1] * H]
                     for part in range(LATE[e][1]):
                         silu_shared(LATE[e][0] + part, place[:, part * H : (part + 1) * H])
                 quantize_words(e, 0, 3 * P)
@@ -408,6 +448,6 @@ def tile_moe_shr_mlp_silu_kernel(tc, xT, w1, w2, gate, offs, out):
         for b in range(BLOCKS):
             for start, width in OUT_CUTS:
                 cols = slice(start, start + width)
-                tile = load_tile()
-                nc.vector.tensor_tensor(tile[:, 0:width], ys[b, start], routed[b][:, cols], ADD)
-                nc.sync.dma_start(out=out[b * P : (b + 1) * P, cols], in_=tile[:, 0:width])
+                tile = load_place(width)
+                nc.vector.tensor_tensor(tile, ys[b, start], routed[b][:, cols], ADD)
+                nc.sync.dma_start(out=out[b * P : (b + 1) * P, cols], in_=tile)

@@ -28,15 +28,14 @@ PASSES = K // PASS
 BANK = 512
 BLOCKS = N // P
 WINDOW = 1408
-LOAD_BUFS = 5
+LOAD_BUFS = 6
 FIRST_SHARE = 104
 VECTOR_TOKENS = {(0, 1): 176}
-PIECES = {1: (0, 160), 2: (160, 320), 4: (320, 544), 5: (544, 704), 6: (704, 864), 7: (864, 1024)}
-AT_H, AT_W2, AT_W1, STEP_WORDS = 0, C, C + N, C + N + PASSES * H
-JOINED = (2, 3, 4)
-WOVEN = (5, 6)
-EARLY = 6
-LATE = {4: (6, 3), 5: (9, 1)}
+SCALAR_JOINS = (320, 160)
+PIECES = {1: (0, 256), 3: (256, 512), 5: (512, 704), 6: (704, 864), 7: (864, 1024)}
+AT_W2, AT_H, AT_W1, STEP_WORDS = 0, 2 * N, 2 * N + 2 * C, 2 * N + 2 * C + PASSES * H
+SCALAR_COLUMNS = {4: 128, 7: 0}
+EARLY = 4
 X_CUTS = ((0, 1024), (1024, 256))
 OUT_CUTS = ((0, 512), (512, 512), (1024, 256))
 
@@ -47,8 +46,18 @@ def tile_moe_shr_mlp_silu_kernel(tc, xT, w1, w2, gate, offs, out):
     with ExitStack() as ctx:
         lists = ctx.enter_context(tc.tile_pool(name="lists", bufs=1))
         held = ctx.enter_context(tc.tile_pool(name="held", bufs=1))
-        ring = ctx.enter_context(tc.tile_pool(name="ring", bufs=2))
-        psum = ctx.enter_context(tc.psum_pool(name="psum", bufs=2))
+        ring = ctx.enter_context(tc.tile_pool(name="ring", bufs=1))
+        psum = ctx.enter_context(tc.psum_pool(name="psum", bufs=1))
+
+        def tile(name, width, dtype, tag=None, bufs=1):
+            pool = held if bufs == 1 else ring
+            return pool.tile([P, width], dtype, name=name, tag=tag or name, bufs=bufs, align_bytes=64)
+
+        def load_tile():
+            return tile("load", PASSES * PACK * H, F32, bufs=LOAD_BUFS)
+
+        def bank_tile(tag):
+            return psum.tile([P, BANK], F32, name=tag, tag=tag, bufs={"first": 3, "shared": 3, "second": 2}[tag])
 
         offsets = lists.tile([P, S // 16], U16, name="offsets")
 
@@ -62,17 +71,17 @@ def tile_moe_shr_mlp_silu_kernel(tc, xT, w1, w2, gate, offs, out):
 
         routed = []
         for b in range(BLOCKS):
-            window = held.tile([P, T], F32, name=f"routed{b}", align_bytes=64)
+            window = tile(f"routed{b}", T, F32)
             (nc.gpsimd if b else nc.vector).memset(window[:], 0.0)
             routed.append(window)
 
-        gates = held.tile([P, S], F32, name="gates", align_bytes=64)
+        gates = tile("gates", S, F32)
         gate_columns = held.tile([P, E], F32, name="gate_columns")
 
         def spread_gates():
             nc.sync.dma_start(out=gate_columns[:], in_=gate[0].rearrange("(n j) -> n j", j=E))
             for half in range(2):
-                bank = psum.tile([P, BANK], F32, name="gate_bank", tag="bank_shared", bufs=4)
+                bank = bank_tile("shared")
                 for j in range(4):
                     column = gate_columns[:, 4 * half + j : 4 * half + j + 1].to_broadcast([P, P])
                     nc.tensor.transpose(bank[:, j * P : (j + 1) * P], column, identity[:])
@@ -81,43 +90,27 @@ def tile_moe_shr_mlp_silu_kernel(tc, xT, w1, w2, gate, offs, out):
                     in_=bank[:].rearrange("p (j n) -> p n j", j=4),
                 )
 
-        x_codes = held.tile([P, PASSES * T], U32, name="x_codes", align_bytes=64)
-        x_scales = held.tile([P, PASSES * T], U8, name="x_scales", align_bytes=64)
-        pairs = [held.tile([P, PACK * WINDOW], BF16, name=f"pairs{c}", tag=f"pairs{c}", align_bytes=64) for c in range(PASSES)]
-        for tile in pairs:
-            nc.vector.memset(tile[:].rearrange("p (u w) -> p u w", u=2)[:, :, 2 * T : 2 * WINDOW], 0.0)
-        slot_codes = held.tile([P, PASSES * S], U32, name="slot_codes", align_bytes=64)
-        slot_scales = held.tile([P, PASSES * S], U8, name="slot_scales", align_bytes=64)
-        hs_scales = held.tile([P, T], U8, name="hs_scales", align_bytes=64)
+        x_codes = tile("x_codes", PASSES * T, U32)
+        x_scales = tile("x_scales", PASSES * T, U8)
+        pairs = [tile(f"pairs{c}", PACK * STEP_WORDS, BF16) for c in range(PASSES)]
+        for part in pairs:
+            nc.vector.memset(part[:, 0 : PACK * WINDOW].rearrange("p (u w) -> p u w", u=2)[:, :, 2 * T : 2 * WINDOW], 0.0)
+        slot_codes = tile("slot_codes", PASSES * S, U32)
+        slot_scales = tile("slot_scales", PASSES * S, U8)
 
-        loaded = {}
-        steps = {}
+        def quantize(codes, scales, values):
+            nc.vector.quantize_mx(out=codes.bitcast(FP8X4), scales=scales, in_=values)
 
-        room = {}
-
-        def load_place(width):
-            if room.get("free", 0) < width:
-                room["tile"] = ring.tile([P, 2 * PACK * H], F32, name="load", tag="load", bufs=LOAD_BUFS, align_bytes=64)
-                room["free"] = 2 * PACK * H
-            at = 2 * PACK * H - room["free"]
-            room["free"] = room["free"] - width
-            return room["tile"][:, at : at + width]
-
-        def stage_tile():
-            return ring.tile([P, PACK * STEP_WORDS], BF16, name="stage", tag="stage", bufs=4, align_bytes=64)
-
-        def load_x(c, u, parts=1):
-            tile = stage_tile()
+        def load_x(c, u, parts):
             rows = xT[c * PASS : (c + 1) * PASS, :].rearrange("(p u e) w -> u p e w", u=2, e=2)[u]
-            places = tile[:, 0 : PACK * T].bitcast(F32).rearrange("p (h e w) -> p h e w", h=parts, e=2)
+            places = load_tile()[:, 0 : 2 * T].rearrange("p (h e w) -> p h e w", h=parts, e=2)
             width = T // parts
             for h in range(parts):
                 nc.sync.dma_start(out=places[:, h], in_=rows[:, :, h * width : (h + 1) * width])
-            loaded["x", c, u] = [places[:, h] for h in range(parts)]
+            return [places[:, h] for h in range(parts)]
 
-        def pair_x(c, u):
+        def pair_x(c, u, parts):
             tokens = pairs[c][:, u * 2 * WINDOW : u * 2 * WINDOW + 2 * T].rearrange("p (g i e) -> p g e i", i=4, e=2)
-            parts = loaded["x", c, u]
             groups = T // 4 // len(parts)
             share = FIRST_SHARE if len(parts) > 1 else VECTOR_TOKENS.get((c, u), 0)
             for h, place in enumerate(parts):
@@ -131,117 +124,94 @@ def tile_moe_shr_mlp_silu_kernel(tc, xT, w1, w2, gate, offs, out):
             window = pairs[c][:, u * 2 * WINDOW : (u + 1) * 2 * WINDOW].bitcast(U32)
             on_vector(out=gathered[:, u * S : (u + 1) * S], in_=window.indirect(offsets[:]))
 
-        def join_pairs(name, source, width, helped=0):
-            tile = ring.tile([P, PACK * width], BF16, name=name, tag=name, bufs=1, align_bytes=64)
-            words = source[:].bitcast(F32).rearrange("p (u w) -> p u w", u=2)[:, :, 0:width]
-            dst = tile[:].bitcast(F32).rearrange("p (g i u) -> p g u i", i=4, u=2)
-            src = words.rearrange("p u (g i) -> p g u i", i=4)
-            on_vector(out=dst[:, helped:], in_=src[:, helped:])
+        def join_pairs(name, words, width, helped):
+            joined = tile(name, PACK * width, BF16)
+            dst = joined[:].bitcast(F32).rearrange("p (g i u) -> p g u i", i=4, u=2)
+            src = words.bitcast(F32).rearrange("p (u w) -> p u w", u=2)[:, :, 0:width].rearrange("p u (g i) -> p g u i", i=4)
+            if helped < width // 4:
+                on_vector(out=dst[:, helped:], in_=src[:, helped:])
             if helped:
                 on_scalar(out=dst[:, 0:helped], in_=src[:, 0:helped])
-            return tile
+            return joined
 
-        def quantize(codes, scales, values):
-            nc.vector.quantize_mx(out=codes.bitcast(FP8X4), scales=scales, in_=values)
-
-        load_x(0, 0, parts=2)
+        x_tiles = {(0, 0): load_x(0, 0, 2)}
         spread_gates()
         nc.sync.dma_start(offsets[:], offs)
         for c, u in ((0, 1), (1, 0), (1, 1)):
-            load_x(c, u)
+            x_tiles[c, u] = load_x(c, u, 1)
         for c in range(PASSES):
-            pair_x(c, 0)
-            gathered = ring.tile([P, 2 * S], U32, name="gathered", tag="gathered", bufs=1, align_bytes=64)
-            gather(c, 0, gathered)
-            pair_x(c, 1)
-            gather(c, 1, gathered)
-            token_values = join_pairs("token_values", pairs[c], T, 160 if c == 0 else 0)
-            slot_values = join_pairs("slot_values", gathered, S)
+            gathered = tile("gathered", 2 * S, U32)
+            for u in range(2):
+                pair_x(c, u, x_tiles[c, u])
+                gather(c, u, gathered)
+            token_values = join_pairs("token_values", pairs[c][:, 0 : PACK * WINDOW], T, SCALAR_JOINS[c])
+            slot_values = join_pairs("slot_values", gathered[:], S, 0)
+            quantize(slot_codes[:, c * S : (c + 1) * S], slot_scales[:, c * S : (c + 1) * S], slot_values[:])
             for start, width in X_CUTS:
                 cols = slice(c * T + start, c * T + start + width)
                 quantize(x_codes[:, cols], x_scales[:, cols], token_values[:, PACK * start : PACK * (start + width)])
-            quantize(slot_codes[:, c * S : (c + 1) * S], slot_scales[:, c * S : (c + 1) * S], slot_values[:])
 
-        y = held.tile([P, BLOCKS * S], F32, name="y", tag="pairs0", align_bytes=64)
-        hs_codes = held.tile([P, T], U32, name="hs_codes", tag="pairs1", align_bytes=64)
+        value_tags = {0: "gathered", 1: "slot_values", 2: "pairs0", 3: "gathered", 4: "pairs1", 5: "shared_values",
+                      6: "pairs0", 7: "shared_values", "shared": "shared_values", "tail": "pairs1"}
+        steps = {}
 
         def step(e):
             if e not in steps:
-                values = stage_tile()
+                words = STEP_WORDS if e in (2, 4, 6) else PASSES * H
+                values = tile("values", PACK * words, BF16, tag=value_tags[e])
                 if e == "shared":
-                    codes = ring.tile([P, STEP_WORDS], U32, name="shared_codes", tag="token_values", bufs=1, align_bytes=64)
-                    scales = ring.tile([P, STEP_WORDS], U8, name="shared_scales", tag="shared_scales", bufs=1, align_bytes=64)
+                    steps[e] = (values, tile("shared_codes", words, U32), tile("shared_scales", words, U8))
                 else:
-                    codes = ring.tile([P, STEP_WORDS], U32, name="step_codes", tag="step_codes", bufs=3, align_bytes=64)
-                    scales = ring.tile([P, STEP_WORDS], U8, name="step_scales", tag="step_scales", bufs=3, align_bytes=64)
-                steps[e] = (values, codes, scales)
+                    steps[e] = (values, tile("codes", words, U32, bufs=3), tile("scales", words, U8, bufs=3))
             return steps[e]
 
         def w1_at(e):
-            return 2 * P if e in WOVEN else AT_W1
+            return AT_W1 if e in (2, 4, 6) else 0
 
         def hidden_at(e):
-            return (E, (e - LAST + 1) * 4 * P) if e >= LAST - 1 else (e + 1, AT_H)
+            return ("tail", (e - 6) * (C + N)) if e >= 6 else (e + 2 - e % 2, AT_H + e % 2 * C)
 
-        def w2_at(e, b):
-            if e >= LAST - 1:
-                return (E, {LAST - 1: (1 + b) * P, LAST: (3 + 2 * b) * P, SHARED: (6 + b) * P}[e])
-            return (e + 1, STEP_WORDS - P if e + 1 in WOVEN and b == 1 else AT_W2 + b * P)
+        def w2_at(e):
+            if e == SHARED:
+                return ("tail", 2 * (C + N))
+            return ("tail", (e - 6) * (C + N) + C) if e >= 6 else (e + 2 - e % 2, AT_W2 + e % 2 * N)
 
-        def hidden_values(e):
-            place, at = hidden_at(e)
-            return step(place)[0][:, PACK * at : PACK * (at + C)]
+        def words_of(place, at, count):
+            return step(place)[0][:, PACK * at : PACK * (at + count)]
 
         def quantize_words(e, first, last):
             values, codes, scales = step(e)
             quantize(codes[:, first:last], scales[:, first:last], values[:, PACK * first : PACK * last])
 
-        def load_joined(e):
-            tile = ring.tile([P, 2 * PACK * H], F32, name="load", tag="load", bufs=LOAD_BUFS, align_bytes=64)
-            nc.sync.dma_start(
-                out=tile[:].rearrange("p (c x) -> p c x", c=PASSES),
-                in_=w1[e].rearrange("(c p j) w -> p c (j w)", c=PASSES, j=PACK),
+        def load_w1(e, parts):
+            places = load_tile()[:].rearrange("p (c x) -> p c x", c=PASSES)
+            source = w1[SHARED if e == "shared" else e].rearrange("(c p j) w -> p c (j w)", c=PASSES, j=PACK)
+            if parts == 1:
+                nc.sync.dma_start(out=places, in_=source)
+            else:
+                for c in range(PASSES):
+                    nc.sync.dma_start(out=places[:, c], in_=source[:, c])
+            return places
+
+        def cast_w1(e, c, loaded, helped):
+            dst = words_of(e, w1_at(e) + c * H, H).rearrange("p (t m a b) -> p m a t b", t=PACK, a=2, b=2)
+            src = loaded[:, c].rearrange("p (a b m t) -> p m a t b", t=PACK, a=2, b=2)
+            if helped:
+                on_scalar(out=dst[:, 0:helped], in_=src[:, 0:helped])
+            if helped < P:
+                on_vector(out=dst[:, helped:P], in_=src[:, helped:P])
+
+        def load_w2(first, count):
+            places = load_tile()[:, 0 : count * PACK * N].rearrange("p (e x) -> p e x", e=count)
+            nc.sync.dma_start(out=places, in_=w2[first : first + count].rearrange("e (p j) w -> p e (j w)", j=PACK))
+            return places
+
+        def cast_w2(first, count, loaded, copy):
+            values = words_of(*w2_at(first), count * N)
+            copy(
+                out=values.rearrange("p (e g i t) -> p e g t i", e=count, i=4, t=PACK),
+                in_=loaded.rearrange("p e (t g i) -> p e g t i", i=4, t=PACK),
             )
-            for c in range(PASSES):
-                loaded["w1", e, c] = tile[:, c * PACK * H : (c + 1) * PACK * H]
-
-        def cast_w1(e, c, engine):
-            if e not in JOINED:
-                tile = load_place(PACK * H)
-                source = w1[SHARED if e == "shared" else e, c * PASS : (c + 1) * PASS, :]
-                nc.sync.dma_start(out=tile, in_=source.rearrange("(p j) w -> p (j w)", j=PACK))
-                loaded["w1", e, c] = tile
-            tile = loaded["w1", e, c]
-            values = step(e)[0][:, PACK * w1_at(e) : PACK * (w1_at(e) + PASSES * H)]
-            if e in WOVEN:
-                dst = values.rearrange("p (t c m a b) -> p c m a t b", t=PACK, c=PASSES, a=2, b=2)[:, 1 - c]
-            else:
-                dst = values.rearrange("p (c t m a b) -> p c m a t b", t=PACK, c=PASSES, a=2, b=2)[:, 1 - c if e in JOINED else c]
-            src = tile.rearrange("p (a b m t) -> p m a t b", t=PACK, a=2, b=2)
-            if engine == "scalar":
-                on_scalar(out=dst, in_=src)
-            elif engine == "vector":
-                on_vector(out=dst, in_=src)
-            elif engine == "both":
-                on_scalar(out=dst[:, :, :, 2:4], in_=src[:, :, :, 2:4])
-                on_vector(out=dst[:, :, :, 0:2], in_=src[:, :, :, 0:2])
-            else:
-                on_vector(out=dst[:, :, :, 0:2], in_=src[:, :, :, 0:2])
-                on_vector(out=dst[:, :, :, 2:4], in_=src[:, :, :, 2:4])
-
-        def cast_w2(e, copy):
-            tile = load_place(PACK * N)
-            nc.sync.dma_start(out=tile, in_=w2[e].rearrange("(p j) w -> p (j w)", j=PACK))
-            src = tile.rearrange("p (t g i) -> p g t i", i=4, t=PACK)
-            place, at = w2_at(e, 0)
-            if w2_at(e, 1)[1] == at + P:
-                values = step(place)[0][:, PACK * at : PACK * (at + N)]
-                copy(out=values.rearrange("p (g i t) -> p g t i", i=4, t=PACK), in_=src)
-            else:
-                for b in range(BLOCKS):
-                    at = w2_at(e, b)[1]
-                    values = step(place)[0][:, PACK * at : PACK * (at + P)]
-                    copy(out=values.rearrange("p (g i t) -> p g t i", i=4, t=PACK), in_=src[:, b * P // 4 : (b + 1) * P // 4])
 
         def multiply(bank, w_codes, w_scales, codes, scales, start=True, stop=True):
             nc.tensor.matmul_mx(
@@ -254,200 +224,169 @@ def tile_moe_shr_mlp_silu_kernel(tc, xT, w1, w2, gate, offs, out):
                 stop=stop,
             )
 
-        def first_layer(e, order, bank, codes, scales, width, first):
+        def first_layer(e, c, quarters, bank, codes, scales, first):
             w_codes, w_scales = step(e)[1:]
-            for c, t in order:
-                at = w1_at(e) + (2 * t + 1 - c) * P if e in WOVEN else AT_W1 + (1 - c if e in JOINED else c) * H + t * P
-                rows = slice(at, at + P)
-                cols = slice(c * width + first, c * width + first + C)
+            for t in quarters:
+                rows = slice(w1_at(e) + c * H + t * P, w1_at(e) + c * H + (t + 1) * P)
                 multiply(
                     bank[:, t * C : (t + 1) * C],
                     w_codes[:, rows],
                     w_scales[:, rows],
-                    codes[:, cols],
-                    scales[:, cols],
-                    start=((c, t) == ((1, 0) if e in WOVEN + JOINED else (0, 0))),
-                    stop=((c, t) == ((0, 3) if e in WOVEN + JOINED else (1, 3))),
+                    codes[:, first : first + C],
+                    scales[:, first : first + C],
+                    start=((c, t) == (0, 0)),
+                    stop=((c, t) == (PASSES - 1, PACK - 1)),
                 )
 
-        def first_pass(e, c, bank, codes, scales, width, first):
-            first_layer(e, [(c, t) for t in range(PACK)], bank, codes, scales, width, first)
+        def routed_first(e, c, quarters, bank):
+            first_layer(e, c, quarters, bank, slot_codes, slot_scales, c * S + e * C)
 
         def silu(place, bank):
             nc.scalar.activation(
                 place.rearrange("p (n t) -> p n t", t=PACK), bank[:].rearrange("p (t n) -> p n t", t=PACK), SILU
             )
 
-        def routed_bank():
-            return psum.tile([P, PACK * C], F32, name="bank_first", tag="bank_routed", bufs=2)
-
-        def silu_shared(group, place):
-            bank = psum.tile([P, PACK * C], F32, name="bank_shared", tag="bank_shared", bufs=4)
-            for c in range(PASSES):
-                first_pass("shared", c, bank, x_codes, x_scales, T, group * C)
-            silu(place, bank)
-
-        def quantize_shared(first, count, place):
-            cols = slice(first * C, (first + count) * C)
-            quantize(hs_codes[:, cols], hs_scales[:, cols], place)
-
-        def second_bank():
-            return psum.tile([P, BLOCKS * C], F32, name="bank_second", tag="bank_second", bufs=2)
-
         def second_layer(e, bank, blocks):
             place, at = hidden_at(e)
             codes, scales = step(place)[1:]
             slots = slice(at, at + C)
             for b in blocks:
-                rows = slice(w2_at(e, b)[1], w2_at(e, b)[1] + P)
-                multiply(bank[:, b * C : (b + 1) * C], codes[:, rows], scales[:, rows], codes[:, slots], scales[:, slots])
+                rows = slice(w2_at(e)[1] + b * P, w2_at(e)[1] + (b + 1) * P)
+                cols = slice((e % 2 * BLOCKS + b) * C, (e % 2 * BLOCKS + b + 1) * C)
+                multiply(bank[:, cols], codes[:, rows], scales[:, rows], codes[:, slots], scales[:, slots])
 
-        def scatter(e, b):
-            if e in PIECES:
-                first, last = PIECES[e]
-                window = routed[b][:].indirect(offsets[:, first // 16 : last // 16])
-                if (e, b) == (LAST, 0):
-                    on_vector(out=window, in_=y[:, b * S + first : b * S + last])
-                else:
-                    nc.scalar.activation(window, y[:, b * S + first : b * S + last], COPY)
-
-        def way_back(e, bank):
-            slots = slice(e * C, (e + 1) * C)
+        def times_gate(first, count, blocks, bank):
+            slots = slice(first * C, (first + count) * C)
+            experts = slice(first % 2, first % 2 + count)
             nc.vector.tensor_tensor(
-                y[:].rearrange("p (b s) -> p b s", b=BLOCKS)[:, :, slots],
-                bank[:].rearrange("p (b n) -> p b n", b=BLOCKS),
-                gates[:, slots].rearrange("p (o n) -> p o n", o=1).to_broadcast([P, BLOCKS, C]),
+                y[:].rearrange("p (b s) -> p b s", b=BLOCKS)[:, blocks, slots].rearrange("p b (e n) -> p e b n", e=count),
+                bank[:].rearrange("p (e b n) -> p e b n", e=2, b=BLOCKS)[:, experts, blocks],
+                gates[:, slots].rearrange("p (e o n) -> p e o n", e=count, o=1).to_broadcast(
+                    [P, count, blocks.stop - blocks.start, C]
+                ),
                 MULT,
             )
-            for b in range(BLOCKS):
-                scatter(e, b)
 
-        def way_back_block(e, bank, b):
-            slots = slice(e * C, (e + 1) * C)
-            nc.vector.tensor_tensor(
-                y[:, b * S + e * C : b * S + (e + 1) * C], bank[:, b * C : (b + 1) * C], gates[:, slots], MULT
-            )
-            scatter(e, b)
-
-        for c in range(PASSES):
-            cast_w1("shared", c, "scalar")
-            quantize_words("shared", AT_W1 + c * H, AT_W1 + (c + 1) * H)
-        bank = routed_bank()
-        for c in range(PASSES):
-            cast_w1(0, c, "scalar")
-            quantize_words(0, AT_W1 + c * H, AT_W1 + (c + 1) * H)
-            first_pass(0, c, bank, slot_codes, slot_scales, S, 0)
-        cast_w2(0, on_scalar)
-        cast_w1(1, 0, "scalar")
-        quantize_words(1, AT_W2, AT_W1 + P)
-        quantize_words(1, AT_W1 + P, AT_W1 + H)
-        cast_w2(1, on_scalar)
-        cast = loaded["w1", 1, 0].bitcast(BF16)
-        for group in range(2):
-            silu_shared(group, cast[:, group * H : (group + 1) * H])
-        silu(cast[:, EARLY * H : (EARLY + 1) * H], bank)
-        quantize(step(1)[1][:, 0:C], step(1)[2][:, 0:C], cast[:, EARLY * H : (EARLY + 1) * H])
-        for group in range(2, EARLY):
-            silu_shared(group, cast[:, group * H : (group + 1) * H])
-
-        for e in range(1, E):
-            bank = routed_bank()
-            if e == LAST:
-                cast_w1(e, 0, "vector")
-                quantize_words(e, AT_W1, AT_W1 + H)
-                first_pass(e, 0, bank, slot_codes, slot_scales, S, e * C)
-                cast_w1(e, 1, "halves")
-                quantize_words(e, AT_W1 + H, AT_W1 + H + H // 2)
-                quantize_words(e, AT_W1 + H + H // 2, STEP_WORDS)
-                first_pass(e, 1, bank, slot_codes, slot_scales, S, e * C)
-                cast_w2(LAST - 1, on_scalar)
-                cast_w2(LAST, on_vector)
-                silu(hidden_values(e), bank)
-            elif e in JOINED:
-                load_joined(e)
-                cast_w1(e, 1, "vector")
-                cast_w1(e, 0, "vector")
-                if e in LATE:
-                    place = loaded["w1", e, 1].bitcast(BF16)[:, 0 : LATE[e][1] * H]
-                    for part in range(LATE[e][1]):
-                        silu_shared(LATE[e][0] + part, place[:, part * H : (part + 1) * H])
-                cast_w2(e, on_scalar)
-                quantize_words(e, 0, 4 * P)
-                second = second_bank()
-                second_layer(e - 1, second, range(BLOCKS))
-                first_layer(e, [(1, 0)], bank, slot_codes, slot_scales, S, e * C)
-                quantize_words(e, 4 * P, 8 * P)
-                first_layer(e, [(1, 1), (1, 2), (1, 3), (0, 0)], bank, slot_codes, slot_scales, S, e * C)
-                way_back(e - 1, second)
-                quantize_words(e, 8 * P, STEP_WORDS)
-                first_layer(e, [(0, 1), (0, 2), (0, 3)], bank, slot_codes, slot_scales, S, e * C)
-                silu(hidden_values(e), bank)
-                if e in LATE:
-                    quantize_shared(LATE[e][0], LATE[e][1], place)
-            elif e in WOVEN:
-                cast_w1(e, 0, "vector")
-                if e < LAST - 1:
-                    cast_w2(e, on_scalar)
-                cast_w1(e, 1, "halves")
-                if e in LATE:
-                    place = loaded["w1", e, 1].bitcast(BF16)[:, 0 : LATE[e][1] * H]
-                    for part in range(LATE[e][1]):
-                        silu_shared(LATE[e][0] + part, place[:, part * H : (part + 1) * H])
-                quantize_words(e, 0, 3 * P)
-                second = second_bank()
-                second_layer(e - 1, second, [0])
-                first_layer(e, [(1, 0)], bank, slot_codes, slot_scales, S, e * C)
-                quantize_words(e, 3 * P, 7 * P)
-                first_layer(e, [(0, 0), (1, 1), (0, 1), (1, 2)], bank, slot_codes, slot_scales, S, e * C)
-                way_back_block(e - 1, second, 0)
-                quantize_words(e, 7 * P, STEP_WORDS)
-                first_layer(e, [(0, 2), (1, 3), (0, 3)], bank, slot_codes, slot_scales, S, e * C)
-                silu(hidden_values(e), bank)
-                second_layer(e - 1, second, [1])
-                way_back_block(e - 1, second, 1)
-                if e in LATE:
-                    quantize_shared(LATE[e][0], LATE[e][1], place)
+        def scatter(e, b, engine):
+            first, last = PIECES[e]
+            window = routed[b][:].indirect(offsets[:, first // 16 : last // 16])
+            if engine == "vector":
+                on_vector(out=window, in_=y[:, b * S + first : b * S + last])
             else:
-                second = second_bank()
-                second_layer(0, second, range(BLOCKS))
-                first_pass(e, 0, bank, slot_codes, slot_scales, S, e * C)
-                cast_w1(e, 1, "halves")
-                quantize_words(e, AT_W1 + H, AT_W1 + H + H // 2)
-                quantize_words(e, AT_W1 + H + H // 2, STEP_WORDS)
-                first_pass(e, 1, bank, slot_codes, slot_scales, S, e * C)
-                silu(hidden_values(e), bank)
-                way_back(0, second)
-                quantize_shared(0, 4, cast[:, 0 : 4 * H])
-                quantize_shared(4, EARLY - 4, cast[:, 4 * H : EARLY * H])
+                nc.scalar.activation(window, y[:, b * S + first : b * S + last], COPY)
 
-        quantize_words(E, 0, 4 * P)
-        second = second_bank()
+        loaded = load_w1("shared", 2)
+        for c in range(PASSES):
+            cast_w1("shared", c, loaded, P)
+            quantize_words("shared", c * H, (c + 1) * H)
+        loaded = load_w1(0, 1)
+        first_bank = bank_tile("first")
+        for c in range(PASSES):
+            cast_w1(0, c, loaded, P)
+            quantize_words(0, c * H, (c + 1) * H)
+        hs_values = [loaded[:, 1].bitcast(BF16)[:, 0 : EARLY * H], tile("hs_values", PACK * T - EARLY * H, BF16, tag="token_values")[:]]
+        for group in range(T // C):
+            bank = bank_tile("shared")
+            for c in range(PASSES):
+                first_layer("shared", c, range(PACK), bank, x_codes, x_scales, c * T + group * C)
+            late = int(group >= EARLY)
+            silu(hs_values[late][:, (group - late * EARLY) * H : (group - late * EARLY + 1) * H], bank)
+        for c in range(PASSES):
+            routed_first(0, c, range(PACK), first_bank)
+        silu(words_of(*hidden_at(0), C), first_bank)
+        y = tile("y", BLOCKS * S, F32, tag="x_codes")
+        hs_scales = tile("hs_scales", T, U8)
+        hs_codes = {}
+
+        def quantize_shared(e, cuts, values):
+            codes = tile("hs_codes", T, U32, tag=value_tags[e])
+            for start, width in cuts:
+                hs_codes[start] = codes[:, start : start + width]
+                at = start - cuts[0][0]
+                quantize(hs_codes[start], hs_scales[:, start : start + width], values[:, PACK * at : PACK * (at + width)])
+
+        def plain_step(e):
+            loaded = load_w1(e, 2 if e == 5 else 1)
+            bank = bank_tile("first")
+            for c in range(PASSES):
+                cast_w1(e, c, loaded, 0)
+            for c in range(PASSES):
+                quantize_words(e, c * H, (c + 1) * H)
+                routed_first(e, c, range(PACK), bank)
+            silu(words_of(*hidden_at(e), C), bank)
+
+        def step_with_way_back(e):
+            loaded = load_w1(e, 2 if e == 6 else 1)
+            bank = bank_tile("first")
+            cast_w1(e, 0, loaded, 0)
+            cast_w1(e, 1, loaded, SCALAR_COLUMNS.get(e, 0))
+            quantize_words(e, 0, 2 * H)
+            second = bank_tile("second")
+            for before in (e - 2, e - 1):
+                second_layer(before, second, range(BLOCKS))
+            routed_first(e, 0, (0, 1), bank)
+            quantize_words(e, 2 * H, AT_W1 + H)
+            routed_first(e, 0, (2, 3), bank)
+            times_gate(e - 2, 2, slice(0, BLOCKS), second)
+            for b in range(BLOCKS):
+                scatter(e - 1, b, "scalar")
+            quantize_words(e, AT_W1 + H, STEP_WORDS)
+            routed_first(e, 1, range(PACK), bank)
+            silu(words_of(*hidden_at(e), C), bank)
+
+        for e in range(1, LAST - 1, 2):
+            cast_w2(e - 1, 2, load_w2(e - 1, 2), on_scalar)
+            plain_step(e)
+            if e == 1:
+                quantize_shared(e, OUT_CUTS[0:1], hs_values[0])
+            if e == 3:
+                quantize_shared(e, OUT_CUTS[1:], hs_values[1])
+            step_with_way_back(e + 1)
+
+        loaded = load_w1(LAST, 2)
+        bank = bank_tile("first")
+        cast_w1(LAST, 0, loaded, 0)
+        quantize_words(LAST, 0, H)
+        routed_first(LAST, 0, range(PACK), bank)
+        cast_w1(LAST, 1, loaded, SCALAR_COLUMNS[LAST])
+        for half in range(2):
+            quantize_words(LAST, H + half * 2 * P, H + (half + 1) * 2 * P)
+            routed_first(LAST, 1, (2 * half, 2 * half + 1), bank)
+        places = load_tile()[:, 0 : 3 * PACK * N].rearrange("p (e x) -> p e x", e=3)
+        for e in range(3):
+            nc.sync.dma_start(out=places[:, e], in_=w2[LAST - 1 + e].rearrange("(p j) w -> p (j w)", j=PACK))
+        cast_w2(LAST - 1, 1, places[:, 0:1], on_scalar)
+        silu(words_of(*hidden_at(LAST), C), bank)
+        cast_w2(LAST, 1, places[:, 1:2], on_vector)
+        quantize_words("tail", 0, C + N)
+        second = bank_tile("second")
         second_layer(LAST - 1, second, range(BLOCKS))
-        way_back(LAST - 1, second)
-        quantize_words(E, 4 * P, 6 * P)
-        second = second_bank()
+        times_gate(LAST - 1, 1, slice(0, BLOCKS), second)
+        scatter(LAST - 1, 0, "scalar")
+        quantize_words("tail", C + N, 2 * (C + N))
+        second = bank_tile("second")
         second_layer(LAST, second, range(BLOCKS))
-        cast_w2(SHARED, on_scalar)
-        quantize_words(E, 6 * P, 8 * P)
-        for b in range(BLOCKS):
-            way_back_block(LAST, second, b)
+        cast_w2(SHARED, 1, places[:, 2:3], on_scalar)
+        scatter(LAST - 1, 1, "scalar")
+        times_gate(LAST, 1, slice(0, BLOCKS), second)
+        quantize_words("tail", 2 * (C + N), 2 * (C + N) + N)
+        scatter(LAST, 0, "vector")
+        scatter(LAST, 1, "scalar")
 
-        w_codes, w_scales = step(E)[1:]
-        narrow = psum.tile([P, BANK], F32, name="narrow", tag="bank_second", bufs=2)
+        w_codes, w_scales = step("tail")[1:]
+        wide = [bank_tile("shared"), bank_tile("shared"), bank_tile("shared"), bank_tile("first")]
+        narrow = bank_tile("first")
         ys = {}
         for b in range(BLOCKS):
-            for start, width in OUT_CUTS:
-                rows = slice((6 + b) * P, (7 + b) * P)
-                if width == BANK:
-                    wide = psum.tile([P, BANK], F32, name="wide", tag="bank_shared", bufs=4)
-                    ys[b, start] = wide[:]
-                else:
-                    ys[b, start] = narrow[:, b * width : (b + 1) * width]
+            rows = slice(w2_at(SHARED)[1] + b * P, w2_at(SHARED)[1] + (b + 1) * P)
+            for index, (start, width) in enumerate(OUT_CUTS):
+                ys[b, start] = wide[2 * b + index][:] if width == BANK else narrow[:, b * width : (b + 1) * width]
                 cols = slice(start, start + width)
-                multiply(ys[b, start], w_codes[:, rows], w_scales[:, rows], hs_codes[:, cols], hs_scales[:, cols])
+                multiply(ys[b, start], w_codes[:, rows], w_scales[:, rows], hs_codes[start], hs_scales[:, cols])
+        result = load_tile()
         for b in range(BLOCKS):
             for start, width in OUT_CUTS:
                 cols = slice(start, start + width)
-                tile = load_place(width)
-                nc.vector.tensor_tensor(tile, ys[b, start], routed[b][:, cols], ADD)
-                nc.sync.dma_start(out=out[b * P : (b + 1) * P, cols], in_=tile)
+                place = result[:, b * T + start : b * T + start + width]
+                nc.vector.tensor_tensor(place, ys[b, start], routed[b][:, cols], ADD)
+                nc.sync.dma_start(out=out[b * P : (b + 1) * P, cols], in_=place)

@@ -34,7 +34,7 @@ VECTOR_TOKENS = {(0, 1): 176}
 SCALAR_JOINS = (320, 160)
 PIECES = {1: (0, 256), 3: (256, 512), 5: (512, 704), 6: (704, 864), 7: (864, 1024)}
 AT_W2, AT_H, AT_W1, STEP_WORDS = 0, 2 * N, 2 * N + 2 * C, 2 * N + 2 * C + PASSES * H
-SCALAR_COLUMNS = {4: 128, 7: 0}
+SCALAR_COLUMNS = {(4, 1): 96, (6, 1): 96}
 EARLY = 4
 X_CUTS = ((0, 1024), (1024, 256))
 OUT_CUTS = ((0, 512), (512, 512), (1024, 256))
@@ -255,11 +255,14 @@ def tile_moe_shr_mlp_silu_kernel(tc, xT, w1, w2, gate, offs, out):
                 cols = slice((e % 2 * BLOCKS + b) * C, (e % 2 * BLOCKS + b + 1) * C)
                 multiply(bank[:, cols], codes[:, rows], scales[:, rows], codes[:, slots], scales[:, slots])
 
+        def y_of(slots):
+            return y[:, :, slots]
+
         def times_gate(first, count, blocks, bank):
             slots = slice(first * C, (first + count) * C)
             experts = slice(first % 2, first % 2 + count)
             nc.vector.tensor_tensor(
-                y[:].rearrange("p (b s) -> p b s", b=BLOCKS)[:, blocks, slots].rearrange("p b (e n) -> p e b n", e=count),
+                y_of(slots)[:, blocks].rearrange("p b (e n) -> p e b n", e=count),
                 bank[:].rearrange("p (e b n) -> p e b n", e=2, b=BLOCKS)[:, experts, blocks],
                 gates[:, slots].rearrange("p (e o n) -> p e o n", e=count, o=1).to_broadcast(
                     [P, count, blocks.stop - blocks.start, C]
@@ -271,9 +274,9 @@ def tile_moe_shr_mlp_silu_kernel(tc, xT, w1, w2, gate, offs, out):
             first, last = PIECES[e]
             window = routed[b][:].indirect(offsets[:, first // 16 : last // 16])
             if engine == "vector":
-                on_vector(out=window, in_=y[:, b * S + first : b * S + last])
+                on_vector(out=window, in_=y_of(slice(first, last))[:, b])
             else:
-                nc.scalar.activation(window, y[:, b * S + first : b * S + last], COPY)
+                nc.scalar.activation(window, y_of(slice(first, last))[:, b], COPY)
 
         loaded = load_w1("shared", 2)
         for c in range(PASSES):
@@ -294,7 +297,7 @@ def tile_moe_shr_mlp_silu_kernel(tc, xT, w1, w2, gate, offs, out):
         for c in range(PASSES):
             routed_first(0, c, range(PACK), first_bank)
         silu(words_of(*hidden_at(0), C), first_bank)
-        y = tile("y", BLOCKS * S, F32, tag="x_codes")
+        y = tile("y", BLOCKS * S, F32, tag="x_codes")[:].rearrange("p (b s) -> p b s", b=BLOCKS)
         hs_scales = tile("hs_scales", T, U8)
         hs_codes = {}
 
@@ -316,10 +319,10 @@ def tile_moe_shr_mlp_silu_kernel(tc, xT, w1, w2, gate, offs, out):
             silu(words_of(*hidden_at(e), C), bank)
 
         def step_with_way_back(e):
-            loaded = load_w1(e, 2 if e == 6 else 1)
+            loaded = load_w1(e, 1 if e == 2 else 2)
             bank = bank_tile("first")
-            cast_w1(e, 0, loaded, 0)
-            cast_w1(e, 1, loaded, SCALAR_COLUMNS.get(e, 0))
+            for c in range(PASSES):
+                cast_w1(e, c, loaded, SCALAR_COLUMNS.get((e, c), 0))
             quantize_words(e, 0, 2 * H)
             second = bank_tile("second")
             for before in (e - 2, e - 1):
@@ -335,8 +338,13 @@ def tile_moe_shr_mlp_silu_kernel(tc, xT, w1, w2, gate, offs, out):
             silu(words_of(*hidden_at(e), C), bank)
 
         for e in range(1, LAST - 1, 2):
-            cast_w2(e - 1, 2, load_w2(e - 1, 2), on_scalar)
+            if e < LAST - 2:
+                cast_w2(e - 1, 2, load_w2(e - 1, 2), on_scalar)
             plain_step(e)
+            if e == LAST - 2:
+                pair = load_w2(e - 1, 2)
+                cast_w2(e - 1, 1, pair[:, 0:1], on_scalar)
+                cast_w2(e, 1, pair[:, 1:2], on_vector)
             if e == 1:
                 quantize_shared(e, OUT_CUTS[0:1], hs_values[0])
             if e == 3:
@@ -348,7 +356,7 @@ def tile_moe_shr_mlp_silu_kernel(tc, xT, w1, w2, gate, offs, out):
         cast_w1(LAST, 0, loaded, 0)
         quantize_words(LAST, 0, H)
         routed_first(LAST, 0, range(PACK), bank)
-        cast_w1(LAST, 1, loaded, SCALAR_COLUMNS[LAST])
+        cast_w1(LAST, 1, loaded, SCALAR_COLUMNS.get((LAST, 1), 0))
         for half in range(2):
             quantize_words(LAST, H + half * 2 * P, H + (half + 1) * 2 * P)
             routed_first(LAST, 1, (2 * half, 2 * half + 1), bank)
@@ -366,7 +374,7 @@ def tile_moe_shr_mlp_silu_kernel(tc, xT, w1, w2, gate, offs, out):
         quantize_words("tail", C + N, 2 * (C + N))
         second = bank_tile("second")
         second_layer(LAST, second, range(BLOCKS))
-        cast_w2(SHARED, 1, places[:, 2:3], on_scalar)
+        cast_w2(SHARED, 1, places[:, 2:3], on_vector)
         scatter(LAST - 1, 1, "scalar")
         times_gate(LAST, 1, slice(0, BLOCKS), second)
         quantize_words("tail", 2 * (C + N), 2 * (C + N) + N)

@@ -34,7 +34,7 @@ VECTOR_TOKENS = {(0, 1): 176}
 SCALAR_JOINS = (320, 160)
 PIECES = {1: (0, 256), 3: (256, 512), 5: (512, 704), 6: (704, 864), 7: (864, 1024)}
 AT_W2, AT_H, AT_W1, STEP_WORDS = 0, 2 * N, 2 * N + 2 * C, 2 * N + 2 * C + PASSES * H
-SCALAR_COLUMNS = {(4, 1): 96, (6, 1): 96}
+SCALAR_COLUMNS = {(2, 1): 96, (4, 1): 96, (6, 1): 96}
 EARLY = 4
 X_CUTS = ((0, 1024), (1024, 256))
 OUT_CUTS = ((0, 512), (512, 512), (1024, 256))
@@ -339,7 +339,7 @@ def tile_moe_shr_mlp_silu_kernel(tc, xT, w1, w2, gate, offs, out):
 
         for e in range(1, LAST - 1, 2):
             if e < LAST - 2:
-                cast_w2(e - 1, 2, load_w2(e - 1, 2), on_scalar)
+                cast_w2(e - 1, 2, load_w2(e - 1, 2), on_vector if e == 1 else on_scalar)
             plain_step(e)
             if e == LAST - 2:
                 pair = load_w2(e - 1, 2)

@@ -32,9 +32,12 @@ LOAD_BUFS = 6
 FIRST_SHARE = 104
 VECTOR_TOKENS = {(0, 1): 176}
 SCALAR_JOINS = (320, 160)
-PIECES = {1: (0, 256), 3: (256, 512), 5: (512, 704), 6: (704, 864), 7: (864, 1024)}
+PIECES = (
+    {1: (0, 224), 3: (224, 384), 4: (384, 544), 5: (544, 704), 6: (704, 864), 7: (864, 1024)},
+    {1: (0, 256), 3: (256, 480), 4: (480, 640), 6: (640, 864), 7: (864, 1024)},
+)
 AT_W2, AT_H, AT_W1, STEP_WORDS = 0, 2 * N, 2 * N + 2 * C, 2 * N + 2 * C + PASSES * H
-SCALAR_COLUMNS = {(2, 1): 96, (4, 1): 96, (6, 1): 96}
+SCALAR_COLUMNS = {(2, 1): 96, (4, 1): 96, (6, 1): 96, (7, 1): 32}
 EARLY = 4
 X_CUTS = ((0, 1024), (1024, 256))
 OUT_CUTS = ((0, 512), (512, 512), (1024, 256))
@@ -157,7 +160,7 @@ def tile_moe_shr_mlp_silu_kernel(tc, xT, w1, w2, gate, offs, out):
 
         def step(e):
             if e not in steps:
-                words = STEP_WORDS if e in (2, 4, 6) else PASSES * H
+                words = STEP_WORDS if e in (2, 4, 6, "tail") else PASSES * H
                 values = tile("values", PACK * words, BF16, tag=value_tags[e])
                 if e == "shared":
                     steps[e] = (values, tile("shared_codes", words, U32), tile("shared_scales", words, U8))
@@ -166,15 +169,17 @@ def tile_moe_shr_mlp_silu_kernel(tc, xT, w1, w2, gate, offs, out):
             return steps[e]
 
         def w1_at(e):
-            return AT_W1 if e in (2, 4, 6) else 0
+            return {2: AT_W1, 4: AT_W1, 6: N + C}.get(e, 0)
 
         def hidden_at(e):
-            return ("tail", (e - 6) * (C + N)) if e >= 6 else (e + 2 - e % 2, AT_H + e % 2 * C)
+            if e >= 5:
+                return ("tail", (e - 5) * (C + N))
+            return (6, N) if e == 4 else (e + 2 - e % 2, AT_H + e % 2 * C)
 
         def w2_at(e):
-            if e == SHARED:
-                return ("tail", 2 * (C + N))
-            return ("tail", (e - 6) * (C + N) + C) if e >= 6 else (e + 2 - e % 2, AT_W2 + e % 2 * N)
+            if e >= 5:
+                return ("tail", (e - 5) * (C + N) + (C if e < SHARED else 0))
+            return (e + 2 - e % 2, AT_W2 + e % 2 * N)
 
         def words_of(place, at, count):
             return step(place)[0][:, PACK * at : PACK * (at + count)]
@@ -271,7 +276,9 @@ def tile_moe_shr_mlp_silu_kernel(tc, xT, w1, w2, gate, offs, out):
             )
 
         def scatter(e, b, engine):
-            first, last = PIECES[e]
+            if e not in PIECES[b]:
+                return
+            first, last = PIECES[b][e]
             window = routed[b][:].indirect(offsets[:, first // 16 : last // 16])
             if engine == "vector":
                 on_vector(out=window, in_=y_of(slice(first, last))[:, b])
@@ -337,19 +344,29 @@ def tile_moe_shr_mlp_silu_kernel(tc, xT, w1, w2, gate, offs, out):
             routed_first(e, 1, range(PACK), bank)
             silu(words_of(*hidden_at(e), C), bank)
 
-        for e in range(1, LAST - 1, 2):
-            if e < LAST - 2:
-                cast_w2(e - 1, 2, load_w2(e - 1, 2), on_vector if e == 1 else on_scalar)
+        for e in (1, 3):
+            cast_w2(e - 1, 2, load_w2(e - 1, 2), on_vector if e == 1 else on_scalar)
             plain_step(e)
-            if e == LAST - 2:
-                pair = load_w2(e - 1, 2)
-                cast_w2(e - 1, 1, pair[:, 0:1], on_scalar)
-                cast_w2(e, 1, pair[:, 1:2], on_vector)
-            if e == 1:
-                quantize_shared(e, OUT_CUTS[0:1], hs_values[0])
-            if e == 3:
-                quantize_shared(e, OUT_CUTS[1:], hs_values[1])
+            quantize_shared(e, OUT_CUTS[0:1] if e == 1 else OUT_CUTS[1:], hs_values[e // 2])
             step_with_way_back(e + 1)
+        plain_step(5)
+        cast_w2(4, 1, load_w2(4, 1), on_scalar)
+        loaded = load_w1(6, 2)
+        bank = bank_tile("first")
+        for c in range(PASSES):
+            cast_w1(6, c, loaded, SCALAR_COLUMNS.get((6, c), 0))
+        quantize_words(6, 0, H)
+        second = bank_tile("second")
+        second_layer(4, second, range(BLOCKS))
+        routed_first(6, 0, (0,), bank)
+        quantize_words(6, H, w1_at(6) + H)
+        routed_first(6, 0, (1, 2, 3), bank)
+        times_gate(4, 1, slice(0, BLOCKS), second)
+        for b in range(BLOCKS):
+            scatter(4, b, "scalar")
+        quantize_words(6, w1_at(6) + H, w1_at(6) + 2 * H)
+        routed_first(6, 1, range(PACK), bank)
+        silu(words_of(*hidden_at(6), C), bank)
 
         loaded = load_w1(LAST, 2)
         bank = bank_tile("first")
@@ -360,26 +377,22 @@ def tile_moe_shr_mlp_silu_kernel(tc, xT, w1, w2, gate, offs, out):
         for half in range(2):
             quantize_words(LAST, H + half * 2 * P, H + (half + 1) * 2 * P)
             routed_first(LAST, 1, (2 * half, 2 * half + 1), bank)
-        places = load_tile()[:, 0 : 3 * PACK * N].rearrange("p (e x) -> p e x", e=3)
-        for e in range(3):
-            nc.sync.dma_start(out=places[:, e], in_=w2[LAST - 1 + e].rearrange("(p j) w -> p (j w)", j=PACK))
-        cast_w2(LAST - 1, 1, places[:, 0:1], on_scalar)
+        places = load_tile()[:].rearrange("p (e x) -> p e x", e=4)
+        for i in range(4):
+            nc.sync.dma_start(out=places[:, i], in_=w2[5 + i].rearrange("(p j) w -> p (j w)", j=PACK))
+        cast_w2(5, 1, places[:, 0:1], on_scalar)
         silu(words_of(*hidden_at(LAST), C), bank)
-        cast_w2(LAST, 1, places[:, 1:2], on_vector)
-        quantize_words("tail", 0, C + N)
-        second = bank_tile("second")
-        second_layer(LAST - 1, second, range(BLOCKS))
-        times_gate(LAST - 1, 1, slice(0, BLOCKS), second)
-        scatter(LAST - 1, 0, "scalar")
-        quantize_words("tail", C + N, 2 * (C + N))
-        second = bank_tile("second")
-        second_layer(LAST, second, range(BLOCKS))
-        cast_w2(SHARED, 1, places[:, 2:3], on_vector)
-        scatter(LAST - 1, 1, "scalar")
-        times_gate(LAST, 1, slice(0, BLOCKS), second)
-        quantize_words("tail", 2 * (C + N), 2 * (C + N) + N)
-        scatter(LAST, 0, "vector")
-        scatter(LAST, 1, "scalar")
+        for e in (5, 6, 7):
+            at = hidden_at(e)[1]
+            quantize_words("tail", at, at + C + N)
+            second = bank_tile("second")
+            second_layer(e, second, range(BLOCKS))
+            cast_w2(e + 1, 1, places[:, e - 4 : e - 3], on_vector)
+            times_gate(e, 1, slice(0, BLOCKS), second)
+            if e == LAST:
+                quantize_words("tail", w2_at(SHARED)[1], w2_at(SHARED)[1] + N)
+            for b in range(BLOCKS):
+                scatter(e, b, "vector" if (e, b) == (LAST, 0) else "scalar")
 
         w_codes, w_scales = step("tail")[1:]
         wide = [bank_tile("shared"), bank_tile("shared"), bank_tile("shared"), bank_tile("first")]

@@ -160,7 +160,7 @@ def tile_moe_shr_mlp_silu_kernel(tc, xT, w1, w2, gate, offs, out):
 
         def step(e):
             if e not in steps:
-                words = STEP_WORDS if e in (2, 4, 6, "tail") else PASSES * H
+                words = STEP_WORDS if e in (2, 4, 6, "tail") else PASSES * H + (C if e == LAST else 0)
                 values = tile("values", PACK * words, BF16, tag=value_tags[e])
                 if e == "shared":
                     steps[e] = (values, tile("shared_codes", words, U32), tile("shared_scales", words, U8))
@@ -168,17 +168,16 @@ def tile_moe_shr_mlp_silu_kernel(tc, xT, w1, w2, gate, offs, out):
                     steps[e] = (values, tile("codes", words, U32, bufs=3), tile("scales", words, U8, bufs=3))
             return steps[e]
 
-        def w1_at(e):
-            return {2: AT_W1, 4: AT_W1, 6: N + C}.get(e, 0)
+        def w1_at(e, c):
+            return {2: AT_W1, 4: AT_W1, 6: N + C, LAST: c * C}.get(e, 0) + c * H
 
         def hidden_at(e):
-            if e >= 5:
-                return ("tail", (e - 5) * (C + N))
-            return (6, N) if e == 4 else (e + 2 - e % 2, AT_H + e % 2 * C)
+            late = {4: (6, N), 5: ("tail", 0), 6: (LAST, H), LAST: ("tail", C + 2 * N)}
+            return late.get(e, (e + 2 - e % 2, AT_H + e % 2 * C))
 
         def w2_at(e):
             if e >= 5:
-                return ("tail", (e - 5) * (C + N) + (C if e < SHARED else 0))
+                return ("tail", C + (e - 5) * N + (C if e >= LAST else 0))
             return (e + 2 - e % 2, AT_W2 + e % 2 * N)
 
         def words_of(place, at, count):
@@ -199,7 +198,7 @@ def tile_moe_shr_mlp_silu_kernel(tc, xT, w1, w2, gate, offs, out):
             return places
 
         def cast_w1(e, c, loaded, helped):
-            dst = words_of(e, w1_at(e) + c * H, H).rearrange("p (t m a b) -> p m a t b", t=PACK, a=2, b=2)
+            dst = words_of(e, w1_at(e, c), H).rearrange("p (t m a b) -> p m a t b", t=PACK, a=2, b=2)
             src = loaded[:, c].rearrange("p (a b m t) -> p m a t b", t=PACK, a=2, b=2)
             if helped:
                 on_scalar(out=dst[:, 0:helped], in_=src[:, 0:helped])
@@ -232,7 +231,7 @@ def tile_moe_shr_mlp_silu_kernel(tc, xT, w1, w2, gate, offs, out):
         def first_layer(e, c, quarters, bank, codes, scales, first):
             w_codes, w_scales = step(e)[1:]
             for t in quarters:
-                rows = slice(w1_at(e) + c * H + t * P, w1_at(e) + c * H + (t + 1) * P)
+                rows = slice(w1_at(e, c) + t * P, w1_at(e, c) + (t + 1) * P)
                 multiply(
                     bank[:, t * C : (t + 1) * C],
                     w_codes[:, rows],
@@ -251,14 +250,21 @@ def tile_moe_shr_mlp_silu_kernel(tc, xT, w1, w2, gate, offs, out):
                 place.rearrange("p (n t) -> p n t", t=PACK), bank[:].rearrange("p (t n) -> p n t", t=PACK), SILU
             )
 
+        def second_product(e, b, place):
+            h_step, h_at = hidden_at(e)
+            w_step, w_at = w2_at(e)
+            rows, slots = slice(w_at + b * P, w_at + (b + 1) * P), slice(h_at, h_at + C)
+            w_codes, w_scales = step(w_step)[1:]
+            codes, scales = step(h_step)[1:]
+            multiply(place, w_codes[:, rows], w_scales[:, rows], codes[:, slots], scales[:, slots])
+
         def second_layer(e, bank, blocks):
-            place, at = hidden_at(e)
-            codes, scales = step(place)[1:]
-            slots = slice(at, at + C)
             for b in blocks:
-                rows = slice(w2_at(e)[1] + b * P, w2_at(e)[1] + (b + 1) * P)
-                cols = slice((e % 2 * BLOCKS + b) * C, (e % 2 * BLOCKS + b + 1) * C)
-                multiply(bank[:, cols], codes[:, rows], scales[:, rows], codes[:, slots], scales[:, slots])
+                second_product(e, b, bank[:, (e % 2 * BLOCKS + b) * C : (e % 2 * BLOCKS + b + 1) * C])
+
+        def block_times_gate(first, count, b, place):
+            slots = slice(first * C, (first + count) * C)
+            nc.vector.tensor_tensor(y_of(slots)[:, b], place, gates[:, slots], MULT)
 
         def y_of(slots):
             return y[:, :, slots]
@@ -316,7 +322,7 @@ def tile_moe_shr_mlp_silu_kernel(tc, xT, w1, w2, gate, offs, out):
                 quantize(hs_codes[start], hs_scales[:, start : start + width], values[:, PACK * at : PACK * (at + width)])
 
         def plain_step(e):
-            loaded = load_w1(e, 2 if e == 5 else 1)
+            loaded = load_w1(e, 1 if e == 1 else 2)
             bank = bank_tile("first")
             for c in range(PASSES):
                 cast_w1(e, c, loaded, 0)
@@ -359,12 +365,12 @@ def tile_moe_shr_mlp_silu_kernel(tc, xT, w1, w2, gate, offs, out):
         second = bank_tile("second")
         second_layer(4, second, range(BLOCKS))
         routed_first(6, 0, (0,), bank)
-        quantize_words(6, H, w1_at(6) + H)
+        quantize_words(6, H, w1_at(6, 1))
         routed_first(6, 0, (1, 2, 3), bank)
         times_gate(4, 1, slice(0, BLOCKS), second)
         for b in range(BLOCKS):
             scatter(4, b, "scalar")
-        quantize_words(6, w1_at(6) + H, w1_at(6) + 2 * H)
+        quantize_words(6, w1_at(6, 1), w1_at(6, 1) + H)
         routed_first(6, 1, range(PACK), bank)
         silu(words_of(*hidden_at(6), C), bank)
 
@@ -374,25 +380,42 @@ def tile_moe_shr_mlp_silu_kernel(tc, xT, w1, w2, gate, offs, out):
         quantize_words(LAST, 0, H)
         routed_first(LAST, 0, range(PACK), bank)
         cast_w1(LAST, 1, loaded, SCALAR_COLUMNS.get((LAST, 1), 0))
-        for half in range(2):
-            quantize_words(LAST, H + half * 2 * P, H + (half + 1) * 2 * P)
-            routed_first(LAST, 1, (2 * half, 2 * half + 1), bank)
+        quantize_words(LAST, H, w1_at(LAST, 1) + 2 * P)
+        routed_first(LAST, 1, (0, 1), bank)
+        quantize_words(LAST, w1_at(LAST, 1) + 2 * P, w1_at(LAST, 1) + H)
+        routed_first(LAST, 1, (2, 3), bank)
         places = load_tile()[:].rearrange("p (e x) -> p e x", e=4)
         for i in range(4):
             nc.sync.dma_start(out=places[:, i], in_=w2[5 + i].rearrange("(p j) w -> p (j w)", j=PACK))
-        cast_w2(5, 1, places[:, 0:1], on_scalar)
+        for b in range(BLOCKS):
+            on_scalar(
+                out=words_of("tail", w2_at(5)[1] + b * P, P).rearrange("p (g i t) -> p g t i", i=4, t=PACK),
+                in_=places[:, 0].rearrange("p (t b g i) -> p b g t i", b=BLOCKS, i=4, t=PACK)[:, b],
+            )
         silu(words_of(*hidden_at(LAST), C), bank)
-        for e in (5, 6, 7):
-            at = hidden_at(e)[1]
-            quantize_words("tail", at, at + C + N)
-            second = bank_tile("second")
-            second_layer(e, second, range(BLOCKS))
-            cast_w2(e + 1, 1, places[:, e - 4 : e - 3], on_vector)
-            times_gate(e, 1, slice(0, BLOCKS), second)
-            if e == LAST:
-                quantize_words("tail", w2_at(SHARED)[1], w2_at(SHARED)[1] + N)
-            for b in range(BLOCKS):
-                scatter(e, b, "vector" if (e, b) == (LAST, 0) else "scalar")
+        quantize_words("tail", 0, C + P)
+        second = bank_tile("second")
+        second_product(5, 0, second[:, 0:C])
+        cast_w2(6, 1, places[:, 1:2], on_vector)
+        block_times_gate(5, 1, 0, second[:, 0:C])
+        scatter(5, 0, "scalar")
+        quantize_words("tail", C + P, C + 2 * N)
+        second = bank_tile("second")
+        for i, (e, b) in enumerate(((6, 0), (5, 1), (6, 1))):
+            second_product(e, b, second[:, i * C : (i + 1) * C])
+        cast_w2(LAST, 1, places[:, 2:3], on_vector)
+        block_times_gate(6, 1, 0, second[:, 0:C])
+        block_times_gate(5, 2, 1, second[:, C : 3 * C])
+        for b in range(BLOCKS):
+            scatter(6, b, "scalar")
+        quantize_words("tail", C + 2 * N, 2 * C + 3 * N)
+        second = bank_tile("second")
+        second_layer(LAST, second, range(BLOCKS))
+        cast_w2(SHARED, 1, places[:, 3:4], on_vector)
+        times_gate(LAST, 1, slice(0, BLOCKS), second)
+        quantize_words("tail", w2_at(SHARED)[1], w2_at(SHARED)[1] + N)
+        scatter(LAST, 0, "vector")
+        scatter(LAST, 1, "scalar")
 
         w_codes, w_scales = step("tail")[1:]
         wide = [bank_tile("shared"), bank_tile("shared"), bank_tile("shared"), bank_tile("first")]

@@ -39,6 +39,7 @@ PIECES = (
 AT_W2, AT_H, AT_W1, STEP_WORDS = 0, 2 * N, 2 * N + 2 * C, 2 * N + 2 * C + PASSES * H
 SCALAR_COLUMNS = {(2, 1): 96, (4, 1): 96, (6, 1): 96, (7, 1): 32}
 EARLY = 4
+WOVEN = (3, 5)
 X_CUTS = ((0, 1024), (1024, 256))
 OUT_CUTS = ((0, 512), (512, 512), (1024, 256))
 
@@ -198,7 +199,10 @@ def tile_moe_shr_mlp_silu_kernel(tc, xT, w1, w2, gate, offs, out):
             return places
 
         def cast_w1(e, c, loaded, helped):
-            dst = words_of(e, w1_at(e, c), H).rearrange("p (t m a b) -> p m a t b", t=PACK, a=2, b=2)
+            if e in WOVEN:
+                dst = words_of(e, 0, PASSES * H).rearrange("p (t c m a b) -> p c m a t b", t=PACK, c=PASSES, a=2, b=2)[:, c]
+            else:
+                dst = words_of(e, w1_at(e, c), H).rearrange("p (t m a b) -> p m a t b", t=PACK, a=2, b=2)
             src = loaded[:, c].rearrange("p (a b m t) -> p m a t b", t=PACK, a=2, b=2)
             if helped:
                 on_scalar(out=dst[:, 0:helped], in_=src[:, 0:helped])
@@ -231,7 +235,8 @@ def tile_moe_shr_mlp_silu_kernel(tc, xT, w1, w2, gate, offs, out):
         def first_layer(e, c, quarters, bank, codes, scales, first):
             w_codes, w_scales = step(e)[1:]
             for t in quarters:
-                rows = slice(w1_at(e, c) + t * P, w1_at(e, c) + (t + 1) * P)
+                at = (PASSES * t + c) * P if e in WOVEN else w1_at(e, c) + t * P
+                rows = slice(at, at + P)
                 multiply(
                     bank[:, t * C : (t + 1) * C],
                     w_codes[:, rows],
@@ -326,9 +331,14 @@ def tile_moe_shr_mlp_silu_kernel(tc, xT, w1, w2, gate, offs, out):
             bank = bank_tile("first")
             for c in range(PASSES):
                 cast_w1(e, c, loaded, 0)
-            for c in range(PASSES):
-                quantize_words(e, c * H, (c + 1) * H)
-                routed_first(e, c, range(PACK), bank)
+            for half in range(2):
+                quantize_words(e, half * H, (half + 1) * H)
+                if e in WOVEN:
+                    for t in (2 * half, 2 * half + 1):
+                        for c in range(PASSES):
+                            routed_first(e, c, (t,), bank)
+                else:
+                    routed_first(e, half, range(PACK), bank)
             silu(words_of(*hidden_at(e), C), bank)
 
         def step_with_way_back(e):

from contextlib import ExitStack

import concourse.mybir as mybir
from concourse.masks import make_identity

FLOPS = 3019898880

K, T, E, C, H, N = 1024, 1280, 8, 128, 512, 256
S = E * C
SHARED = E
LAST = E - 1

F32 = mybir.dt.float32
BF16 = mybir.dt.bfloat16
U32 = mybir.dt.uint32
U16 = mybir.dt.uint16
U8 = mybir.dt.uint8
FP8X4 = mybir.dt.float8_e4m3fn_x4
COPY = mybir.ActivationFunctionType.Copy
SILU = mybir.ActivationFunctionType.Silu
MULT = mybir.AluOpType.mult
ADD = mybir.AluOpType.add

P = 128
PACK = 4
PASS = P * PACK
PASSES = K // PASS
BANK = 512
BLOCKS = N // P
WINDOW = 1408
LOAD_BUFS = 6
FIRST_SHARE = 104
VECTOR_TOKENS = {(0, 1): 176}
SCALAR_JOINS = (320, 160)
PIECES = (
    {1: (0, 224), 3: (224, 384), 4: (384, 544), 5: (544, 704), 6: (704, 864), 7: (864, 1024)},
    {1: (0, 256), 3: (256, 480), 4: (480, 640), 6: (640, 864), 7: (864, 1024)},
)
AT_W2, AT_H, AT_W1, STEP_WORDS = 0, 2 * N, 2 * N + 2 * C, 2 * N + 2 * C + PASSES * H
SCALAR_COLUMNS = {(2, 1): 96, (4, 1): 96, (6, 1): 96, (7, 1): 32}
EARLY = 4
WOVEN = (3, 5)
X_CUTS = ((0, 1024), (1024, 256))
OUT_CUTS = ((0, 512), (512, 512), (1024, 256))


def tile_moe_shr_mlp_silu_kernel(tc, xT, w1, w2, gate, offs, out):
    nc = tc.nc
    on_vector, on_scalar = nc.vector.tensor_copy, nc.scalar.copy
    with ExitStack() as ctx:
        lists = ctx.enter_context(tc.tile_pool(name="lists", bufs=1))
        held = ctx.enter_context(tc.tile_pool(name="held", bufs=1))
        ring = ctx.enter_context(tc.tile_pool(name="ring", bufs=1))
        psum = ctx.enter_context(tc.psum_pool(name="psum", bufs=1))

        def tile(name, width, dtype, tag=None, bufs=1):
            pool = held if bufs == 1 else ring
            return pool.tile([P, width], dtype, name=name, tag=tag or name, bufs=bufs, align_bytes=64)

        def load_tile():
            return tile("load", PASSES * PACK * H, F32, bufs=LOAD_BUFS)

        def bank_tile(tag):
            return psum.tile([P, BANK], F32, name=tag, tag=tag, bufs={"first": 3, "shared": 3, "second": 2}[tag])

        offsets = lists.tile([P, S // 16], U16, name="offsets")

        zero = held.tile([P, 1], F32, name="zero")
        zero_out = held.tile([P, 1], F32, name="zero_out")
        nc.vector.memset(zero[:], 0.0)
        nc.scalar.activation(zero_out[:], zero[:], SILU)

        identity = held.tile([P, P], F32, name="identity")
        make_identity(nc, identity[:])

        routed = []
        for b in range(BLOCKS):
            window = tile(f"routed{b}", T, F32)
            (nc.gpsimd if b else nc.vector).memset(window[:], 0.0)
            routed.append(window)

        gates = tile("gates", S, F32)
        gate_columns = held.tile([P, E], F32, name="gate_columns")

        def spread_gates():
            nc.sync.dma_start(out=gate_columns[:], in_=gate[0].rearrange("(n j) -> n j", j=E))
            for half in range(2):
                bank = bank_tile("shared")
                for j in range(4):
                    column = gate_columns[:, 4 * half + j : 4 * half + j + 1].to_broadcast([P, P])
                    nc.tensor.transpose(bank[:, j * P : (j + 1) * P], column, identity[:])
                nc.scalar.copy(
                    out=gates[:].rearrange("p (n h j) -> p h n j", h=2, j=4)[:, half],
                    in_=bank[:].rearrange("p (j n) -> p n j", j=4),
                )

        x_codes = tile("x_codes", PASSES * T, U32)
        x_scales = tile("x_scales", PASSES * T, U8)
        pairs = [tile(f"pairs{c}", PACK * STEP_WORDS, BF16) for c in range(PASSES)]
        for part in pairs:
            nc.vector.memset(part[:, 0 : PACK * WINDOW].rearrange("p (u w) -> p u w", u=2)[:, :, 2 * T : 2 * WINDOW], 0.0)
        slot_codes = tile("slot_codes", PASSES * S, U32)
        slot_scales = tile("slot_scales", PASSES * S, U8)

        def quantize(codes, scales, values):
            nc.vector.quantize_mx(out=codes.bitcast(FP8X4), scales=scales, in_=values)

        def load_x(c, u, parts):
            rows = xT[c * PASS : (c + 1) * PASS, :].rearrange("(p u e) w -> u p e w", u=2, e=2)[u]
            places = load_tile()[:, 0 : 2 * T].rearrange("p (h e w) -> p h e w", h=parts, e=2)
            width = T // parts
            for h in range(parts):
                nc.sync.dma_start(out=places[:, h], in_=rows[:, :, h * width : (h + 1) * width])
            return [places[:, h] for h in range(parts)]

        def pair_x(c, u, parts):
            tokens = pairs[c][:, u * 2 * WINDOW : u * 2 * WINDOW + 2 * T].rearrange("p (g i e) -> p g e i", i=4, e=2)
            groups = T // 4 // len(parts)
            share = FIRST_SHARE if len(parts) > 1 else VECTOR_TOKENS.get((c, u), 0)
            for h, place in enumerate(parts):
                dst = tokens[:, h * groups : (h + 1) * groups]
                src = place.rearrange("p e (g i) -> p g e i", i=4)
                if share > 0:
                    on_vector(out=dst[:, 0:share], in_=src[:, 0:share])
                on_scalar(out=dst[:, share:groups], in_=src[:, share:groups])

        def gather(c, u, gathered):
            window = pairs[c][:, u * 2 * WINDOW : (u + 1) * 2 * WINDOW].bitcast(U32)
            on_vector(out=gathered[:, u * S : (u + 1) * S], in_=window.indirect(offsets[:]))

        def join_pairs(name, words, width, helped):
            joined = tile(name, PACK * width, BF16)
            dst = joined[:].bitcast(F32).rearrange("p (g i u) -> p g u i", i=4, u=2)
            src = words.bitcast(F32).rearrange("p (u w) -> p u w", u=2)[:, :, 0:width].rearrange("p u (g i) -> p g u i", i=4)
            if helped < width // 4:
                on_vector(out=dst[:, helped:], in_=src[:, helped:])
            if helped:
                on_scalar(out=dst[:, 0:helped], in_=src[:, 0:helped])
            return joined

        x_tiles = {(0, 0): load_x(0, 0, 2)}
        spread_gates()
        nc.sync.dma_start(offsets[:], offs)
        for c, u in ((0, 1), (1, 0), (1, 1)):
            x_tiles[c, u] = load_x(c, u, 1)
        for c in range(PASSES):
            gathered = tile("gathered", 2 * S, U32)
            for u in range(2):
                pair_x(c, u, x_tiles[c, u])
                gather(c, u, gathered)
            token_values = join_pairs("token_values", pairs[c][:, 0 : PACK * WINDOW], T, SCALAR_JOINS[c])
            slot_values = join_pairs("slot_values", gathered[:], S, 0)
            quantize(slot_codes[:, c * S : (c + 1) * S], slot_scales[:, c * S : (c + 1) * S], slot_values[:])
            for start, width in X_CUTS:
                cols = slice(c * T + start, c * T + start + width)
                quantize(x_codes[:, cols], x_scales[:, cols], token_values[:, PACK * start : PACK * (start + width)])

        value_tags = {0: "gathered", 1: "slot_values", 2: "pairs0", 3: "gathered", 4: "pairs1", 5: "shared_values",
                      6: "pairs0", 7: "shared_values", "shared": "shared_values", "tail": "pairs1"}
        steps = {}

        def step(e):
            if e not in steps:
                words = STEP_WORDS if e in (2, 4, 6, "tail") else PASSES * H + (C if e == LAST else 0)
                values = tile("values", PACK * words, BF16, tag=value_tags[e])
                if e == "shared":
                    steps[e] = (values, tile("shared_codes", words, U32), tile("shared_scales", words, U8))
                else:
                    steps[e] = (values, tile("codes", words, U32, bufs=3), tile("scales", words, U8, bufs=3))
            return steps[e]

        def w1_at(e, c):
            return {2: AT_W1, 4: AT_W1, 6: N + C, LAST: c * C}.get(e, 0) + c * H

        def hidden_at(e):
            late = {4: (6, N), 5: ("tail", 0), 6: (LAST, H), LAST: ("tail", C + 2 * N)}
            return late.get(e, (e + 2 - e % 2, AT_H + e % 2 * C))

        def w2_at(e):
            if e >= 5:
                return ("tail", C + (e - 5) * N + (C if e >= LAST else 0))
            return (e + 2 - e % 2, AT_W2 + e % 2 * N)

        def words_of(place, at, count):
            return step(place)[0][:, PACK * at : PACK * (at + count)]

        def quantize_words(e, first, last):
            values, codes, scales = step(e)
            quantize(codes[:, first:last], scales[:, first:last], values[:, PACK * first : PACK * last])

        def load_w1(e, parts):
            places = load_tile()[:].rearrange("p (c x) -> p c x", c=PASSES)
            source = w1[SHARED if e == "shared" else e].rearrange("(c p j) w -> p c (j w)", c=PASSES, j=PACK)
            if parts == 1:
                nc.sync.dma_start(out=places, in_=source)
            else:
                for c in range(PASSES):
                    nc.sync.dma_start(out=places[:, c], in_=source[:, c])
            return places

        def cast_w1(e, c, loaded, helped):
            if e in WOVEN:
                dst = words_of(e, 0, PASSES * H).rearrange("p (t c m a b) -> p c m a t b", t=PACK, c=PASSES, a=2, b=2)[:, c]
            else:
                dst = words_of(e, w1_at(e, c), H).rearrange("p (t m a b) -> p m a t b", t=PACK, a=2, b=2)
            src = loaded[:, c].rearrange("p (a b m t) -> p m a t b", t=PACK, a=2, b=2)
            if helped:
                on_scalar(out=dst[:, 0:helped], in_=src[:, 0:helped])
            if helped < P:
                on_vector(out=dst[:, helped:P], in_=src[:, helped:P])

        def load_w2(first, count):
            places = load_tile()[:, 0 : count * PACK * N].rearrange("p (e x) -> p e x", e=count)
            nc.sync.dma_start(out=places, in_=w2[first : first + count].rearrange("e (p j) w -> p e (j w)", j=PACK))
            return places

        def cast_w2(first, count, loaded, copy):
            values = words_of(*w2_at(first), count * N)
            copy(
                out=values.rearrange("p (e g i t) -> p e g t i", e=count, i=4, t=PACK),
                in_=loaded.rearrange("p e (t g i) -> p e g t i", i=4, t=PACK),
            )

        def multiply(bank, w_codes, w_scales, codes, scales, start=True, stop=True):
            nc.tensor.matmul_mx(
                out=bank,
                lhsT=w_codes.bitcast(FP8X4),
                lhsT_scale=w_scales,
                rhs=codes.bitcast(FP8X4),
                rhs_scale=scales,
                start=start,
                stop=stop,
            )

        def first_layer(e, c, quarters, bank, codes, scales, first):
            w_codes, w_scales = step(e)[1:]
            for t in quarters:
                at = (PASSES * t + c) * P if e in WOVEN else w1_at(e, c) + t * P
                rows = slice(at, at + P)
                multiply(
                    bank[:, t * C : (t + 1) * C],
                    w_codes[:, rows],
                    w_scales[:, rows],
                    codes[:, first : first + C],
                    scales[:, first : first + C],
                    start=((c, t) == (0, 0)),
                    stop=((c, t) == (PASSES - 1, PACK - 1)),
                )

        def routed_first(e, c, quarters, bank):
            first_layer(e, c, quarters, bank, slot_codes, slot_scales, c * S + e * C)

        def silu(place, bank):
            nc.scalar.activation(
                place.rearrange("p (n t) -> p n t", t=PACK), bank[:].rearrange("p (t n) -> p n t", t=PACK), SILU
            )

        def second_product(e, b, place):
            h_step, h_at = hidden_at(e)
            w_step, w_at = w2_at(e)
            rows, slots = slice(w_at + b * P, w_at + (b + 1) * P), slice(h_at, h_at + C)
            w_codes, w_scales = step(w_step)[1:]
            codes, scales = step(h_step)[1:]
            multiply(place, w_codes[:, rows], w_scales[:, rows], codes[:, slots], scales[:, slots])

        def second_layer(e, bank, blocks):
            for b in blocks:
                second_product(e, b, bank[:, (e % 2 * BLOCKS + b) * C : (e % 2 * BLOCKS + b + 1) * C])

        def block_times_gate(first, count, b, place):
            slots = slice(first * C, (first + count) * C)
            nc.vector.tensor_tensor(y_of(slots)[:, b], place, gates[:, slots], MULT)

        def y_of(slots):
            return y[:, :, slots]

        def times_gate(first, count, blocks, bank):
            slots = slice(first * C, (first + count) * C)
            experts = slice(first % 2, first % 2 + count)
            nc.vector.tensor_tensor(
                y_of(slots)[:, blocks].rearrange("p b (e n) -> p e b n", e=count),
                bank[:].rearrange("p (e b n) -> p e b n", e=2, b=BLOCKS)[:, experts, blocks],
                gates[:, slots].rearrange("p (e o n) -> p e o n", e=count, o=1).to_broadcast(
                    [P, count, blocks.stop - blocks.start, C]
                ),
                MULT,
            )

        def scatter(e, b, engine):
            if e not in PIECES[b]:
                return
            first, last = PIECES[b][e]
            window = routed[b][:].indirect(offsets[:, first // 16 : last // 16])
            if engine == "vector":
                on_vector(out=window, in_=y_of(slice(first, last))[:, b])
            else:
                nc.scalar.activation(window, y_of(slice(first, last))[:, b], COPY)

        loaded = load_w1("shared", 2)
        for c in range(PASSES):
            cast_w1("shared", c, loaded, P)
            quantize_words("shared", c * H, (c + 1) * H)
        loaded = load_w1(0, 1)
        first_bank = bank_tile("first")
        for c in range(PASSES):
            cast_w1(0, c, loaded, P)
            quantize_words(0, c * H, (c + 1) * H)
        hs_values = [loaded[:, 1].bitcast(BF16)[:, 0 : EARLY * H], tile("hs_values", PACK * T - EARLY * H, BF16, tag="token_values")[:]]
        for group in range(T // C):
            bank = bank_tile("shared")
            for c in range(PASSES):
                first_layer("shared", c, range(PACK), bank, x_codes, x_scales, c * T + group * C)
            late = int(group >= EARLY)
            silu(hs_values[late][:, (group - late * EARLY) * H : (group - late * EARLY + 1) * H], bank)
        for c in range(PASSES):
            routed_first(0, c, range(PACK), first_bank)
        silu(words_of(*hidden_at(0), C), first_bank)
        y = tile("y", BLOCKS * S, F32, tag="x_codes")[:].rearrange("p (b s) -> p b s", b=BLOCKS)
        hs_scales = tile("hs_scales", T, U8)
        hs_codes = {}

        def quantize_shared(e, cuts, values):
            codes = tile("hs_codes", T, U32, tag=value_tags[e])
            for start, width in cuts:
                hs_codes[start] = codes[:, start : start + width]
                at = start - cuts[0][0]
                quantize(hs_codes[start], hs_scales[:, start : start + width], values[:, PACK * at : PACK * (at + width)])

        def plain_step(e):
            loaded = load_w1(e, 1 if e == 1 else 2)
            bank = bank_tile("first")
            for c in range(PASSES):
                cast_w1(e, c, loaded, 0)
            for half in range(2):
                quantize_words(e, half * H, (half + 1) * H)
                if e in WOVEN:
                    for t in (2 * half, 2 * half + 1):
                        for c in range(PASSES):
                            routed_first(e, c, (t,), bank)
                else:
                    routed_first(e, half, range(PACK), bank)
            silu(words_of(*hidden_at(e), C), bank)

        def step_with_way_back(e):
            loaded = load_w1(e, 1 if e == 2 else 2)
            bank = bank_tile("first")
            for c in range(PASSES):
                cast_w1(e, c, loaded, SCALAR_COLUMNS.get((e, c), 0))
            quantize_words(e, 0, 2 * H)
            second = bank_tile("second")
            for before in (e - 2, e - 1):
                second_layer(before, second, range(BLOCKS))
            routed_first(e, 0, (0, 1), bank)
            quantize_words(e, 2 * H, AT_W1 + H)
            routed_first(e, 0, (2, 3), bank)
            times_gate(e - 2, 2, slice(0, BLOCKS), second)
            for b in range(BLOCKS):
                scatter(e - 1, b, "scalar")
            quantize_words(e, AT_W1 + H, STEP_WORDS)
            routed_first(e, 1, range(PACK), bank)
            silu(words_of(*hidden_at(e), C), bank)

        for e in (1, 3):
            cast_w2(e - 1, 2, load_w2(e - 1, 2), on_vector if e == 1 else on_scalar)
            plain_step(e)
            quantize_shared(e, OUT_CUTS[0:1] if e == 1 else OUT_CUTS[1:], hs_values[e // 2])
            step_with_way_back(e + 1)
        plain_step(5)
        cast_w2(4, 1, load_w2(4, 1), on_scalar)
        loaded = load_w1(6, 2)
        bank = bank_tile("first")
        for c in range(PASSES):
            cast_w1(6, c, loaded, SCALAR_COLUMNS.get((6, c), 0))
        quantize_words(6, 0, H)
        second = bank_tile("second")
        second_layer(4, second, range(BLOCKS))
        routed_first(6, 0, (0,), bank)
        quantize_words(6, H, w1_at(6, 1))
        routed_first(6, 0, (1, 2, 3), bank)
        times_gate(4, 1, slice(0, BLOCKS), second)
        for b in range(BLOCKS):
            scatter(4, b, "scalar")
        quantize_words(6, w1_at(6, 1), w1_at(6, 1) + H)
        routed_first(6, 1, range(PACK), bank)
        silu(words_of(*hidden_at(6), C), bank)

        loaded = load_w1(LAST, 2)
        bank = bank_tile("first")
        cast_w1(LAST, 0, loaded, 0)
        quantize_words(LAST, 0, H)
        routed_first(LAST, 0, range(PACK), bank)
        cast_w1(LAST, 1, loaded, SCALAR_COLUMNS.get((LAST, 1), 0))
        quantize_words(LAST, H, w1_at(LAST, 1) + 2 * P)
        routed_first(LAST, 1, (0, 1), bank)
        quantize_words(LAST, w1_at(LAST, 1) + 2 * P, w1_at(LAST, 1) + H)
        routed_first(LAST, 1, (2, 3), bank)
        places = load_tile()[:].rearrange("p (e x) -> p e x", e=4)
        for i in range(4):
            nc.sync.dma_start(out=places[:, i], in_=w2[5 + i].rearrange("(p j) w -> p (j w)", j=PACK))
        for b in range(BLOCKS):
            on_scalar(
                out=words_of("tail", w2_at(5)[1] + b * P, P).rearrange("p (g i t) -> p g t i", i=4, t=PACK),
                in_=places[:, 0].rearrange("p (t b g i) -> p b g t i", b=BLOCKS, i=4, t=PACK)[:, b],
            )
        silu(words_of(*hidden_at(LAST), C), bank)
        quantize_words("tail", 0, C + P)
        second = bank_tile("second")
        second_product(5, 0, second[:, 0:C])
        cast_w2(6, 1, places[:, 1:2], on_vector)
        block_times_gate(5, 1, 0, second[:, 0:C])
        scatter(5, 0, "scalar")
        quantize_words("tail", C + P, C + 2 * N)
        second = bank_tile("second")
        for i, (e, b) in enumerate(((6, 0), (5, 1), (6, 1))):
            second_product(e, b, second[:, i * C : (i + 1) * C])
        cast_w2(LAST, 1, places[:, 2:3], on_vector)
        block_times_gate(6, 1, 0, second[:, 0:C])
        block_times_gate(5, 2, 1, second[:, C : 3 * C])
        for b in range(BLOCKS):
            scatter(6, b, "scalar")
        quantize_words("tail", C + 2 * N, 2 * C + 3 * N)
        second = bank_tile("second")
        second_layer(LAST, second, range(BLOCKS))
        cast_w2(SHARED, 1, places[:, 3:4], on_vector)
        times_gate(LAST, 1, slice(0, BLOCKS), second)
        quantize_words("tail", w2_at(SHARED)[1], w2_at(SHARED)[1] + N)
        scatter(LAST, 0, "vector")
        scatter(LAST, 1, "scalar")

        w_codes, w_scales = step("tail")[1:]
        wide = [bank_tile("shared"), bank_tile("shared"), bank_tile("shared"), bank_tile("first")]
        narrow = bank_tile("first")
        ys = {}
        for b in range(BLOCKS):
            rows = slice(w2_at(SHARED)[1] + b * P, w2_at(SHARED)[1] + (b + 1) * P)
            for index, (start, width) in enumerate(OUT_CUTS):
                ys[b, start] = wide[2 * b + index][:] if width == BANK else narrow[:, b * width : (b + 1) * width]
                cols = slice(start, start + width)
                multiply(ys[b, start], w_codes[:, rows], w_scales[:, rows], hs_codes[start], hs_scales[:, cols])
        result = load_tile()
        for b in range(BLOCKS):
            for start, width in OUT_CUTS:
                cols = slice(start, start + width)
                place = result[:, b * T + start : b * T + start + width]
                nc.vector.tensor_tensor(place, ys[b, start], routed[b][:, cols], ADD)
                nc.sync.dma_start(out=out[b * P : (b + 1) * P, cols], in_=place)
